import numpy as np
import ml_dtypes


def mxq(x, axis, fmt="e4m3"):
    dtype, down = {"e4m3": (ml_dtypes.float8_e4m3fn, 7), "e5m2": (ml_dtypes.float8_e5m2, 14)}[fmt]
    v = np.moveaxis(np.asarray(x, np.float32).astype(ml_dtypes.bfloat16).astype(np.float64), axis, -1)
    blocks = v.reshape(v.shape[:-1] + (-1, 32))
    amax = np.abs(blocks).max(-1, keepdims=True)
    byte = np.maximum(np.where(amax > 0, np.frexp(amax)[1] - 1 + 127, 0) - down, 1)
    scale = np.exp2(byte - 127.0)
    codes = (blocks / scale).astype(np.float32).astype(dtype).astype(np.float64)
    return np.moveaxis((codes * scale).reshape(v.shape), -1, axis)


WIDE = False


def mx_kscale(k):
    if not WIDE:
        return np.ones(k)
    levels = np.array([10, -10, 5, -5, 0])
    if k % 512:
        return np.exp2(np.random.permutation(np.resize(levels, k // 32))).repeat(32)
    a = np.empty((k // 512, 16))
    for p in range(k // 512):
        a[p, :8] = np.random.permutation(np.resize(levels, 8))
        for g in range(8):
            far = levels[np.abs(levels - a[p, g]) >= 10]
            a[p, g + 8] = far[np.random.randint(len(far))]
    return np.exp2(a.ravel()).repeat(32)


def f64(x):
    return np.asarray(x).astype(np.float64)


def striped(idx):
    return np.tile(idx.reshape(-1, 16).T, (8, 1)).astype(np.uint16)


def unstriped(offs):
    return offs[:16].T.reshape(-1).astype(np.int64)


E2M1 = np.array([0.0, 0.5, 1.0, 1.5, 2.0, 3.0, 4.0, 6.0, -0.0, -0.5, -1.0, -1.5, -2.0, -3.0, -4.0, -6.0])


def pack_weight(w, fmt):
    k, n = w.shape
    w = f64(np.asarray(w, np.float32).astype(ml_dtypes.bfloat16)).reshape(k // 32, 32, n)
    amax = np.abs(w).max(1)
    if fmt == "e4m3":
        byte = np.frexp(amax)[1] - 1 + 127 - 7
    else:
        mant, ex = np.frexp(amax / 6.0)
        byte = np.where(mant > 0.5, ex, ex - 1) + 127
    byte = np.clip(np.where(amax > 0, byte, 1), 1, 254)
    scaled = (w * np.exp2(127.0 - byte)[:, None, :]).reshape(k, n).astype(np.float32)
    by_word = np.ascontiguousarray(scaled.reshape(k // 512, 128, 4, n).transpose(0, 1, 3, 2))
    if fmt == "e4m3":
        words = by_word.astype(ml_dtypes.float8_e4m3fn).view(np.uint8)
    else:
        c = by_word.astype(ml_dtypes.float4_e2m1fn).view(np.uint8) & 0xF
        words = (c[..., 0::2] | (c[..., 1::2] << 4)).reshape(k // 512, 128, 2 * n)
    return np.ascontiguousarray(words), np.ascontiguousarray(byte.astype(np.uint8).reshape(k // 512, 16, n))


def unpack_weight(words, scales, fmt):
    g, _, n = scales.shape
    words = np.ascontiguousarray(words).reshape(g, 128, n, -1)
    if fmt == "e4m3":
        vals = words.view(ml_dtypes.float8_e4m3fn).astype(np.float64)
    else:
        nib = np.empty((g, 128, n, 4), np.uint8)
        nib[..., 0::2] = words & 0xF
        nib[..., 1::2] = words >> 4
        vals = E2M1[nib]
    vals = vals * np.repeat(np.exp2(scales.astype(np.float64) - 127.0), 8, axis=1)[..., None]
    return vals.transpose(0, 1, 3, 2).reshape(g * 512, n)


def gelu(v):
    return 0.5 * v * (1.0 + np.tanh(np.sqrt(2.0 / np.pi) * (v + 0.044715 * v**3)))


K, T, S, P, H, N = 1536, 2048, 1024, 512, 1024, 512

def setup_inputs():
    n = np.random.standard_normal
    s = mx_kscale(K)[:, None]
    u = mx_kscale(H)[:, None]
    tab_words, tab_scales = pack_weight(n((K, T)) * s, "e4m3")
    w4_words, w4_scales = pack_weight(1.2 * n((H, N)) / np.sqrt(H) / u, "e2m1")
    joints = np.random.permutation(S)
    return {
        "tab_words": tab_words, "tab_scales": tab_scales,
        "offs": striped(np.random.permutation(T)[:S]),
        "pos1": striped(joints[:P]),
        "pos2": striped(joints[P:2 * P]),
        "w1": (n((K, H)) / np.sqrt(K) / s * u.T).astype(np.float32),
        "b1": (0.3 * n(H) * u[:, 0]).astype(np.float32),
        "w2": (1.2 * n((H, N)) / np.sqrt(H) / u).astype(np.float32),
        "w4_words": w4_words, "w4_scales": w4_scales,
        "b3": (0.3 * n(N)).astype(np.float32),
    }

def reference(tab_words, tab_scales, offs, pos1, pos2, w1, b1, w2, w4_words, w4_scales, b3):
    v = unpack_weight(tab_words, tab_scales, "e4m3")[:, unstriped(offs)]
    w4 = unpack_weight(w4_words, w4_scales, "e2m1")
    h = np.maximum((mxq(f64(w1), 0, "e4m3").T @ v) + f64(b1)[:, None], 0.0)
    a = h[:, unstriped(pos1)]
    b = h[:, unstriped(pos2)]
    z = mxq(a - b, 0, "e4m3")
    y1 = mxq(f64(w2), 0, "e4m3").T @ z
    y2 = w4.T @ z
    return np.maximum(y1, y2) + f64(b3)[:, None]

@@ -1,0 +1,295 @@
+from contextlib import ExitStack
+
+import concourse.mybir as mybir
+
+K, T, S, J, H, N = 1536, 2048, 1024, 512, 1024, 512
+FLOPS = 2 * K * H * S + 2 * 2 * H * N * J
+
+F32 = mybir.dt.float32
+BF16 = mybir.dt.bfloat16
+I32 = mybir.dt.int32
+U32 = mybir.dt.uint32
+U16 = mybir.dt.uint16
+U8 = mybir.dt.uint8
+FP8X4 = mybir.dt.float8_e4m3fn_x4
+FP4X4 = mybir.dt.float4_e2m1fn_x4
+ALU = mybir.AluOpType
+ACT = mybir.ActivationFunctionType
+
+P = 128
+PACK = 4
+PASS = P * PACK
+KA = K // PASS
+HB = H // PASS
+BANK = 512
+HALF = J // 2
+
+
+def tile_list_limb_pair_scores_kernel(
+    tc, tab_words, tab_scales, offs, pos1, pos2, w1, b1, w2, w4_words, w4_scales, b3, out
+):
+    nc = tc.nc
+    with ExitStack() as ctx:
+        keep = ctx.enter_context(tc.tile_pool(name="keep", bufs=1))
+        ring = ctx.enter_context(tc.tile_pool(name="ring", bufs=3))
+        psum = ctx.enter_context(tc.psum_pool(name="psum", bufs=1))
+
+        def bank(i):
+            return psum.tile([P, BANK], F32, name="bank%d" % i)
+
+        offs_sb = keep.tile([P, S // 16], U16, name="offs_sb")
+        pos1_sb = keep.tile([P, J // 16], U16, name="pos1_sb")
+        pos2_sb = keep.tile([P, J // 16], U16, name="pos2_sb")
+        tab_w = [keep.tile([P, T], I32, name="tab_w%d" % a, align_bytes=64) for a in range(KA)]
+        tab_s = keep.tile([P, T], U8, name="tab_s", align_bytes=64)
+        tab_s_in = keep.tile([P, T // 4], I32, name="tab_s_in", align_bytes=64)
+        w4_w = keep.tile([P, HB, 2 * N], U8, name="w4_w", align_bytes=64)
+        w4_s = keep.tile([P, HB, N], U8, name="w4_s", align_bytes=64)
+        b1_sb = keep.tile([P, HB, PACK], F32, name="b1_sb")
+        b3_sb = keep.tile([P, N // P], F32, name="b3_sb")
+        w1_raw = {
+            (a, b): keep.tile([P, PACK, PASS], F32, name="w1_raw%d%d" % (a, b), align_bytes=64)
+            for b in range(HB) for a in range(KA)
+        }
+        w2_raw = [keep.tile([P, PACK, N], F32, name="w2_raw%d" % b, align_bytes=64) for b in range(HB)]
+        warm = keep.tile([P, 8], F32, name="warm")
+
+        nc.vector.memset(tab_s[:].bitcast(I32), 0)
+        nc.vector.memset(w4_s[:].rearrange("p b n -> p (b n)").bitcast(I32), 0)
+        nc.vector.memset(warm[:, 0:4], 0.0)
+
+        def load_tab(a):
+            nc.sync.dma_start(out=tab_w[a][:], in_=tab_words[a].rearrange("p t i -> p (t i)").bitcast(I32))
+
+        def load_w1(a, b):
+            rows = w1[a * PASS : (a + 1) * PASS, b * PASS : (b + 1) * PASS]
+            nc.sync.dma_start(out=w1_raw[a, b][:], in_=rows.rearrange("(p i) c -> p i c", i=PACK))
+
+        nc.sync.dma_start(offs_sb[:], offs)
+        load_tab(0)
+        for q in range(4):
+            queue = nc.scalar if q < 2 else nc.sync
+            queue.dma_start(
+                out=tab_s_in[32 * q : 32 * q + 4 * KA, :],
+                in_=tab_scales[:, 4 * q : 4 * q + 4, :].bitcast(I32),
+            )
+        nc.scalar.dma_start(out=b1_sb[:], in_=b1.rearrange("(b p t) -> p b t", b=HB, t=PACK))
+        nc.scalar.activation(out=warm[:, 4:8], in_=warm[:, 0:4], func=ACT.Relu)
+        load_w1(0, 0)
+        load_tab(1)
+        load_w1(1, 0)
+        load_tab(2)
+        nc.sync.dma_start(pos2_sb[:], pos2)
+        nc.sync.dma_start(pos1_sb[:], pos1)
+        load_w1(2, 0)
+        for a in range(KA):
+            load_w1(a, 1)
+        for b in range(HB):
+            nc.sync.dma_start(
+                out=w2_raw[b][:], in_=w2[b * PASS : (b + 1) * PASS, :].rearrange("(p i) n -> p i n", i=PACK)
+            )
+        nc.sync.dma_start(out=w4_w[:].bitcast(I32), in_=w4_words.rearrange("b p n -> p b n").bitcast(I32))
+        for q in range(4):
+            nc.sync.dma_start(
+                out=w4_s[32 * q : 32 * q + 4, :, :].bitcast(I32),
+                in_=w4_scales[:, 4 * q : 4 * q + 4, :].rearrange("b r n -> r b n").bitcast(I32),
+            )
+        with nc.allow_non_contiguous_dma(reason="one bias value a partition"):
+            nc.sync.dma_start(out=b3_sb[:], in_=b3.rearrange("(c p) -> p c", p=P))
+
+        v_w = [keep.tile([P, S], U32, name="v_w%d" % a, align_bytes=64) for a in range(KA)]
+        v_s = keep.tile([P, S], U8, name="v_s", align_bytes=64)
+        last_w1 = (KA - 1, HB - 1)
+        w1_w = {
+            ab: keep.tile([P, PASS], U32, name="w1_w%d%d" % ab, tag="slot_a" if ab == last_w1 else "", align_bytes=64)
+            for ab in w1_raw
+        }
+        w1_s = {
+            ab: keep.tile([P, PASS], U8, name="w1_s%d%d" % ab, tag="slot_b" if ab == last_w1 else "", align_bytes=64)
+            for ab in w1_raw
+        }
+        w2_w = [keep.tile([P, N], U32, name="w2_w%d" % b, align_bytes=64) for b in range(HB)]
+        w2_s = [keep.tile([P, N], U8, name="w2_s%d" % b, align_bytes=64) for b in range(HB)]
+        h = {
+            (b, t): keep.tile([P, S], F32, name="h%d%d" % (b, t), align_bytes=64)
+            for b in range(HB) for t in range(PACK)
+        }
+        z_f = [keep.tile([P, PACK, J], F32, name="z_f%d" % b, align_bytes=64) for b in range(HB)]
+        z_w = [keep.tile([P, J], U32, name="z_w%d" % b, align_bytes=64) for b in range(HB)]
+        z_s = [keep.tile([P, J], U8, name="z_s%d" % b, align_bytes=64) for b in range(HB)]
+
+        def gather_tab(a):
+            nc.vector.tensor_copy(v_w[a][:], tab_w[a][:].bitcast(U32).indirect(offs_sb[:]))
+
+        def round_w1(a, b, split=None):
+            g = ring.tile([P, PASS * PACK], BF16, name="grouped", align_bytes=64)
+            dst = g[:].rearrange("p (t m i) -> p m i t", t=PACK, i=PACK)
+            src = w1_raw[a, b][:].rearrange("p i (m t) -> p m i t", t=PACK)
+            if split is None:
+                nc.scalar.copy(out=dst, in_=src)
+            else:
+                nc.scalar.copy(out=dst[:, :split], in_=src[:, :split])
+                nc.vector.tensor_copy(out=dst[:, split:], in_=src[:, split:])
+            return g
+
+        def quant(words, scales, src):
+            nc.vector.quantize_mx(out=words.bitcast(FP8X4), scales=scales, in_=src)
+
+        def interleave(dst, src, engine_copy):
+            engine_copy(
+                out=dst.rearrange("p (c u) t -> p c t u", u=4),
+                in_=src.rearrange("p t (c u) -> p c t u", u=4),
+            )
+
+        def round_w2(b, slot):
+            g = keep.tile([P, N, PACK], BF16, name="w2_g%d" % b, tag=slot, align_bytes=64)
+            interleave(g[:], w2_raw[b][:], nc.scalar.copy)
+            quant(w2_w[b][:], w2_s[b][:], g[:].rearrange("p n i -> p (n i)"))
+
+        def h_pass(acc, a, b, t, s):
+            cols = slice(t * P, (t + 1) * P)
+            ent = slice(s * BANK, (s + 1) * BANK)
+            nc.tensor.matmul_mx(
+                out=acc[:],
+                lhsT=w1_w[a, b][:, cols].bitcast(FP8X4),
+                lhsT_scale=w1_s[a, b][:, cols],
+                rhs=v_w[a][:, ent].bitcast(FP8X4),
+                rhs_scale=v_s[4 * a :, ent],
+                start=(a == 0),
+                stop=(a == KA - 1),
+            )
+
+        def evict_h(acc, b, t, s, on_vector=False):
+            dst = h[b, t][:, s * BANK : (s + 1) * BANK]
+            if on_vector:
+                nc.vector.tensor_scalar(dst, acc[:], b1_sb[:, b, t : t + 1], 0.0, ALU.add, ALU.max)
+            else:
+                nc.scalar.activation(out=dst, in_=acc[:], func=ACT.Relu, bias=b1_sb[:, b, t : t + 1])
+
+        def pair(b, units, slot=None):
+            width = units[0][2] - units[0][1]
+            if slot is None:
+                child = ring.tile([P, 2, width], F32, name="child", align_bytes=64)
+            else:
+                child = keep.tile([P, 2, width], F32, name="child_" + slot, tag=slot, align_bytes=64)
+            for n, (t, j0, j1) in enumerate(units):
+                nc.vector.tensor_copy(child[:, n, :], h[b, t][:].indirect(pos2_sb[:, j0 // 16 : j1 // 16]))
+            for n, (t, j0, j1) in enumerate(units):
+                nc.vector.tensor_tensor(
+                    z_f[b][:, t, j0:j1],
+                    h[b, t][:].indirect(pos1_sb[:, j0 // 16 : j1 // 16]),
+                    child[:, n, :],
+                    ALU.subtract,
+                )
+
+        def halves(t, j0, j1):
+            mid = (j0 + j1) // 2
+            return [(t, j0, mid), (t, mid, j1)]
+
+        def round_z(b, j0, j1, slot, cut=None):
+            g = keep.tile([P, j1 - j0, PACK], BF16, name="z_g%d_%d" % (b, j0), tag=slot, align_bytes=64)
+            if cut is None:
+                interleave(g[:], z_f[b][:, :, j0:j1], nc.scalar.copy)
+            else:
+                interleave(g[:, :cut, :], z_f[b][:, :, j0 : j0 + cut], nc.scalar.copy)
+                interleave(g[:, cut:, :], z_f[b][:, :, j0 + cut : j1], nc.vector.tensor_copy)
+            quant(z_w[b][:, j0:j1], z_s[b][:, j0:j1], g[:].rearrange("p j t -> p (j t)"))
+
+        def y_passes(y1, y2, c, b, j0, j1, start, stop):
+            cols = slice(c * P, (c + 1) * P)
+            nc.tensor.matmul_mx(
+                out=y1[:, j0:j1],
+                lhsT=w2_w[b][:, cols].bitcast(FP8X4),
+                lhsT_scale=w2_s[b][:, cols],
+                rhs=z_w[b][:, j0:j1].bitcast(FP8X4),
+                rhs_scale=z_s[b][:, j0:j1],
+                start=start,
+                stop=stop,
+            )
+            width = j1 - j0 if j1 - j0 == BANK else P
+            for j in range(j0, j1, width):
+                nc.tensor.matmul_mx(
+                    out=y2[:, j : j + width],
+                    lhsT=w4_w[:, b, 2 * c * P : 2 * (c + 1) * P].bitcast(FP4X4),
+                    lhsT_scale=w4_s[:, b, cols],
+                    rhs=z_w[b][:, j : j + width].bitcast(FP8X4),
+                    rhs_scale=z_s[b][:, j : j + width],
+                    start=start and j == j0,
+                    stop=stop and j + width == j1,
+                )
+
+        for q in range(4):
+            rows = slice(32 * q, 32 * q + 4 * KA)
+            nc.vector.tensor_copy(tab_s[:].bitcast(I32)[rows, :], tab_s_in[rows, :])
+        gather_tab(0)
+        nc.vector.tensor_copy(v_s[:], tab_s[:].indirect(offs_sb[:]))
+        acc0 = {(t, s): bank(2 * t + s) for t in range(PACK) for s in range(2)}
+        for a in range(KA):
+            if a > 0:
+                gather_tab(a)
+            last = a == KA - 1
+            g = round_w1(a, 0, split=40 if last else None)
+            if last:
+                quant(w1_w[a, 0][:, :P], w1_s[a, 0][:, :P], g[:, :PASS])
+                quant(w1_w[a, 0][:, P : 2 * P], w1_s[a, 0][:, P : 2 * P], g[:, PASS : 2 * PASS])
+                quant(w1_w[a, 0][:, 2 * P :], w1_s[a, 0][:, 2 * P :], g[:, 2 * PASS :])
+            else:
+                quant(w1_w[a, 0][:], w1_s[a, 0][:], g[:])
+            for t in range(PACK):
+                for s in range(2):
+                    h_pass(acc0[t, s], a, 0, t, s)
+
+        def finish0(t):
+            for s in range(2):
+                evict_h(acc0[t, s], 0, t, s, on_vector=(t == 0 and s == 1))
+            pair(0, halves(t, 0, J))
+
+        def prep1(a):
+            g = round_w1(a, 1)
+            quant(w1_w[a, 1][:], w1_s[a, 1][:], g[:])
+
+        finish0(0)
+        pass
+        finish0(1)
+        prep1(0)
+        finish0(2)
+        prep1(1)
+        prep1(2)
+        acc1 = {(t, s): bank(2 * t + s) for t in range(PACK - 1) for s in range(2)}
+        for a in range(KA):
+            for t in range(PACK - 1):
+                for s in range(2):
+                    h_pass(acc1[t, s], a, 1, t, s)
+        finish0(3)
+        pass
+        for s in range(2):
+            acc1[3, s] = bank(6 + s)
+            for a in range(KA):
+                h_pass(acc1[3, s], a, 1, 3, s)
+        for t in range(PACK):
+            for s in range(2):
+                evict_h(acc1[t, s], 1, t, s)
+
+        pair(1, halves(0, 0, J))
+        pair(1, halves(1, 0, J))
+        round_z(0, 0, J, "slot_b")
+        round_w2(0, "slot_a")
+        y1 = [bank(2 * c) for c in range(N // P)]
+        y2 = [bank(2 * c + 1) for c in range(N // P)]
+        for c in range(N // P):
+            y_passes(y1[c], y2[c], c, 0, 0, J, True, False)
+        pair(1, [(2, 0, HALF), (3, 0, HALF)], "slot_a")
+        round_w2(1, "slot_b")
+        round_z(1, 0, HALF, "slot_c")
+        pair(1, halves(2, HALF, J), "slot_b")
+        for c in range(N // P):
+            y_passes(y1[c], y2[c], c, 1, 0, HALF, False, False)
+        pair(1, halves(3, HALF, J), "slot_c")
+        round_z(1, HALF, J, "slot_d", cut=80)
+        for c in range(N // P):
+            y_passes(y1[c], y2[c], c, 1, HALF, J, False, True)
+            y1b = ring.tile([P, J], F32, name="y1b", bufs=4)
+            nc.scalar.activation(out=y1b[:], in_=y1[c][:], func=ACT.Identity, bias=b3_sb[:, c : c + 1])
+            res = ring.tile([P, J], F32, name="res", bufs=4)
+            nc.vector.scalar_tensor_tensor(res[:], y2[c][:], b3_sb[:, c : c + 1], y1b[:], ALU.add, ALU.max)
+            nc.sync.dma_start(out=out[c * P : (c + 1) * P, :], in_=res[:])

@@ -31,6 +31,7 @@ def tile_list_limb_pair_scores_kernel(
     nc = tc.nc
     with ExitStack() as ctx:
         keep = ctx.enter_context(tc.tile_pool(name="keep", bufs=1))
+        late = ctx.enter_context(tc.tile_pool(name="late", bufs=1))
         ring = ctx.enter_context(tc.tile_pool(name="ring", bufs=3))
         psum = ctx.enter_context(tc.psum_pool(name="psum", bufs=1))
 
@@ -45,7 +46,8 @@ def tile_list_limb_pair_scores_kernel(
         tab_s_in = keep.tile([P, T // 4], I32, name="tab_s_in", align_bytes=64)
         w4_w = keep.tile([P, HB, 2 * N], U8, name="w4_w", align_bytes=64)
         w4_s = keep.tile([P, HB, N], U8, name="w4_s", align_bytes=64)
-        b1_sb = keep.tile([P, HB, PACK], F32, name="b1_sb")
+        b1_pad = late.tile([P, 1024 + 32], F32, name="b1_pad", offset=4096 - 64, align_bytes=64)
+        b1_sb = b1_pad[:, : HB * PACK].rearrange("p (b t) -> p b t", b=HB)
         b3_sb = keep.tile([P, N // P], F32, name="b3_sb")
         w1_raw = {
             (a, b): keep.tile([P, PACK, PASS], F32, name="w1_raw%d%d" % (a, b), align_bytes=64)
@@ -73,15 +75,15 @@ def tile_list_limb_pair_scores_kernel(
                 out=tab_s_in[32 * q : 32 * q + 4 * KA, :],
                 in_=tab_scales[:, 4 * q : 4 * q + 4, :].bitcast(I32),
             )
-        nc.scalar.dma_start(out=b1_sb[:], in_=b1.rearrange("(b p t) -> p b t", b=HB, t=PACK))
+        nc.scalar.dma_start(out=b1_sb, in_=b1.rearrange("(b p t) -> p b t", b=HB, t=PACK))
         nc.scalar.activation(out=warm[:, 4:8], in_=warm[:, 0:4], func=ACT.Relu)
-        load_w1(0, 0)
         load_tab(1)
-        load_w1(1, 0)
+        load_w1(0, 0)
         load_tab(2)
+        load_w1(1, 0)
+        load_w1(2, 0)
         nc.sync.dma_start(pos2_sb[:], pos2)
         nc.sync.dma_start(pos1_sb[:], pos1)
-        load_w1(2, 0)
         for a in range(KA):
             load_w1(a, 1)
         for b in range(HB):
@@ -99,13 +101,9 @@ def tile_list_limb_pair_scores_kernel(
 
         v_w = [keep.tile([P, S], U32, name="v_w%d" % a, align_bytes=64) for a in range(KA)]
         v_s = keep.tile([P, S], U8, name="v_s", align_bytes=64)
-        last_w1 = (KA - 1, HB - 1)
-        w1_w = {
-            ab: keep.tile([P, PASS], U32, name="w1_w%d%d" % ab, tag="slot_a" if ab == last_w1 else "", align_bytes=64)
-            for ab in w1_raw
-        }
+        w1_w = {ab: keep.tile([P, PASS], U32, name="w1_w%d%d" % ab, align_bytes=64) for ab in w1_raw}
         w1_s = {
-            ab: keep.tile([P, PASS], U8, name="w1_s%d%d" % ab, tag="slot_b" if ab == last_w1 else "", align_bytes=64)
+            ab: keep.tile([P, PASS], U8, name="w1_s%d%d" % ab, align_bytes=64)
             for ab in w1_raw
         }
         w2_w = [keep.tile([P, N], U32, name="w2_w%d" % b, align_bytes=64) for b in range(HB)]
@@ -121,16 +119,11 @@ def tile_list_limb_pair_scores_kernel(
         def gather_tab(a):
             nc.vector.tensor_copy(v_w[a][:], tab_w[a][:].bitcast(U32).indirect(offs_sb[:]))
 
-        def round_w1(a, b, split=None):
+        def w1_views(a, b):
             g = ring.tile([P, PASS * PACK], BF16, name="grouped", align_bytes=64)
-            dst = g[:].rearrange("p (t m i) -> p m i t", t=PACK, i=PACK)
-            src = w1_raw[a, b][:].rearrange("p i (m t) -> p m i t", t=PACK)
-            if split is None:
-                nc.scalar.copy(out=dst, in_=src)
-            else:
-                nc.scalar.copy(out=dst[:, :split], in_=src[:, :split])
-                nc.vector.tensor_copy(out=dst[:, split:], in_=src[:, split:])
-            return g
+            dst = g[:].rearrange("p (u t m i) -> p u m i t", u=2, t=2, i=PACK)
+            src = w1_raw[a, b][:].rearrange("p i (m u t) -> p u m i t", u=2, t=2)
+            return g, dst, src
 
         def quant(words, scales, src):
             nc.vector.quantize_mx(out=words.bitcast(FP8X4), scales=scales, in_=src)
@@ -141,12 +134,11 @@ def tile_list_limb_pair_scores_kernel(
                 in_=src.rearrange("p t (c u) -> p c t u", u=4),
             )
 
-        def round_w2(b, slot):
-            g = keep.tile([P, N, PACK], BF16, name="w2_g%d" % b, tag=slot, align_bytes=64)
-            interleave(g[:], w2_raw[b][:], nc.scalar.copy)
-            quant(w2_w[b][:], w2_s[b][:], g[:].rearrange("p n i -> p (n i)"))
+        def round_w2(b, g):
+            interleave(g.rearrange("p (n i) -> p n i", i=PACK), w2_raw[b][:], nc.scalar.copy)
+            quant(w2_w[b][:], w2_s[b][:], g)
 
-        def h_pass(acc, a, b, t, s):
+        def h_pass(acc, a, b, t, s, start, stop):
             cols = slice(t * P, (t + 1) * P)
             ent = slice(s * BANK, (s + 1) * BANK)
             nc.tensor.matmul_mx(
@@ -155,8 +147,8 @@ def tile_list_limb_pair_scores_kernel(
                 lhsT_scale=w1_s[a, b][:, cols],
                 rhs=v_w[a][:, ent].bitcast(FP8X4),
                 rhs_scale=v_s[4 * a :, ent],
-                start=(a == 0),
-                stop=(a == KA - 1),
+                start=start,
+                stop=stop,
             )
 
         def evict_h(acc, b, t, s, on_vector=False):
@@ -166,12 +158,10 @@ def tile_list_limb_pair_scores_kernel(
             else:
                 nc.scalar.activation(out=dst, in_=acc[:], func=ACT.Relu, bias=b1_sb[:, b, t : t + 1])
 
-        def pair(b, units, slot=None):
+        def pair(b, units, child=None):
             width = units[0][2] - units[0][1]
-            if slot is None:
+            if child is None:
                 child = ring.tile([P, 2, width], F32, name="child", align_bytes=64)
-            else:
-                child = keep.tile([P, 2, width], F32, name="child_" + slot, tag=slot, align_bytes=64)
             for n, (t, j0, j1) in enumerate(units):
                 nc.vector.tensor_copy(child[:, n, :], h[b, t][:].indirect(pos2_sb[:, j0 // 16 : j1 // 16]))
             for n, (t, j0, j1) in enumerate(units):
@@ -186,8 +176,7 @@ def tile_list_limb_pair_scores_kernel(
             mid = (j0 + j1) // 2
             return [(t, j0, mid), (t, mid, j1)]
 
-        def round_z(b, j0, j1, slot, cut=None):
-            g = keep.tile([P, j1 - j0, PACK], BF16, name="z_g%d_%d" % (b, j0), tag=slot, align_bytes=64)
+        def round_z(b, j0, j1, g, cut=None):
             if cut is None:
                 interleave(g[:], z_f[b][:, :, j0:j1], nc.scalar.copy)
             else:
@@ -195,101 +184,118 @@ def tile_list_limb_pair_scores_kernel(
                 interleave(g[:, cut:, :], z_f[b][:, :, j0 + cut : j1], nc.vector.tensor_copy)
             quant(z_w[b][:, j0:j1], z_s[b][:, j0:j1], g[:].rearrange("p j t -> p (j t)"))
 
-        def y_passes(y1, y2, c, b, j0, j1, start, stop):
+        def y_passes(y, c, b, u):
             cols = slice(c * P, (c + 1) * P)
+            j0 = u * HALF
             nc.tensor.matmul_mx(
-                out=y1[:, j0:j1],
+                out=y[:, :HALF],
                 lhsT=w2_w[b][:, cols].bitcast(FP8X4),
                 lhsT_scale=w2_s[b][:, cols],
-                rhs=z_w[b][:, j0:j1].bitcast(FP8X4),
-                rhs_scale=z_s[b][:, j0:j1],
-                start=start,
-                stop=stop,
+                rhs=z_w[b][:, j0 : j0 + HALF].bitcast(FP8X4),
+                rhs_scale=z_s[b][:, j0 : j0 + HALF],
+                start=(b == 0),
+                stop=False,
             )
-            width = j1 - j0 if j1 - j0 == BANK else P
-            for j in range(j0, j1, width):
+            for j in range(0, HALF, P):
                 nc.tensor.matmul_mx(
-                    out=y2[:, j : j + width],
+                    out=y[:, HALF + j : HALF + j + P],
                     lhsT=w4_w[:, b, 2 * c * P : 2 * (c + 1) * P].bitcast(FP4X4),
                     lhsT_scale=w4_s[:, b, cols],
-                    rhs=z_w[b][:, j : j + width].bitcast(FP8X4),
-                    rhs_scale=z_s[b][:, j : j + width],
-                    start=start and j == j0,
-                    stop=stop and j + width == j1,
+                    rhs=z_w[b][:, j0 + j : j0 + j + P].bitcast(FP8X4),
+                    rhs_scale=z_s[b][:, j0 + j : j0 + j + P],
+                    start=False,
+                    stop=(b == HB - 1 and j + P == HALF),
                 )
+
+        def finish_y(y, c, u):
+            y_passes(y, c, 1, u)
+            y1b = ring.tile([P, HALF], F32, name="y1b", bufs=4)
+            nc.scalar.activation(out=y1b[:], in_=y[:, :HALF], func=ACT.Identity, bias=b3_sb[:, c : c + 1])
+            res = ring.tile([P, HALF], F32, name="res", bufs=8)
+            nc.vector.scalar_tensor_tensor(res[:], y[:, HALF:], b3_sb[:, c : c + 1], y1b[:], ALU.add, ALU.max)
+            nc.sync.dma_start(out=out[c * P : (c + 1) * P, u * HALF : (u + 1) * HALF], in_=res[:])
 
         for q in range(4):
             rows = slice(32 * q, 32 * q + 4 * KA)
             nc.vector.tensor_copy(tab_s[:].bitcast(I32)[rows, :], tab_s_in[rows, :])
-        gather_tab(0)
         nc.vector.tensor_copy(v_s[:], tab_s[:].indirect(offs_sb[:]))
+        gather_tab(0)
+        gather_tab(1)
         acc0 = {(t, s): bank(2 * t + s) for t in range(PACK) for s in range(2)}
-        for a in range(KA):
-            if a > 0:
-                gather_tab(a)
-            last = a == KA - 1
-            g = round_w1(a, 0, split=40 if last else None)
-            if last:
-                quant(w1_w[a, 0][:, :P], w1_s[a, 0][:, :P], g[:, :PASS])
-                quant(w1_w[a, 0][:, P : 2 * P], w1_s[a, 0][:, P : 2 * P], g[:, PASS : 2 * PASS])
-                quant(w1_w[a, 0][:, 2 * P :], w1_s[a, 0][:, 2 * P :], g[:, 2 * PASS :])
-            else:
-                quant(w1_w[a, 0][:], w1_s[a, 0][:], g[:])
-            for t in range(PACK):
+        g, dst, src = w1_views(0, 0)
+        nc.scalar.copy(out=dst, in_=src)
+        quant(w1_w[0, 0][:], w1_s[0, 0][:], g[:])
+        for t in range(PACK):
+            for s in range(2):
+                h_pass(acc0[t, s], 0, 0, t, s, True, False)
+        gather_tab(2)
+        g, dst, src = w1_views(1, 0)
+        nc.scalar.copy(out=dst[:, :, :88], in_=src[:, :, :88])
+        nc.vector.tensor_copy(out=dst[:, :, 88:], in_=src[:, :, 88:])
+        quant(w1_w[1, 0][:], w1_s[1, 0][:], g[:])
+        g, dst, src = w1_views(2, 0)
+        nc.scalar.copy(out=dst[:, 0, :40], in_=src[:, 0, :40])
+        nc.vector.tensor_copy(out=dst[:, 0, 40:], in_=src[:, 0, 40:])
+        quant(w1_w[2, 0][:, : 2 * P], w1_s[2, 0][:, : 2 * P], g[:, : 2 * PASS])
+        nc.scalar.copy(out=dst[:, 1], in_=src[:, 1])
+        quant(w1_w[2, 0][:, 2 * P :], w1_s[2, 0][:, 2 * P :], g[:, 2 * PASS :])
+        for t in range(PACK):
+            order = (1, 2) if t == 0 else (2, 1)
+            for a in order:
                 for s in range(2):
-                    h_pass(acc0[t, s], a, 0, t, s)
+                    h_pass(acc0[t, s], a, 0, t, s, False, a == order[-1])
 
         def finish0(t):
             for s in range(2):
                 evict_h(acc0[t, s], 0, t, s, on_vector=(t == 0 and s == 1))
             pair(0, halves(t, 0, J))
 
-        def prep1(a):
-            g = round_w1(a, 1)
+        def prep1(a, engine_copy):
+            g, dst, src = w1_views(a, 1)
+            engine_copy(out=dst, in_=src)
             quant(w1_w[a, 1][:], w1_s[a, 1][:], g[:])
 
         finish0(0)
-        pass
         finish0(1)
-        prep1(0)
+        prep1(0, nc.scalar.copy)
         finish0(2)
-        prep1(1)
-        prep1(2)
+        prep1(1, nc.scalar.copy)
+        prep1(2, nc.scalar.copy)
         acc1 = {(t, s): bank(2 * t + s) for t in range(PACK - 1) for s in range(2)}
-        for a in range(KA):
-            for t in range(PACK - 1):
+        for t in range(PACK - 1):
+            for s in range(2):
+                h_pass(acc1[t, s], 0, 1, t, s, True, False)
+        for t in range(PACK - 1):
+            order = (1, 2) if t == 0 else (2, 1)
+            for a in order:
                 for s in range(2):
-                    h_pass(acc1[t, s], a, 1, t, s)
+                    h_pass(acc1[t, s], a, 1, t, s, False, a == order[-1])
+        order = (0, 1, 2)
         finish0(3)
-        pass
         for s in range(2):
             acc1[3, s] = bank(6 + s)
-            for a in range(KA):
-                h_pass(acc1[3, s], a, 1, 3, s)
+            for a in order:
+                h_pass(acc1[3, s], a, 1, 3, s, a == order[0], a == order[-1])
         for t in range(PACK):
             for s in range(2):
                 evict_h(acc1[t, s], 1, t, s)
 
+        pass
         pair(1, halves(0, 0, J))
         pair(1, halves(1, 0, J))
-        round_z(0, 0, J, "slot_b")
-        round_w2(0, "slot_a")
-        y1 = [bank(2 * c) for c in range(N // P)]
-        y2 = [bank(2 * c + 1) for c in range(N // P)]
-        for c in range(N // P):
-            y_passes(y1[c], y2[c], c, 0, 0, J, True, False)
-        pair(1, [(2, 0, HALF), (3, 0, HALF)], "slot_a")
-        round_w2(1, "slot_b")
-        round_z(1, 0, HALF, "slot_c")
-        pair(1, halves(2, HALF, J), "slot_b")
-        for c in range(N // P):
-            y_passes(y1[c], y2[c], c, 1, 0, HALF, False, False)
-        pair(1, halves(3, HALF, J), "slot_c")
-        round_z(1, HALF, J, "slot_d", cut=80)
-        for c in range(N // P):
-            y_passes(y1[c], y2[c], c, 1, HALF, J, False, True)
-            y1b = ring.tile([P, J], F32, name="y1b", bufs=4)
-            nc.scalar.activation(out=y1b[:], in_=y1[c][:], func=ACT.Identity, bias=b3_sb[:, c : c + 1])
-            res = ring.tile([P, J], F32, name="res", bufs=4)
-            nc.vector.scalar_tensor_tensor(res[:], y2[c][:], b3_sb[:, c : c + 1], y1b[:], ALU.add, ALU.max)
-            nc.sync.dma_start(out=out[c * P : (c + 1) * P, :], in_=res[:])
+        round_z(0, 0, J, late.tile([P, J, PACK], BF16, name="z_g0", offset=0, align_bytes=64))
+        pair(1, [(2, 0, HALF), (3, 0, HALF)], late.tile([P, 2, HALF], F32, name="child_a", offset=0, align_bytes=64))
+        pass
+        round_w2(0, late.tile([P, N * PACK], BF16, name="w2_g0", offset=4096, align_bytes=64)[:])
+        y = {(c, u): bank(4 * u + c) for u in range(2) for c in range(N // P)}
+        for u in range(2):
+            for c in range(N // P):
+                y_passes(y[c, u], c, 0, u)
+        pair(1, halves(2, HALF, J), late.tile([P, 2, P], F32, name="child_b", offset=4096, align_bytes=64))
+        round_w2(1, late.tile([P, N * PACK], BF16, name="w2_g1", offset=8192, align_bytes=64)[:])
+        round_z(1, 0, HALF, keep.tile([P, HALF, PACK], BF16, name="z_g1a", tag="slot_c", align_bytes=64))
+        pair(1, halves(3, HALF, J), keep.tile([P, 2, P], F32, name="child_c", tag="slot_c", align_bytes=64))
+        round_z(1, HALF, J, keep.tile([P, HALF, PACK], BF16, name="z_g1b", align_bytes=64), cut=80)
+        for u in range(2):
+            for c in range(N // P):
+                finish_y(y[c, u], c, u)

@@ -41,9 +41,8 @@ def tile_list_limb_pair_scores_kernel(
         offs_sb = keep.tile([P, S // 16], U16, name="offs_sb")
         pos1_sb = keep.tile([P, J // 16], U16, name="pos1_sb")
         pos2_sb = keep.tile([P, J // 16], U16, name="pos2_sb")
-        tab_w = [keep.tile([P, T], I32, name="tab_w%d" % a, align_bytes=64) for a in range(KA)]
+        tab_w = [keep.tile([P, T], I32, name="tab_w%d" % a, tag="tab_w%d" % a, align_bytes=64) for a in range(KA)]
         tab_s = keep.tile([P, T], U8, name="tab_s", align_bytes=64)
-        tab_s_in = keep.tile([P, T // 4], I32, name="tab_s_in", align_bytes=64)
         w4_w = keep.tile([P, HB, 2 * N], U8, name="w4_w", align_bytes=64)
         w4_s = keep.tile([P, HB, N], U8, name="w4_s", align_bytes=64)
         b1_pad = late.tile([P, 1024 + 32], F32, name="b1_pad", offset=4096 - 64, align_bytes=64)
@@ -56,7 +55,7 @@ def tile_list_limb_pair_scores_kernel(
         w2_raw = [keep.tile([P, PACK, N], F32, name="w2_raw%d" % b, align_bytes=64) for b in range(HB)]
         warm = keep.tile([P, 8], F32, name="warm")
 
-        nc.vector.memset(tab_s[:].bitcast(I32), 0)
+        nc.gpsimd.memset(tab_s[:].bitcast(I32), 0)
         nc.vector.memset(w4_s[:].rearrange("p b n -> p (b n)").bitcast(I32), 0)
         nc.vector.memset(warm[:, 0:4], 0.0)
 
@@ -67,12 +66,12 @@ def tile_list_limb_pair_scores_kernel(
             rows = w1[a * PASS : (a + 1) * PASS, b * PASS : (b + 1) * PASS]
             nc.sync.dma_start(out=w1_raw[a, b][:], in_=rows.rearrange("(p i) c -> p i c", i=PACK))
 
-        nc.sync.dma_start(offs_sb[:], offs)
         load_tab(0)
+        nc.sync.dma_start(offs_sb[:], offs)
         for q in range(4):
-            queue = nc.scalar if q < 2 else nc.sync
+            queue = nc.gpsimd if q < 3 else nc.scalar
             queue.dma_start(
-                out=tab_s_in[32 * q : 32 * q + 4 * KA, :],
+                out=tab_s[32 * q : 32 * q + 4 * KA, :].bitcast(I32),
                 in_=tab_scales[:, 4 * q : 4 * q + 4, :].bitcast(I32),
             )
         nc.scalar.dma_start(out=b1_sb, in_=b1.rearrange("(b p t) -> p b t", b=HB, t=PACK))
@@ -100,7 +99,6 @@ def tile_list_limb_pair_scores_kernel(
             nc.sync.dma_start(out=b3_sb[:], in_=b3.rearrange("(c p) -> p c", p=P))
 
         v_w = [keep.tile([P, S], U32, name="v_w%d" % a, align_bytes=64) for a in range(KA)]
-        v_s = keep.tile([P, S], U8, name="v_s", align_bytes=64)
         w1_w = {ab: keep.tile([P, PASS], U32, name="w1_w%d%d" % ab, align_bytes=64) for ab in w1_raw}
         w1_s = {
             ab: keep.tile([P, PASS], U8, name="w1_s%d%d" % ab, align_bytes=64)
@@ -176,27 +174,23 @@ def tile_list_limb_pair_scores_kernel(
             mid = (j0 + j1) // 2
             return [(t, j0, mid), (t, mid, j1)]
 
-        def round_z(b, j0, j1, g, cut=None):
-            if cut is None:
-                interleave(g[:], z_f[b][:, :, j0:j1], nc.scalar.copy)
-            else:
-                interleave(g[:, :cut, :], z_f[b][:, :, j0 : j0 + cut], nc.scalar.copy)
-                interleave(g[:, cut:, :], z_f[b][:, :, j0 + cut : j1], nc.vector.tensor_copy)
+        def round_z(b, j0, j1, g, engine_copy=nc.scalar.copy):
+            interleave(g[:], z_f[b][:, :, j0:j1], engine_copy)
             quant(z_w[b][:, j0:j1], z_s[b][:, j0:j1], g[:].rearrange("p j t -> p (j t)"))
 
-        def y_passes(y, c, b, u):
+        def y_passes(y, c, b, u, lo, hi):
             cols = slice(c * P, (c + 1) * P)
             j0 = u * HALF
             nc.tensor.matmul_mx(
-                out=y[:, :HALF],
+                out=y[:, lo:hi],
                 lhsT=w2_w[b][:, cols].bitcast(FP8X4),
                 lhsT_scale=w2_s[b][:, cols],
-                rhs=z_w[b][:, j0 : j0 + HALF].bitcast(FP8X4),
-                rhs_scale=z_s[b][:, j0 : j0 + HALF],
+                rhs=z_w[b][:, j0 + lo : j0 + hi].bitcast(FP8X4),
+                rhs_scale=z_s[b][:, j0 + lo : j0 + hi],
                 start=(b == 0),
                 stop=False,
             )
-            for j in range(0, HALF, P):
+            for j in range(lo, hi, P):
                 nc.tensor.matmul_mx(
                     out=y[:, HALF + j : HALF + j + P],
                     lhsT=w4_w[:, b, 2 * c * P : 2 * (c + 1) * P].bitcast(FP4X4),
@@ -208,19 +202,16 @@ def tile_list_limb_pair_scores_kernel(
                 )
 
         def finish_y(y, c, u):
-            y_passes(y, c, 1, u)
             y1b = ring.tile([P, HALF], F32, name="y1b", bufs=4)
             nc.scalar.activation(out=y1b[:], in_=y[:, :HALF], func=ACT.Identity, bias=b3_sb[:, c : c + 1])
             res = ring.tile([P, HALF], F32, name="res", bufs=8)
             nc.vector.scalar_tensor_tensor(res[:], y[:, HALF:], b3_sb[:, c : c + 1], y1b[:], ALU.add, ALU.max)
             nc.sync.dma_start(out=out[c * P : (c + 1) * P, u * HALF : (u + 1) * HALF], in_=res[:])
 
-        for q in range(4):
-            rows = slice(32 * q, 32 * q + 4 * KA)
-            nc.vector.tensor_copy(tab_s[:].bitcast(I32)[rows, :], tab_s_in[rows, :])
-        nc.vector.tensor_copy(v_s[:], tab_s[:].indirect(offs_sb[:]))
         gather_tab(0)
         gather_tab(1)
+        v_s = keep.tile([P, S], U8, name="v_s", tag="tab_w1", align_bytes=64)
+        nc.vector.tensor_copy(v_s[:], tab_s[:].indirect(offs_sb[:]))
         acc0 = {(t, s): bank(2 * t + s) for t in range(PACK) for s in range(2)}
         g, dst, src = w1_views(0, 0)
         nc.scalar.copy(out=dst, in_=src)
@@ -290,12 +281,20 @@ def tile_list_limb_pair_scores_kernel(
         y = {(c, u): bank(4 * u + c) for u in range(2) for c in range(N // P)}
         for u in range(2):
             for c in range(N // P):
-                y_passes(y[c, u], c, 0, u)
-        pair(1, halves(2, HALF, J), late.tile([P, 2, P], F32, name="child_b", offset=4096, align_bytes=64))
+                y_passes(y[c, u], c, 0, u, 0, HALF)
+        cut = HALF + P
+        pair(1, [(2, HALF, cut), (3, HALF, cut)], late.tile([P, 2, P], F32, name="child_b", offset=4096, align_bytes=64))
         round_w2(1, late.tile([P, N * PACK], BF16, name="w2_g1", offset=8192, align_bytes=64)[:])
         round_z(1, 0, HALF, keep.tile([P, HALF, PACK], BF16, name="z_g1a", tag="slot_c", align_bytes=64))
-        pair(1, halves(3, HALF, J), keep.tile([P, 2, P], F32, name="child_c", tag="slot_c", align_bytes=64))
-        round_z(1, HALF, J, keep.tile([P, HALF, PACK], BF16, name="z_g1b", align_bytes=64), cut=80)
+        for c in range(N // P):
+            y_passes(y[c, 0], c, 1, 0, 0, HALF)
+        pair(1, [(2, cut, J), (3, cut, J)], keep.tile([P, 2, P], F32, name="child_c", tag="slot_c", align_bytes=64))
+        round_z(1, HALF, cut, keep.tile([P, P, PACK], BF16, name="z_g1b", align_bytes=64))
+        for c in range(N // P):
+            y_passes(y[c, 1], c, 1, 1, 0, P)
+        round_z(1, cut, J, keep.tile([P, P, PACK], BF16, name="z_g1c", align_bytes=64), nc.vector.tensor_copy)
+        for c in range(N // P):
+            y_passes(y[c, 1], c, 1, 1, P, HALF)
         for u in range(2):
             for c in range(N // P):
                 finish_y(y[c, u], c, u)

@@ -21,8 +21,10 @@ PACK = 4
 PASS = P * PACK
 KA = K // PASS
 HB = H // PASS
+NC = N // P
 BANK = 512
 HALF = J // 2
+KB = 1024
 
 
 def tile_list_limb_pair_scores_kernel(
@@ -31,33 +33,35 @@ def tile_list_limb_pair_scores_kernel(
     nc = tc.nc
     with ExitStack() as ctx:
         keep = ctx.enter_context(tc.tile_pool(name="keep", bufs=1))
-        late = ctx.enter_context(tc.tile_pool(name="late", bufs=1))
-        ring = ctx.enter_context(tc.tile_pool(name="ring", bufs=3))
+        arena = ctx.enter_context(tc.tile_pool(name="arena", bufs=1))
         psum = ctx.enter_context(tc.psum_pool(name="psum", bufs=1))
 
         def bank(i):
             return psum.tile([P, BANK], F32, name="bank%d" % i)
 
+        def own(name, shape, dtype):
+            return keep.tile([P] + shape, dtype, name=name, align_bytes=64)
+
+        def placed(name, shape, dtype, offset):
+            return arena.tile([P] + shape, dtype, name=name, offset=offset, align_bytes=64)
+
+        def tile_at(name, shape, dtype, offset):
+            return own(name, shape, dtype) if offset is None else placed(name, shape, dtype, offset)
+
         offs_sb = keep.tile([P, S // 16], U16, name="offs_sb")
         pos1_sb = keep.tile([P, J // 16], U16, name="pos1_sb")
         pos2_sb = keep.tile([P, J // 16], U16, name="pos2_sb")
-        tab_w = [keep.tile([P, T], I32, name="tab_w%d" % a, tag="tab_w%d" % a, align_bytes=64) for a in range(KA)]
-        tab_s = keep.tile([P, T], U8, name="tab_s", align_bytes=64)
-        w4_w = keep.tile([P, HB, 2 * N], U8, name="w4_w", align_bytes=64)
-        w4_s = keep.tile([P, HB, N], U8, name="w4_s", align_bytes=64)
-        b1_pad = late.tile([P, 1024 + 32], F32, name="b1_pad", offset=4096 - 64, align_bytes=64)
-        b1_sb = b1_pad[:, : HB * PACK].rearrange("p (b t) -> p b t", b=HB)
-        b3_sb = keep.tile([P, N // P], F32, name="b3_sb")
-        w1_raw = {
-            (a, b): keep.tile([P, PACK, PASS], F32, name="w1_raw%d%d" % (a, b), align_bytes=64)
-            for b in range(HB) for a in range(KA)
-        }
-        w2_raw = [keep.tile([P, PACK, N], F32, name="w2_raw%d" % b, align_bytes=64) for b in range(HB)]
-        warm = keep.tile([P, 8], F32, name="warm")
+        tab_w = [placed("tab_w%d" % a, [T], I32, 8 * KB * a) for a in range(KA)]
+        tab_s = placed("tab_s", [T], U8, 24 * KB)
+        w4_w = own("w4_w", [HB, 2 * N], U8)
+        w4_s = own("w4_s", [HB, N], U8)
+        b1_sb = own("b1_sb", [HB, PACK], F32)
+        b3_sb = own("b3_sb", [NC], F32)
+        w1_raw = {(a, b): own("w1_raw%d%d" % (a, b), [PACK, PASS], F32) for b in range(HB) for a in range(KA)}
+        w2_raw = [own("w2_raw%d" % b, [PACK, N], F32) for b in range(HB)]
 
         nc.gpsimd.memset(tab_s[:].bitcast(I32), 0)
         nc.vector.memset(w4_s[:].rearrange("p b n -> p (b n)").bitcast(I32), 0)
-        nc.vector.memset(warm[:, 0:4], 0.0)
 
         def load_tab(a):
             nc.sync.dma_start(out=tab_w[a][:], in_=tab_words[a].rearrange("p t i -> p (t i)").bitcast(I32))
@@ -69,18 +73,16 @@ def tile_list_limb_pair_scores_kernel(
         load_tab(0)
         nc.sync.dma_start(offs_sb[:], offs)
         for q in range(4):
-            queue = nc.gpsimd if q < 3 else nc.scalar
-            queue.dma_start(
+            nc.gpsimd.dma_start(
                 out=tab_s[32 * q : 32 * q + 4 * KA, :].bitcast(I32),
                 in_=tab_scales[:, 4 * q : 4 * q + 4, :].bitcast(I32),
             )
-        nc.scalar.dma_start(out=b1_sb, in_=b1.rearrange("(b p t) -> p b t", b=HB, t=PACK))
-        nc.scalar.activation(out=warm[:, 4:8], in_=warm[:, 0:4], func=ACT.Relu)
         load_tab(1)
-        load_w1(0, 0)
         load_tab(2)
+        load_w1(0, 0)
         load_w1(1, 0)
         load_w1(2, 0)
+        nc.sync.dma_start(out=b1_sb[:], in_=b1.rearrange("(b p t) -> p b t", b=HB, t=PACK))
         nc.sync.dma_start(pos2_sb[:], pos2)
         nc.sync.dma_start(pos1_sb[:], pos1)
         for a in range(KA):
@@ -98,68 +100,70 @@ def tile_list_limb_pair_scores_kernel(
         with nc.allow_non_contiguous_dma(reason="one bias value a partition"):
             nc.sync.dma_start(out=b3_sb[:], in_=b3.rearrange("(c p) -> p c", p=P))
 
-        v_w = [keep.tile([P, S], U32, name="v_w%d" % a, align_bytes=64) for a in range(KA)]
-        w1_w = {ab: keep.tile([P, PASS], U32, name="w1_w%d%d" % ab, align_bytes=64) for ab in w1_raw}
-        w1_s = {
-            ab: keep.tile([P, PASS], U8, name="w1_s%d%d" % ab, align_bytes=64)
-            for ab in w1_raw
-        }
-        w2_w = [keep.tile([P, N], U32, name="w2_w%d" % b, align_bytes=64) for b in range(HB)]
-        w2_s = [keep.tile([P, N], U8, name="w2_s%d" % b, align_bytes=64) for b in range(HB)]
-        h = {
-            (b, t): keep.tile([P, S], F32, name="h%d%d" % (b, t), align_bytes=64)
-            for b in range(HB) for t in range(PACK)
-        }
-        z_f = [keep.tile([P, PACK, J], F32, name="z_f%d" % b, align_bytes=64) for b in range(HB)]
-        z_w = [keep.tile([P, J], U32, name="z_w%d" % b, align_bytes=64) for b in range(HB)]
-        z_s = [keep.tile([P, J], U8, name="z_s%d" % b, align_bytes=64) for b in range(HB)]
+        pieces = [(a, b, u) for b in range(HB) for a in range(KA) for u in range(2)]
+        v_w = [own("v_w0", [S], U32), own("v_w1", [S], U32), own("v_w2", [S], U32)]
+        w1_w_at = {(2, 0, 0): 11 * KB, (1, 0, 0): 18 * KB, (1, 1, 0): 21 * KB + 512, (2, 1, 1): 32 * KB + 512}
+        w1_s_at = {(1, 0, 0): 24 * KB, (1, 0, 1): 24 * KB + 256, (2, 0, 1): 24 * KB + 512, (2, 0, 0): 2 * KB + 512, (2, 1, 1): 38 * KB - 128}
+        w1_w = {k: tile_at("w1_w%d%d%d" % k, [2 * P], U32, w1_w_at.get(k)) for k in pieces}
+        w1_s = {k: tile_at("w1_s%d%d%d" % k, [2 * P], U8, w1_s_at.get(k)) for k in pieces}
+        w2_w = [own("w2_w%d" % b, [N], U32) for b in range(HB)]
+        w2_s = [own("w2_s%d" % b, [N], U8) for b in range(HB)]
+        h_at = {(0, 2): 3 * KB + 512, (0, 3): 12 * KB}
+        h = {(b, t): tile_at("h%d%d" % (b, t), [S], F32, h_at.get((b, t))) for b in range(HB) for t in range(PACK)}
+        z_f = [own("z_f%d" % b, [PACK, J], F32) for b in range(HB)]
+        z_w = [own("z_w%d" % b, [J], U32) for b in range(HB)]
+        z_s = [own("z_s%d" % b, [J], U8) for b in range(HB)]
 
         def gather_tab(a):
             nc.vector.tensor_copy(v_w[a][:], tab_w[a][:].bitcast(U32).indirect(offs_sb[:]))
 
-        def w1_views(a, b):
-            g = ring.tile([P, PASS * PACK], BF16, name="grouped", align_bytes=64)
-            dst = g[:].rearrange("p (u t m i) -> p u m i t", u=2, t=2, i=PACK)
-            src = w1_raw[a, b][:].rearrange("p i (m u t) -> p u m i t", u=2, t=2)
-            return g, dst, src
-
         def quant(words, scales, src):
             nc.vector.quantize_mx(out=words.bitcast(FP8X4), scales=scales, in_=src)
 
-        def interleave(dst, src, engine_copy):
+        def round_w1(g, a, b, u, engine_copy, m0=0, m1=P):
+            dst = g[:].rearrange("p (t m i) -> p m i t", t=2, i=PACK)
+            src = w1_raw[a, b][:].rearrange("p i (m u t) -> p u m i t", u=2, t=2)
+            engine_copy(out=dst[:, m0:m1], in_=src[:, u, m0:m1])
+
+        def quant_w1(g, a, b, u):
+            quant(w1_w[a, b, u][:], w1_s[a, b, u][:], g[:])
+
+        def interleave(g, src, engine_copy):
             engine_copy(
-                out=dst.rearrange("p (c u) t -> p c t u", u=4),
+                out=g[:].rearrange("p (c u t) -> p c t u", u=4, t=PACK),
                 in_=src.rearrange("p t (c u) -> p c t u", u=4),
             )
 
-        def round_w2(b, g):
-            interleave(g.rearrange("p (n i) -> p n i", i=PACK), w2_raw[b][:], nc.scalar.copy)
-            quant(w2_w[b][:], w2_s[b][:], g)
-
         def h_pass(acc, a, b, t, s, start, stop):
-            cols = slice(t * P, (t + 1) * P)
+            cols = slice((t % 2) * P, (t % 2 + 1) * P)
             ent = slice(s * BANK, (s + 1) * BANK)
             nc.tensor.matmul_mx(
                 out=acc[:],
-                lhsT=w1_w[a, b][:, cols].bitcast(FP8X4),
-                lhsT_scale=w1_s[a, b][:, cols],
+                lhsT=w1_w[a, b, t // 2][:, cols].bitcast(FP8X4),
+                lhsT_scale=w1_s[a, b, t // 2][:, cols],
                 rhs=v_w[a][:, ent].bitcast(FP8X4),
                 rhs_scale=v_s[4 * a :, ent],
                 start=start,
                 stop=stop,
             )
 
+        def h_passes(acc, b, t, order, first=False, last=True):
+            for a in order:
+                for s in range(2):
+                    h_pass(acc[t, s], a, b, t, s, first and a == order[0], last and a == order[-1])
+
         def evict_h(acc, b, t, s, on_vector=False):
             dst = h[b, t][:, s * BANK : (s + 1) * BANK]
             if on_vector:
-                nc.vector.tensor_scalar(dst, acc[:], b1_sb[:, b, t : t + 1], 0.0, ALU.add, ALU.max)
+                nc.vector.tensor_scalar(dst, acc[t, s][:], b1_sb[:, b, t : t + 1], 0.0, ALU.add, ALU.max)
             else:
-                nc.scalar.activation(out=dst, in_=acc[:], func=ACT.Relu, bias=b1_sb[:, b, t : t + 1])
+                nc.scalar.activation(out=dst, in_=acc[t, s][:], func=ACT.Relu, bias=b1_sb[:, b, t : t + 1])
 
-        def pair(b, units, child=None):
-            width = units[0][2] - units[0][1]
-            if child is None:
-                child = ring.tile([P, 2, width], F32, name="child", align_bytes=64)
+        def evict_slice(acc, b, t):
+            for s in range(2):
+                evict_h(acc, b, t, s)
+
+        def pair(b, units, child):
             for n, (t, j0, j1) in enumerate(units):
                 nc.vector.tensor_copy(child[:, n, :], h[b, t][:].indirect(pos2_sb[:, j0 // 16 : j1 // 16]))
             for n, (t, j0, j1) in enumerate(units):
@@ -170,131 +174,180 @@ def tile_list_limb_pair_scores_kernel(
                     ALU.subtract,
                 )
 
-        def halves(t, j0, j1):
-            mid = (j0 + j1) // 2
-            return [(t, j0, mid), (t, mid, j1)]
+        def slice_pairs(b, t, offset=None):
+            name = "child%d%d" % (b, t)
+            child = own(name, [2, HALF], F32) if offset is None else placed(name, [2, HALF], F32, offset)
+            pair(b, [(t, 0, HALF), (t, HALF, J)], child)
 
-        def round_z(b, j0, j1, g, engine_copy=nc.scalar.copy):
-            interleave(g[:], z_f[b][:, :, j0:j1], engine_copy)
-            quant(z_w[b][:, j0:j1], z_s[b][:, j0:j1], g[:].rearrange("p j t -> p (j t)"))
+        def scalar_identity(out, in_):
+            nc.scalar.activation(out=out, in_=in_, func=ACT.Identity)
 
-        def y_passes(y, c, b, u, lo, hi):
+        def quant_w2(g, b, n0, n1):
+            quant(w2_w[b][:, n0:n1], w2_s[b][:, n0:n1], g[:])
+
+        def quant_z(g, b, j0, j1):
+            quant(z_w[b][:, j0:j1], z_s[b][:, j0:j1], g[:])
+
+        def y_passes(y, col, c, b, j0, j1, start, stop):
+            width = j1 - j0
             cols = slice(c * P, (c + 1) * P)
-            j0 = u * HALF
             nc.tensor.matmul_mx(
-                out=y[:, lo:hi],
+                out=y[:, col : col + width],
                 lhsT=w2_w[b][:, cols].bitcast(FP8X4),
                 lhsT_scale=w2_s[b][:, cols],
-                rhs=z_w[b][:, j0 + lo : j0 + hi].bitcast(FP8X4),
-                rhs_scale=z_s[b][:, j0 + lo : j0 + hi],
-                start=(b == 0),
+                rhs=z_w[b][:, j0:j1].bitcast(FP8X4),
+                rhs_scale=z_s[b][:, j0:j1],
+                start=start,
                 stop=False,
             )
-            for j in range(lo, hi, P):
+            for j in range(0, width, P):
                 nc.tensor.matmul_mx(
-                    out=y[:, HALF + j : HALF + j + P],
+                    out=y[:, col + width + j : col + width + j + P],
                     lhsT=w4_w[:, b, 2 * c * P : 2 * (c + 1) * P].bitcast(FP4X4),
                     lhsT_scale=w4_s[:, b, cols],
                     rhs=z_w[b][:, j0 + j : j0 + j + P].bitcast(FP8X4),
                     rhs_scale=z_s[b][:, j0 + j : j0 + j + P],
                     start=False,
-                    stop=(b == HB - 1 and j + P == HALF),
+                    stop=(stop and j + P == width),
                 )
 
-        def finish_y(y, c, u):
-            y1b = ring.tile([P, HALF], F32, name="y1b", bufs=4)
-            nc.scalar.activation(out=y1b[:], in_=y[:, :HALF], func=ACT.Identity, bias=b3_sb[:, c : c + 1])
-            res = ring.tile([P, HALF], F32, name="res", bufs=8)
-            nc.vector.scalar_tensor_tensor(res[:], y[:, HALF:], b3_sb[:, c : c + 1], y1b[:], ALU.add, ALU.max)
-            nc.sync.dma_start(out=out[c * P : (c + 1) * P, u * HALF : (u + 1) * HALF], in_=res[:])
+        def run_passes(banks, b, j0, j1):
+            per_bank = NC // len(banks)
+            for c in range(NC):
+                n = c % per_bank
+                y_passes(banks[c // per_bank], 2 * n * (j1 - j0), c, b, j0, j1,
+                         b == 0 and n == 0, b == HB - 1 and n == per_bank - 1)
 
-        gather_tab(0)
-        gather_tab(1)
-        v_s = keep.tile([P, S], U8, name="v_s", tag="tab_w1", align_bytes=64)
-        nc.vector.tensor_copy(v_s[:], tab_s[:].indirect(offs_sb[:]))
+        def finish_run(banks, j0, j1, stores):
+            width = j1 - j0
+            per_bank = NC // len(banks)
+            per_store = NC // stores
+            for c in range(NC):
+                if c % per_store == 0:
+                    res = own("res%d_%d" % (j0, c), [per_store, width], F32)
+                y = banks[c // per_bank]
+                col = 2 * (c % per_bank) * width
+                y1b = own("y1b%d_%d" % (j0, c), [width], F32)
+                nc.scalar.activation(out=y1b[:], in_=y[:, col : col + width], func=ACT.Identity, bias=b3_sb[:, c : c + 1])
+                nc.vector.scalar_tensor_tensor(
+                    res[:, c % per_store, :], y[:, col + width : col + 2 * width], b3_sb[:, c : c + 1], y1b[:], ALU.add, ALU.max
+                )
+                if c % per_store == per_store - 1:
+                    rows = out[(c + 1 - per_store) * P : (c + 1) * P, j0:j1]
+                    nc.sync.dma_start(out=rows.rearrange("(c p) j -> p c j", p=P), in_=res[:])
+
+        def stage(name, offset, width=2 * PASS):
+            return placed(name, [width], BF16, offset)
+
+        for a in range(KA):
+            gather_tab(a)
         acc0 = {(t, s): bank(2 * t + s) for t in range(PACK) for s in range(2)}
-        g, dst, src = w1_views(0, 0)
-        nc.scalar.copy(out=dst, in_=src)
-        quant(w1_w[0, 0][:], w1_s[0, 0][:], g[:])
-        for t in range(PACK):
-            for s in range(2):
-                h_pass(acc0[t, s], 0, 0, t, s, True, False)
-        gather_tab(2)
-        g, dst, src = w1_views(1, 0)
-        nc.scalar.copy(out=dst[:, :, :88], in_=src[:, :, :88])
-        nc.vector.tensor_copy(out=dst[:, :, 88:], in_=src[:, :, 88:])
-        quant(w1_w[1, 0][:], w1_s[1, 0][:], g[:])
-        g, dst, src = w1_views(2, 0)
-        nc.scalar.copy(out=dst[:, 0, :40], in_=src[:, 0, :40])
-        nc.vector.tensor_copy(out=dst[:, 0, 40:], in_=src[:, 0, 40:])
-        quant(w1_w[2, 0][:, : 2 * P], w1_s[2, 0][:, : 2 * P], g[:, : 2 * PASS])
-        nc.scalar.copy(out=dst[:, 1], in_=src[:, 1])
-        quant(w1_w[2, 0][:, 2 * P :], w1_s[2, 0][:, 2 * P :], g[:, 2 * PASS :])
-        for t in range(PACK):
-            order = (1, 2) if t == 0 else (2, 1)
-            for a in order:
-                for s in range(2):
-                    h_pass(acc0[t, s], a, 0, t, s, False, a == order[-1])
-
-        def finish0(t):
-            for s in range(2):
-                evict_h(acc0[t, s], 0, t, s, on_vector=(t == 0 and s == 1))
-            pair(0, halves(t, 0, J))
-
-        def prep1(a, engine_copy):
-            g, dst, src = w1_views(a, 1)
-            engine_copy(out=dst, in_=src)
-            quant(w1_w[a, 1][:], w1_s[a, 1][:], g[:])
-
-        finish0(0)
-        finish0(1)
-        prep1(0, nc.scalar.copy)
-        finish0(2)
-        prep1(1, nc.scalar.copy)
-        prep1(2, nc.scalar.copy)
-        acc1 = {(t, s): bank(2 * t + s) for t in range(PACK - 1) for s in range(2)}
-        for t in range(PACK - 1):
-            for s in range(2):
-                h_pass(acc1[t, s], 0, 1, t, s, True, False)
-        for t in range(PACK - 1):
-            order = (1, 2) if t == 0 else (2, 1)
-            for a in order:
-                for s in range(2):
-                    h_pass(acc1[t, s], a, 1, t, s, False, a == order[-1])
-        order = (0, 1, 2)
-        finish0(3)
-        for s in range(2):
-            acc1[3, s] = bank(6 + s)
-            for a in order:
-                h_pass(acc1[3, s], a, 1, 3, s, a == order[0], a == order[-1])
-        for t in range(PACK):
-            for s in range(2):
-                evict_h(acc1[t, s], 1, t, s)
-
-        pass
-        pair(1, halves(0, 0, J))
-        pair(1, halves(1, 0, J))
-        round_z(0, 0, J, late.tile([P, J, PACK], BF16, name="z_g0", offset=0, align_bytes=64))
-        pair(1, [(2, 0, HALF), (3, 0, HALF)], late.tile([P, 2, HALF], F32, name="child_a", offset=0, align_bytes=64))
-        pass
-        round_w2(0, late.tile([P, N * PACK], BF16, name="w2_g0", offset=4096, align_bytes=64)[:])
-        y = {(c, u): bank(4 * u + c) for u in range(2) for c in range(N // P)}
+        g0_at = {(0, 1): 27 * KB, (2, 0): 25 * KB}
+        g0 = {(a, u): tile_at("g0_%d%d" % (a, u), [2 * PASS], BF16, g0_at.get((a, u))) for a in range(KA) for u in range(2)}
+        round_w1(g0[0, 0], 0, 0, 0, scalar_identity)
+        round_w1(g0[0, 1], 0, 0, 1, nc.vector.tensor_copy)
         for u in range(2):
-            for c in range(N // P):
-                y_passes(y[c, u], c, 0, u, 0, HALF)
+            quant_w1(g0[0, u], 0, 0, u)
+        v_s = placed("v_s", [S], U8, 28 * KB)
+        nc.vector.tensor_copy(v_s[:], tab_s[:].indirect(offs_sb[:]))
+        for u in range(2):
+            round_w1(g0[1, u], 1, 0, u, nc.scalar.copy)
+        quant_w1(g0[1, 0], 1, 0, 0)
+        round_w1(g0[2, 0], 2, 0, 0, nc.vector.tensor_copy)
+        quant_w1(g0[1, 1], 1, 0, 1)
+        quant_w1(g0[2, 0], 2, 0, 0)
+        round_w1(g0[2, 1], 2, 0, 1, nc.scalar.copy)
+        h_passes(acc0, 0, 0, (0, 1, 2), first=True)
+        h_passes(acc0, 0, 1, (2, 1, 0), first=True)
+        quant_w1(g0[2, 1], 2, 0, 1)
+        h_passes(acc0, 0, 2, (2, 1, 0), first=True)
+        h_passes(acc0, 0, 3, (2, 1, 0), first=True)
+        evict_h(acc0, 0, 0, 0)
+        evict_h(acc0, 0, 0, 1, on_vector=True)
+
+        acc1 = {}
+        slice_pairs(0, 0)
+        evict_slice(acc0, 0, 1)
+        g010 = stage("g010", 2 * KB)
+        round_w1(g010, 0, 1, 0, nc.scalar.copy)
+        quant_w1(g010, 0, 1, 0)
+        for t in range(2):
+            for s in range(2):
+                acc1[t, s] = bank(2 * t + s)
+            h_passes(acc1, 1, t, (0,), first=True, last=False)
+        slice_pairs(0, 1, 512)
+        g110 = stage("g110", 10 * KB + 512)
+        round_w1(g110, 1, 1, 0, nc.scalar.copy)
+        quant_w1(g110, 1, 1, 0)
+        evict_slice(acc0, 0, 2)
+        slice_pairs(0, 2, 9 * KB)
+        g210 = stage("g210", 17 * KB + 512)
+        round_w1(g210, 2, 1, 0, nc.scalar.copy)
+        quant_w1(g210, 2, 1, 0)
+        h_passes(acc1, 1, 0, (1, 2))
+        h_passes(acc1, 1, 1, (2, 1))
+        evict_slice(acc0, 0, 3)
+        slice_pairs(0, 3, 16 * KB)
+        g011 = stage("g011", KB)
+        round_w1(g011, 0, 1, 1, nc.scalar.copy)
+        quant_w1(g011, 0, 1, 1)
+        g111 = stage("g111", 19 * KB)
+        round_w1(g111, 1, 1, 1, nc.scalar.copy)
+        quant_w1(g111, 1, 1, 1)
+        for t in range(2, PACK):
+            for s in range(2):
+                acc1[t, s] = bank(2 * t + s)
+            h_passes(acc1, 1, t, (0, 1), first=True, last=False)
+
+        evict_slice(acc1, 1, 0)
+        slice_pairs(1, 0)
+        evict_slice(acc1, 1, 1)
+        g211 = stage("g211", 21 * KB)
+        round_w1(g211, 2, 1, 1, nc.scalar.copy)
+        quant_w1(g211, 2, 1, 1)
+        for t in range(2, PACK):
+            h_passes(acc1, 1, t, (2,))
+        gz0a = own("gz0a", [2 * PASS], BF16)
+        interleave(gz0a, z_f[0][:, :, :HALF], nc.scalar.copy)
+        slice_pairs(1, 1, 22 * KB + 512)
+        quant_z(gz0a, 0, 0, HALF)
+        evict_slice(acc1, 1, 2)
+        evict_slice(acc1, 1, 3)
+        pair(1, [(2, 0, HALF), (3, 0, HALF)], own("child_a", [2, HALF], F32))
+        gw2 = {(0, 0): stage("gw200", 31 * KB), (0, 1): stage("gw201", 33 * KB), (1, 0): stage("gw210", 36 * KB), (1, 1): stage("gw211", 38 * KB)}
+
+        def round_w2(b, n, engine_copy):
+            interleave(gw2[b, n], w2_raw[b][:, :, n * HALF : (n + 1) * HALF], engine_copy)
+            quant_w2(gw2[b, n], b, n * HALF, (n + 1) * HALF)
+
+        round_w2(0, 0, nc.scalar.copy)
+        round_w2(0, 1, nc.scalar.copy)
+        y_a = [bank(c) for c in range(NC)]
+        run_passes(y_a, 0, 0, HALF)
         cut = HALF + P
-        pair(1, [(2, HALF, cut), (3, HALF, cut)], late.tile([P, 2, P], F32, name="child_b", offset=4096, align_bytes=64))
-        round_w2(1, late.tile([P, N * PACK], BF16, name="w2_g1", offset=8192, align_bytes=64)[:])
-        round_z(1, 0, HALF, keep.tile([P, HALF, PACK], BF16, name="z_g1a", tag="slot_c", align_bytes=64))
-        for c in range(N // P):
-            y_passes(y[c, 0], c, 1, 0, 0, HALF)
-        pair(1, [(2, cut, J), (3, cut, J)], keep.tile([P, 2, P], F32, name="child_c", tag="slot_c", align_bytes=64))
-        round_z(1, HALF, cut, keep.tile([P, P, PACK], BF16, name="z_g1b", align_bytes=64))
-        for c in range(N // P):
-            y_passes(y[c, 1], c, 1, 1, 0, P)
-        round_z(1, cut, J, keep.tile([P, P, PACK], BF16, name="z_g1c", align_bytes=64), nc.vector.tensor_copy)
-        for c in range(N // P):
-            y_passes(y[c, 1], c, 1, 1, P, HALF)
-        for u in range(2):
-            for c in range(N // P):
-                finish_y(y[c, u], c, u)
+        pair(1, [(2, HALF, cut), (3, HALF, cut)], placed("child_b", [2, P], F32, 31 * KB))
+        round_w2(1, 0, nc.scalar.copy)
+        round_w2(1, 1, nc.scalar.copy)
+        pair(1, [(2, cut, J), (3, cut, J)], placed("child_c", [2, P], F32, 36 * KB))
+        gz1a = stage("gz1a", 40 * KB)
+        interleave(gz1a, z_f[1][:, :, :HALF], nc.scalar.copy)
+        quant_z(gz1a, 1, 0, HALF)
+        run_passes(y_a, 1, 0, HALF)
+        gz0b = stage("gz0b", 42 * KB)
+        interleave(gz0b, z_f[0][:, :, HALF:], nc.vector.tensor_copy)
+        gz1b = stage("gz1b", 44 * KB, PASS)
+        interleave(gz1b, z_f[1][:, :, HALF:cut], nc.scalar.copy)
+        quant_z(gz0b, 0, HALF, J)
+        y_b = [bank(4), bank(5)]
+        y_c = [bank(6), bank(7)]
+        run_passes(y_b, 0, HALF, cut)
+        run_passes(y_c, 0, cut, J)
+        quant_z(gz1b, 1, HALF, cut)
+        run_passes(y_b, 1, HALF, cut)
+        gz1c = stage("gz1c", 45 * KB, PASS)
+        interleave(gz1c, z_f[1][:, :, cut:], nc.vector.tensor_copy)
+        quant_z(gz1c, 1, cut, J)
+        run_passes(y_c, 1, cut, J)
+        finish_run(y_a, 0, HALF, 2)
+        finish_run(y_b, HALF, cut, 1)
+        finish_run(y_c, cut, J, 2)

@@ -61,7 +61,7 @@ def tile_list_limb_pair_scores_kernel(
         w2_raw = [own("w2_raw%d" % b, [PACK, N], F32) for b in range(HB)]
 
         nc.gpsimd.memset(tab_s[:].bitcast(I32), 0)
-        nc.vector.memset(w4_s[:].rearrange("p b n -> p (b n)").bitcast(I32), 0)
+        nc.gpsimd.memset(w4_s[:].rearrange("p b n -> p (b n)").bitcast(I32), 0)
 
         def load_tab(a):
             nc.sync.dma_start(out=tab_w[a][:], in_=tab_words[a].rearrange("p t i -> p (t i)").bitcast(I32))
@@ -72,17 +72,17 @@ def tile_list_limb_pair_scores_kernel(
 
         load_tab(0)
         nc.sync.dma_start(offs_sb[:], offs)
+        nc.scalar.dma_start(out=b1_sb[:], in_=b1.rearrange("(b p t) -> p b t", b=HB, t=PACK))
         for q in range(4):
-            nc.gpsimd.dma_start(
+            nc.scalar.dma_start(
                 out=tab_s[32 * q : 32 * q + 4 * KA, :].bitcast(I32),
                 in_=tab_scales[:, 4 * q : 4 * q + 4, :].bitcast(I32),
             )
         load_tab(1)
-        load_tab(2)
         load_w1(0, 0)
         load_w1(1, 0)
+        load_tab(2)
         load_w1(2, 0)
-        nc.sync.dma_start(out=b1_sb[:], in_=b1.rearrange("(b p t) -> p b t", b=HB, t=PACK))
         nc.sync.dma_start(pos2_sb[:], pos2)
         nc.sync.dma_start(pos1_sb[:], pos1)
         for a in range(KA):
@@ -101,16 +101,22 @@ def tile_list_limb_pair_scores_kernel(
             nc.sync.dma_start(out=b3_sb[:], in_=b3.rearrange("(c p) -> p c", p=P))
 
         pieces = [(a, b, u) for b in range(HB) for a in range(KA) for u in range(2)]
-        v_w = [own("v_w0", [S], U32), own("v_w1", [S], U32), own("v_w2", [S], U32)]
-        w1_w_at = {(2, 0, 0): 11 * KB, (1, 0, 0): 18 * KB, (1, 1, 0): 21 * KB + 512, (2, 1, 1): 32 * KB + 512}
-        w1_s_at = {(1, 0, 0): 24 * KB, (1, 0, 1): 24 * KB + 256, (2, 0, 1): 24 * KB + 512, (2, 0, 0): 2 * KB + 512, (2, 1, 1): 38 * KB - 128}
+        v_w = [own("v_w0", [S], U32), own("v_w1", [S], U32), placed("v_w2", [S], U32, 29 * KB)]
+        w1_w_at = {(2, 0, 0): KB + 512, (2, 0, 1): 5 * KB + 512, (2, 1, 0): 12 * KB, (2, 1, 1): 17 * KB + 512}
+        w1_s_at = {(0, 0, 0): 24 * KB, (2, 0, 1): 10 * KB - 128, (2, 1, 1): 20 * KB}
         w1_w = {k: tile_at("w1_w%d%d%d" % k, [2 * P], U32, w1_w_at.get(k)) for k in pieces}
         w1_s = {k: tile_at("w1_s%d%d%d" % k, [2 * P], U8, w1_s_at.get(k)) for k in pieces}
         w2_w = [own("w2_w%d" % b, [N], U32) for b in range(HB)]
         w2_s = [own("w2_s%d" % b, [N], U8) for b in range(HB)]
-        h_at = {(0, 2): 3 * KB + 512, (0, 3): 12 * KB}
-        h = {(b, t): tile_at("h%d%d" % (b, t), [S], F32, h_at.get((b, t))) for b in range(HB) for t in range(PACK)}
-        z_f = [own("z_f%d" % b, [PACK, J], F32) for b in range(HB)]
+        h = {(b, t): own("h%d%d" % (b, t), [S], F32) for b in range(HB) for t in range(PACK)}
+        cut = HALF + P
+        runs = {0: [(0, HALF), (HALF, J)], 1: [(0, HALF), (HALF, J)]}
+        z_f = {(b, j0): own("z_f%d_%d" % (b, j0), [PACK, j1 - j0], F32) for b in range(HB) for j0, j1 in runs[b]}
+
+        def z_part(b, t, j0, j1):
+            r0 = max(x for x, y in runs[b] if x <= j0)
+            return z_f[b, r0][:, t, j0 - r0 : j1 - r0]
+
         z_w = [own("z_w%d" % b, [J], U32) for b in range(HB)]
         z_s = [own("z_s%d" % b, [J], U8) for b in range(HB)]
 
@@ -164,20 +170,19 @@ def tile_list_limb_pair_scores_kernel(
                 evict_h(acc, b, t, s)
 
         def pair(b, units, child):
+            ends = [sum(j1 - j0 for t, j0, j1 in units[:n]) for n in range(len(units) + 1)]
             for n, (t, j0, j1) in enumerate(units):
-                nc.vector.tensor_copy(child[:, n, :], h[b, t][:].indirect(pos2_sb[:, j0 // 16 : j1 // 16]))
+                nc.vector.tensor_copy(child[:, ends[n] : ends[n + 1]], h[b, t][:].indirect(pos2_sb[:, j0 // 16 : j1 // 16]))
             for n, (t, j0, j1) in enumerate(units):
                 nc.vector.tensor_tensor(
-                    z_f[b][:, t, j0:j1],
+                    z_part(b, t, j0, j1),
                     h[b, t][:].indirect(pos1_sb[:, j0 // 16 : j1 // 16]),
-                    child[:, n, :],
+                    child[:, ends[n] : ends[n + 1]],
                     ALU.subtract,
                 )
 
         def slice_pairs(b, t, offset=None):
-            name = "child%d%d" % (b, t)
-            child = own(name, [2, HALF], F32) if offset is None else placed(name, [2, HALF], F32, offset)
-            pair(b, [(t, 0, HALF), (t, HALF, J)], child)
+            pair(b, [(t, 0, HALF), (t, HALF, J)], tile_at("child%d%d" % (b, t), [J], F32, offset))
 
         def scalar_identity(out, in_):
             nc.scalar.activation(out=out, in_=in_, func=ACT.Identity)
@@ -188,166 +193,126 @@ def tile_list_limb_pair_scores_kernel(
         def quant_z(g, b, j0, j1):
             quant(z_w[b][:, j0:j1], z_s[b][:, j0:j1], g[:])
 
-        def y_passes(y, col, c, b, j0, j1, start, stop):
-            width = j1 - j0
-            cols = slice(c * P, (c + 1) * P)
-            nc.tensor.matmul_mx(
-                out=y[:, col : col + width],
-                lhsT=w2_w[b][:, cols].bitcast(FP8X4),
-                lhsT_scale=w2_s[b][:, cols],
-                rhs=z_w[b][:, j0:j1].bitcast(FP8X4),
-                rhs_scale=z_s[b][:, j0:j1],
-                start=start,
-                stop=False,
-            )
-            for j in range(0, width, P):
+        def y_passes(y, u, b, j0, j1):
+            for c in range(NC):
+                cols = slice(c * P, (c + 1) * P)
+                lo, hi = j0 - u * HALF, j1 - u * HALF
                 nc.tensor.matmul_mx(
-                    out=y[:, col + width + j : col + width + j + P],
-                    lhsT=w4_w[:, b, 2 * c * P : 2 * (c + 1) * P].bitcast(FP4X4),
-                    lhsT_scale=w4_s[:, b, cols],
-                    rhs=z_w[b][:, j0 + j : j0 + j + P].bitcast(FP8X4),
-                    rhs_scale=z_s[b][:, j0 + j : j0 + j + P],
-                    start=False,
-                    stop=(stop and j + P == width),
+                    out=y[c][:, lo:hi],
+                    lhsT=w2_w[b][:, cols].bitcast(FP8X4),
+                    lhsT_scale=w2_s[b][:, cols],
+                    rhs=z_w[b][:, j0:j1].bitcast(FP8X4),
+                    rhs_scale=z_s[b][:, j0:j1],
+                    start=(b == 0),
+                    stop=False,
                 )
+                for j in range(lo, hi, P):
+                    nc.tensor.matmul_mx(
+                        out=y[c][:, HALF + j : HALF + j + P],
+                        lhsT=w4_w[:, b, 2 * c * P : 2 * (c + 1) * P].bitcast(FP4X4),
+                        lhsT_scale=w4_s[:, b, cols],
+                        rhs=z_w[b][:, u * HALF + j : u * HALF + j + P].bitcast(FP8X4),
+                        rhs_scale=z_s[b][:, u * HALF + j : u * HALF + j + P],
+                        start=False,
+                        stop=(b == HB - 1 and j + P == HALF),
+                    )
 
-        def run_passes(banks, b, j0, j1):
-            per_bank = NC // len(banks)
+        def finish_y(y, u):
             for c in range(NC):
-                n = c % per_bank
-                y_passes(banks[c // per_bank], 2 * n * (j1 - j0), c, b, j0, j1,
-                         b == 0 and n == 0, b == HB - 1 and n == per_bank - 1)
-
-        def finish_run(banks, j0, j1, stores):
-            width = j1 - j0
-            per_bank = NC // len(banks)
-            per_store = NC // stores
-            for c in range(NC):
-                if c % per_store == 0:
-                    res = own("res%d_%d" % (j0, c), [per_store, width], F32)
-                y = banks[c // per_bank]
-                col = 2 * (c % per_bank) * width
-                y1b = own("y1b%d_%d" % (j0, c), [width], F32)
-                nc.scalar.activation(out=y1b[:], in_=y[:, col : col + width], func=ACT.Identity, bias=b3_sb[:, c : c + 1])
-                nc.vector.scalar_tensor_tensor(
-                    res[:, c % per_store, :], y[:, col + width : col + 2 * width], b3_sb[:, c : c + 1], y1b[:], ALU.add, ALU.max
-                )
-                if c % per_store == per_store - 1:
-                    rows = out[(c + 1 - per_store) * P : (c + 1) * P, j0:j1]
-                    nc.sync.dma_start(out=rows.rearrange("(c p) j -> p c j", p=P), in_=res[:])
+                y1b = own("y1b%d_%d" % (u, c), [HALF], F32)
+                nc.scalar.activation(out=y1b[:], in_=y[c][:, :HALF], func=ACT.Identity, bias=b3_sb[:, c : c + 1])
+                res = own("res%d_%d" % (u, c), [HALF], F32)
+                nc.vector.scalar_tensor_tensor(res[:], y[c][:, HALF:], b3_sb[:, c : c + 1], y1b[:], ALU.add, ALU.max)
+                nc.sync.dma_start(out=out[c * P : (c + 1) * P, u * HALF : (u + 1) * HALF], in_=res[:])
 
         def stage(name, offset, width=2 * PASS):
             return placed(name, [width], BF16, offset)
 
-        for a in range(KA):
-            gather_tab(a)
-        acc0 = {(t, s): bank(2 * t + s) for t in range(PACK) for s in range(2)}
-        g0_at = {(0, 1): 27 * KB, (2, 0): 25 * KB}
-        g0 = {(a, u): tile_at("g0_%d%d" % (a, u), [2 * PASS], BF16, g0_at.get((a, u))) for a in range(KA) for u in range(2)}
-        round_w1(g0[0, 0], 0, 0, 0, scalar_identity)
-        round_w1(g0[0, 1], 0, 0, 1, nc.vector.tensor_copy)
-        for u in range(2):
-            quant_w1(g0[0, u], 0, 0, u)
-        v_s = placed("v_s", [S], U8, 28 * KB)
+        gather_tab(0)
+        gather_tab(1)
+        v_s = placed("v_s", [S], U8, 14 * KB)
         nc.vector.tensor_copy(v_s[:], tab_s[:].indirect(offs_sb[:]))
+        acc0 = {(t, s): bank(2 * t + s) for t in range(PACK) for s in range(2)}
+        g0_at = {(1, 0): 28 * KB}
+        g0 = {(a, u): tile_at("g0_%d%d" % (a, u), [2 * PASS], BF16, g0_at.get((a, u))) for a in range(KA) for u in range(2)}
+        for a in range(KA - 1):
+            for u in range(2):
+                round_w1(g0[a, u], a, 0, u, scalar_identity if (a, u) == (0, 0) else nc.scalar.copy)
+                quant_w1(g0[a, u], a, 0, u)
+            for t in range(PACK):
+                h_passes(acc0, 0, t, (a,), first=(a == 0), last=False)
+        gather_tab(2)
         for u in range(2):
-            round_w1(g0[1, u], 1, 0, u, nc.scalar.copy)
-        quant_w1(g0[1, 0], 1, 0, 0)
-        round_w1(g0[2, 0], 2, 0, 0, nc.vector.tensor_copy)
-        quant_w1(g0[1, 1], 1, 0, 1)
-        quant_w1(g0[2, 0], 2, 0, 0)
-        round_w1(g0[2, 1], 2, 0, 1, nc.scalar.copy)
-        h_passes(acc0, 0, 0, (0, 1, 2), first=True)
-        h_passes(acc0, 0, 1, (2, 1, 0), first=True)
-        quant_w1(g0[2, 1], 2, 0, 1)
-        h_passes(acc0, 0, 2, (2, 1, 0), first=True)
-        h_passes(acc0, 0, 3, (2, 1, 0), first=True)
-        evict_h(acc0, 0, 0, 0)
-        evict_h(acc0, 0, 0, 1, on_vector=True)
+            round_w1(g0[2, u], 2, 0, u, nc.scalar.copy)
+            quant_w1(g0[2, u], 2, 0, u)
+        for t in range(PACK):
+            h_passes(acc0, 0, t, (2,))
+        evict_slice(acc0, 0, 0)
+
+        def prepare_w1(a, u, offset):
+            g = stage("g%d1%d" % (a, u), offset)
+            round_w1(g, a, 1, u, nc.scalar.copy)
+            quant_w1(g, a, 1, u)
+
+        def prepare_w2(b, n, offset):
+            g = stage("gw2%d%d" % (b, n), offset)
+            interleave(g, w2_raw[b][:, :, n * HALF : (n + 1) * HALF], nc.scalar.copy)
+            quant_w2(g, b, n * HALF, (n + 1) * HALF)
+
+        def round_z(b, j0, j1, engine_copy):
+            g = own("gz%d_%d" % (b, j0), [PACK * (j1 - j0)], BF16)
+            r0 = j0 // HALF * HALF
+            interleave(g, z_f[b, r0][:, :, j0 - r0 : j1 - r0], engine_copy)
+            return g
 
         acc1 = {}
         slice_pairs(0, 0)
         evict_slice(acc0, 0, 1)
-        g010 = stage("g010", 2 * KB)
-        round_w1(g010, 0, 1, 0, nc.scalar.copy)
-        quant_w1(g010, 0, 1, 0)
+        slice_pairs(0, 1)
+        prepare_w1(0, 0, 0)
+        prepare_w1(1, 0, 2 * KB)
         for t in range(2):
             for s in range(2):
                 acc1[t, s] = bank(2 * t + s)
             h_passes(acc1, 1, t, (0,), first=True, last=False)
-        slice_pairs(0, 1, 512)
-        g110 = stage("g110", 10 * KB + 512)
-        round_w1(g110, 1, 1, 0, nc.scalar.copy)
-        quant_w1(g110, 1, 1, 0)
         evict_slice(acc0, 0, 2)
-        slice_pairs(0, 2, 9 * KB)
-        g210 = stage("g210", 17 * KB + 512)
-        round_w1(g210, 2, 1, 0, nc.scalar.copy)
-        quant_w1(g210, 2, 1, 0)
+        slice_pairs(0, 2)
+        prepare_w1(2, 0, 4 * KB)
         h_passes(acc1, 1, 0, (1, 2))
         h_passes(acc1, 1, 1, (2, 1))
         evict_slice(acc0, 0, 3)
-        slice_pairs(0, 3, 16 * KB)
-        g011 = stage("g011", KB)
-        round_w1(g011, 0, 1, 1, nc.scalar.copy)
-        quant_w1(g011, 0, 1, 1)
-        g111 = stage("g111", 19 * KB)
-        round_w1(g111, 1, 1, 1, nc.scalar.copy)
-        quant_w1(g111, 1, 1, 1)
+        slice_pairs(0, 3, 4 * KB)
+        prepare_w1(0, 1, 6 * KB)
+        prepare_w1(1, 1, 8 * KB)
+        evict_slice(acc1, 1, 0)
+        prepare_w1(2, 1, 10 * KB)
         for t in range(2, PACK):
             for s in range(2):
                 acc1[t, s] = bank(2 * t + s)
-            h_passes(acc1, 1, t, (0, 1), first=True, last=False)
+            h_passes(acc1, 1, t, (0, 1, 2), first=True)
 
-        evict_slice(acc1, 1, 0)
         slice_pairs(1, 0)
         evict_slice(acc1, 1, 1)
-        g211 = stage("g211", 21 * KB)
-        round_w1(g211, 2, 1, 1, nc.scalar.copy)
-        quant_w1(g211, 2, 1, 1)
-        for t in range(2, PACK):
-            h_passes(acc1, 1, t, (2,))
-        gz0a = own("gz0a", [2 * PASS], BF16)
-        interleave(gz0a, z_f[0][:, :, :HALF], nc.scalar.copy)
-        slice_pairs(1, 1, 22 * KB + 512)
-        quant_z(gz0a, 0, 0, HALF)
+        slice_pairs(1, 1)
+        quant_z(round_z(0, 0, HALF, nc.scalar.copy), 0, 0, HALF)
         evict_slice(acc1, 1, 2)
+        prepare_w2(0, 0, 12 * KB)
         evict_slice(acc1, 1, 3)
-        pair(1, [(2, 0, HALF), (3, 0, HALF)], own("child_a", [2, HALF], F32))
-        gw2 = {(0, 0): stage("gw200", 31 * KB), (0, 1): stage("gw201", 33 * KB), (1, 0): stage("gw210", 36 * KB), (1, 1): stage("gw211", 38 * KB)}
-
-        def round_w2(b, n, engine_copy):
-            interleave(gw2[b, n], w2_raw[b][:, :, n * HALF : (n + 1) * HALF], engine_copy)
-            quant_w2(gw2[b, n], b, n * HALF, (n + 1) * HALF)
-
-        round_w2(0, 0, nc.scalar.copy)
-        round_w2(0, 1, nc.scalar.copy)
+        pair(1, [(2, 0, HALF), (3, 0, HALF)], own("child_a", [J], F32))
+        prepare_w2(0, 1, 16 * KB)
         y_a = [bank(c) for c in range(NC)]
-        run_passes(y_a, 0, 0, HALF)
-        cut = HALF + P
-        pair(1, [(2, HALF, cut), (3, HALF, cut)], placed("child_b", [2, P], F32, 31 * KB))
-        round_w2(1, 0, nc.scalar.copy)
-        round_w2(1, 1, nc.scalar.copy)
-        pair(1, [(2, cut, J), (3, cut, J)], placed("child_c", [2, P], F32, 36 * KB))
-        gz1a = stage("gz1a", 40 * KB)
-        interleave(gz1a, z_f[1][:, :, :HALF], nc.scalar.copy)
-        quant_z(gz1a, 1, 0, HALF)
-        run_passes(y_a, 1, 0, HALF)
-        gz0b = stage("gz0b", 42 * KB)
-        interleave(gz0b, z_f[0][:, :, HALF:], nc.vector.tensor_copy)
-        gz1b = stage("gz1b", 44 * KB, PASS)
-        interleave(gz1b, z_f[1][:, :, HALF:cut], nc.scalar.copy)
-        quant_z(gz0b, 0, HALF, J)
-        y_b = [bank(4), bank(5)]
-        y_c = [bank(6), bank(7)]
-        run_passes(y_b, 0, HALF, cut)
-        run_passes(y_c, 0, cut, J)
-        quant_z(gz1b, 1, HALF, cut)
-        run_passes(y_b, 1, HALF, cut)
-        gz1c = stage("gz1c", 45 * KB, PASS)
-        interleave(gz1c, z_f[1][:, :, cut:], nc.vector.tensor_copy)
-        quant_z(gz1c, 1, cut, J)
-        run_passes(y_c, 1, cut, J)
-        finish_run(y_a, 0, HALF, 2)
-        finish_run(y_b, HALF, cut, 1)
-        finish_run(y_c, cut, J, 2)
+        y_passes(y_a, 0, 0, 0, HALF)
+        prepare_w2(1, 0, 18 * KB)
+        pair(1, [(2, HALF, cut), (3, HALF, cut)], keep.tile([P, HALF], F32, name="child_b", tag="w2_raw0", align_bytes=64))
+        prepare_w2(1, 1, 20 * KB)
+        quant_z(round_z(1, 0, HALF, nc.scalar.copy), 1, 0, HALF)
+        y_passes(y_a, 0, 1, 0, HALF)
+        pair(1, [(2, cut, J), (3, cut, J)], keep.tile([P, HALF], F32, name="child_c", tag="z_f1_0", align_bytes=64))
+        quant_z(round_z(0, HALF, J, nc.scalar.copy), 0, HALF, J)
+        y_b = [bank(NC + c) for c in range(NC)]
+        y_passes(y_b, 1, 0, HALF, J)
+        quant_z(round_z(1, HALF, cut, nc.scalar.copy), 1, HALF, cut)
+        quant_z(round_z(1, cut, J, nc.scalar.copy), 1, cut, J)
+        y_passes(y_b, 1, 1, HALF, J)
+        finish_y(y_a, 0)
+        finish_y(y_b, 1)

@@ -80,8 +80,8 @@ def tile_list_limb_pair_scores_kernel(
             )
         load_tab(1)
         load_w1(0, 0)
-        load_w1(1, 0)
         load_tab(2)
+        load_w1(1, 0)
         load_w1(2, 0)
         nc.sync.dma_start(pos2_sb[:], pos2)
         nc.sync.dma_start(pos1_sb[:], pos1)
@@ -100,12 +100,20 @@ def tile_list_limb_pair_scores_kernel(
         with nc.allow_non_contiguous_dma(reason="one bias value a partition"):
             nc.sync.dma_start(out=b3_sb[:], in_=b3.rearrange("(c p) -> p c", p=P))
 
-        pieces = [(a, b, u) for b in range(HB) for a in range(KA) for u in range(2)]
         v_w = [own("v_w0", [S], U32), own("v_w1", [S], U32), placed("v_w2", [S], U32, 29 * KB)]
-        w1_w_at = {(2, 0, 0): KB + 512, (2, 0, 1): 5 * KB + 512, (2, 1, 0): 12 * KB, (2, 1, 1): 17 * KB + 512}
-        w1_s_at = {(0, 0, 0): 24 * KB, (2, 0, 1): 10 * KB - 128, (2, 1, 1): 20 * KB}
-        w1_w = {k: tile_at("w1_w%d%d%d" % k, [2 * P], U32, w1_w_at.get(k)) for k in pieces}
-        w1_s = {k: tile_at("w1_s%d%d%d" % k, [2 * P], U8, w1_s_at.get(k)) for k in pieces}
+        groups = {
+            0: [[(0, 0), (0, 1)], [(1, 0)], [(1, 1)], [(2, 0)], [(2, 1)]],
+            1: [[(0, 0)], [(1, 0), (2, 0)], [(0, 1), (1, 1)], [(2, 1)]],
+        }
+        w1_w_at = {(0, 3): KB + 512, (0, 4): 9 * KB + 512, (1, 1): 33 * KB, (1, 3): 17 * KB + 512}
+        w1_s_at = {(0, 0): 24 * KB}
+        w1_w, w1_s, w1_home = {}, {}, {}
+        for b in range(HB):
+            for n, group in enumerate(groups[b]):
+                w1_w[b, n] = tile_at("w1_w%d%d" % (b, n), [2 * P * len(group)], U32, w1_w_at.get((b, n)))
+                w1_s[b, n] = tile_at("w1_s%d%d" % (b, n), [2 * P * len(group)], U8, w1_s_at.get((b, n)))
+                for m, (a, u) in enumerate(group):
+                    w1_home[a, b, u] = (n, 2 * P * m)
         w2_w = [own("w2_w%d" % b, [N], U32) for b in range(HB)]
         w2_s = [own("w2_s%d" % b, [N], U8) for b in range(HB)]
         h = {(b, t): own("h%d%d" % (b, t), [S], F32) for b in range(HB) for t in range(PACK)}
@@ -126,27 +134,29 @@ def tile_list_limb_pair_scores_kernel(
         def quant(words, scales, src):
             nc.vector.quantize_mx(out=words.bitcast(FP8X4), scales=scales, in_=src)
 
-        def round_w1(g, a, b, u, engine_copy, m0=0, m1=P):
-            dst = g[:].rearrange("p (t m i) -> p m i t", t=2, i=PACK)
+        def round_w1(g, a, b, u, engine_copy=nc.scalar.copy, m0=0, m1=P):
+            col = PACK * w1_home[a, b, u][1]
+            dst = g[:, col : col + 2 * PASS].rearrange("p (t m i) -> p m i t", t=2, i=PACK)
             src = w1_raw[a, b][:].rearrange("p i (m u t) -> p u m i t", u=2, t=2)
             engine_copy(out=dst[:, m0:m1], in_=src[:, u, m0:m1])
 
-        def quant_w1(g, a, b, u):
-            quant(w1_w[a, b, u][:], w1_s[a, b, u][:], g[:])
+        def quant_w1(g, b, n):
+            quant(w1_w[b, n][:], w1_s[b, n][:], g)
 
         def interleave(g, src, engine_copy):
             engine_copy(
-                out=g[:].rearrange("p (c u t) -> p c t u", u=4, t=PACK),
+                out=g.rearrange("p (c u t) -> p c t u", u=4, t=PACK),
                 in_=src.rearrange("p t (c u) -> p c t u", u=4),
             )
 
         def h_pass(acc, a, b, t, s, start, stop):
-            cols = slice((t % 2) * P, (t % 2 + 1) * P)
+            n, col = w1_home[a, b, t // 2]
+            cols = slice(col + (t % 2) * P, col + (t % 2 + 1) * P)
             ent = slice(s * BANK, (s + 1) * BANK)
             nc.tensor.matmul_mx(
                 out=acc[:],
-                lhsT=w1_w[a, b, t // 2][:, cols].bitcast(FP8X4),
-                lhsT_scale=w1_s[a, b, t // 2][:, cols],
+                lhsT=w1_w[b, n][:, cols].bitcast(FP8X4),
+                lhsT_scale=w1_s[b, n][:, cols],
                 rhs=v_w[a][:, ent].bitcast(FP8X4),
                 rhs_scale=v_s[4 * a :, ent],
                 start=start,
@@ -187,11 +197,8 @@ def tile_list_limb_pair_scores_kernel(
         def scalar_identity(out, in_):
             nc.scalar.activation(out=out, in_=in_, func=ACT.Identity)
 
-        def quant_w2(g, b, n0, n1):
-            quant(w2_w[b][:, n0:n1], w2_s[b][:, n0:n1], g[:])
-
         def quant_z(g, b, j0, j1):
-            quant(z_w[b][:, j0:j1], z_s[b][:, j0:j1], g[:])
+            quant(z_w[b][:, j0:j1], z_s[b][:, j0:j1], g)
 
         def y_passes(y, u, b, j0, j1):
             for c in range(NC):
@@ -226,66 +233,80 @@ def tile_list_limb_pair_scores_kernel(
                 nc.sync.dma_start(out=out[c * P : (c + 1) * P, u * HALF : (u + 1) * HALF], in_=res[:])
 
         def stage(name, offset, width=2 * PASS):
-            return placed(name, [width], BF16, offset)
+            return tile_at(name, [width], BF16, offset)[:]
+
+        def w1_stage(b, n, offset=None):
+            return stage("g%d%d" % (b, n), offset, 2 * PASS * len(groups[b][n]))
+
+        def round_w2(g, b, n):
+            interleave(g[:, n * 2 * PASS : (n + 1) * 2 * PASS], w2_raw[b][:, :, n * HALF : (n + 1) * HALF], nc.scalar.copy)
+
+        def round_z(g, b, j0, j1, engine_copy=nc.scalar.copy):
+            r0 = j0 // HALF * HALF
+            interleave(g[:, PACK * (j0 - r0) : PACK * (j1 - r0)], z_f[b, r0][:, :, j0 - r0 : j1 - r0], engine_copy)
+
+        def finish_z(b, j0):
+            g = stage("gz%d_%d" % (b, j0), None)
+            round_z(g, b, j0, j0 + HALF)
+            quant_z(g, b, j0, j0 + HALF)
 
         gather_tab(0)
         gather_tab(1)
         v_s = placed("v_s", [S], U8, 14 * KB)
         nc.vector.tensor_copy(v_s[:], tab_s[:].indirect(offs_sb[:]))
         acc0 = {(t, s): bank(2 * t + s) for t in range(PACK) for s in range(2)}
-        g0_at = {(1, 0): 28 * KB}
-        g0 = {(a, u): tile_at("g0_%d%d" % (a, u), [2 * PASS], BF16, g0_at.get((a, u))) for a in range(KA) for u in range(2)}
-        for a in range(KA - 1):
-            for u in range(2):
-                round_w1(g0[a, u], a, 0, u, scalar_identity if (a, u) == (0, 0) else nc.scalar.copy)
-                quant_w1(g0[a, u], a, 0, u)
-            for t in range(PACK):
-                h_passes(acc0, 0, t, (a,), first=(a == 0), last=False)
-        gather_tab(2)
-        for u in range(2):
-            round_w1(g0[2, u], 2, 0, u, nc.scalar.copy)
-            quant_w1(g0[2, u], 2, 0, u)
+        g0 = [w1_stage(0, n, 26 * KB if n == 0 else None) for n in range(5)]
+        round_w1(g0[0], 0, 0, 0, scalar_identity)
+        round_w1(g0[0], 0, 0, 1)
+        quant_w1(g0[0], 0, 0)
         for t in range(PACK):
-            h_passes(acc0, 0, t, (2,))
-        evict_slice(acc0, 0, 0)
-
-        def prepare_w1(a, u, offset):
-            g = stage("g%d1%d" % (a, u), offset)
-            round_w1(g, a, 1, u, nc.scalar.copy)
-            quant_w1(g, a, 1, u)
-
-        def prepare_w2(b, n, offset):
-            g = stage("gw2%d%d" % (b, n), offset)
-            interleave(g, w2_raw[b][:, :, n * HALF : (n + 1) * HALF], nc.scalar.copy)
-            quant_w2(g, b, n * HALF, (n + 1) * HALF)
-
-        def round_z(b, j0, j1, engine_copy):
-            g = own("gz%d_%d" % (b, j0), [PACK * (j1 - j0)], BF16)
-            r0 = j0 // HALF * HALF
-            interleave(g, z_f[b, r0][:, :, j0 - r0 : j1 - r0], engine_copy)
-            return g
+            h_passes(acc0, 0, t, (0,), first=True, last=False)
+        gather_tab(2)
+        round_w1(g0[1], 1, 0, 0)
+        round_w1(g0[2], 1, 0, 1)
+        quant_w1(g0[1], 0, 1)
+        round_w1(g0[3], 2, 0, 0, nc.scalar.copy, 0, 40)
+        round_w1(g0[3], 2, 0, 0, nc.vector.tensor_copy, 40, P)
+        quant_w1(g0[2], 0, 2)
+        quant_w1(g0[3], 0, 3)
+        round_w1(g0[4], 2, 0, 1)
+        h_passes(acc0, 0, 0, (1, 2))
+        h_passes(acc0, 0, 1, (2, 1))
+        evict_h(acc0, 0, 0, 0)
+        evict_h(acc0, 0, 0, 1, on_vector=True)
+        quant_w1(g0[4], 0, 4)
+        h_passes(acc0, 0, 2, (2, 1))
+        h_passes(acc0, 0, 3, (2, 1))
 
         acc1 = {}
         slice_pairs(0, 0)
         evict_slice(acc0, 0, 1)
         slice_pairs(0, 1)
-        prepare_w1(0, 0, 0)
-        prepare_w1(1, 0, 2 * KB)
+        g10 = w1_stage(1, 0, 0)
+        round_w1(g10, 0, 1, 0)
+        quant_w1(g10, 1, 0)
         for t in range(2):
             for s in range(2):
                 acc1[t, s] = bank(2 * t + s)
             h_passes(acc1, 1, t, (0,), first=True, last=False)
+        g11 = w1_stage(1, 1, 2 * KB)
+        round_w1(g11, 1, 1, 0)
         evict_slice(acc0, 0, 2)
         slice_pairs(0, 2)
-        prepare_w1(2, 0, 4 * KB)
-        h_passes(acc1, 1, 0, (1, 2))
-        h_passes(acc1, 1, 1, (2, 1))
+        round_w1(g11, 2, 1, 0)
+        quant_w1(g11, 1, 1)
+        for t in range(2):
+            h_passes(acc1, 1, t, (1, 2))
         evict_slice(acc0, 0, 3)
         slice_pairs(0, 3, 4 * KB)
-        prepare_w1(0, 1, 6 * KB)
-        prepare_w1(1, 1, 8 * KB)
+        g12 = w1_stage(1, 2, 6 * KB)
+        round_w1(g12, 0, 1, 1)
+        round_w1(g12, 1, 1, 1)
+        quant_w1(g12, 1, 2)
         evict_slice(acc1, 1, 0)
-        prepare_w1(2, 1, 10 * KB)
+        g13 = w1_stage(1, 3, 10 * KB)
+        round_w1(g13, 2, 1, 1)
+        quant_w1(g13, 1, 3)
         for t in range(2, PACK):
             for s in range(2):
                 acc1[t, s] = bank(2 * t + s)
@@ -294,25 +315,31 @@ def tile_list_limb_pair_scores_kernel(
         slice_pairs(1, 0)
         evict_slice(acc1, 1, 1)
         slice_pairs(1, 1)
-        quant_z(round_z(0, 0, HALF, nc.scalar.copy), 0, 0, HALF)
+        finish_z(0, 0)
         evict_slice(acc1, 1, 2)
-        prepare_w2(0, 0, 12 * KB)
+        gw20 = stage("gw20", 33 * KB, 4 * PASS)
+        round_w2(gw20, 0, 0)
         evict_slice(acc1, 1, 3)
         pair(1, [(2, 0, HALF), (3, 0, HALF)], own("child_a", [J], F32))
-        prepare_w2(0, 1, 16 * KB)
+        round_w2(gw20, 0, 1)
+        quant(w2_w[0][:], w2_s[0][:], gw20)
         y_a = [bank(c) for c in range(NC)]
         y_passes(y_a, 0, 0, 0, HALF)
-        prepare_w2(1, 0, 18 * KB)
         pair(1, [(2, HALF, cut), (3, HALF, cut)], keep.tile([P, HALF], F32, name="child_b", tag="w2_raw0", align_bytes=64))
-        prepare_w2(1, 1, 20 * KB)
-        quant_z(round_z(1, 0, HALF, nc.scalar.copy), 1, 0, HALF)
+        gw21 = stage("gw21", 16 * KB, 4 * PASS)
+        round_w2(gw21, 1, 0)
+        round_w2(gw21, 1, 1)
+        quant(w2_w[1][:], w2_s[1][:], gw21)
+        finish_z(1, 0)
         y_passes(y_a, 0, 1, 0, HALF)
         pair(1, [(2, cut, J), (3, cut, J)], keep.tile([P, HALF], F32, name="child_c", tag="z_f1_0", align_bytes=64))
-        quant_z(round_z(0, HALF, J, nc.scalar.copy), 0, HALF, J)
+        finish_z(0, HALF)
         y_b = [bank(NC + c) for c in range(NC)]
         y_passes(y_b, 1, 0, HALF, J)
-        quant_z(round_z(1, HALF, cut, nc.scalar.copy), 1, HALF, cut)
-        quant_z(round_z(1, cut, J, nc.scalar.copy), 1, cut, J)
+        gz = stage("gz_last", None)
+        round_z(gz, 1, HALF, cut)
+        round_z(gz, 1, cut, J, nc.vector.tensor_copy)
+        quant_z(gz, 1, HALF, J)
         y_passes(y_b, 1, 1, HALF, J)
         finish_y(y_a, 0)
         finish_y(y_b, 1)

@@ -15,6 +15,7 @@ FP8X4 = mybir.dt.float8_e4m3fn_x4
 FP4X4 = mybir.dt.float4_e2m1fn_x4
 ALU = mybir.AluOpType
 ACT = mybir.ActivationFunctionType
+SIZE = {F32: 4, BF16: 2, I32: 4, U32: 4, U8: 1}
 
 P = 128
 PACK = 4
@@ -24,7 +25,7 @@ HB = H // PASS
 NC = N // P
 BANK = 512
 HALF = J // 2
-KB = 1024
+RUNS = [(0, 256), (256, 512)]
 
 
 def tile_list_limb_pair_scores_kernel(
@@ -35,58 +36,83 @@ def tile_list_limb_pair_scores_kernel(
         keep = ctx.enter_context(tc.tile_pool(name="keep", bufs=1))
         arena = ctx.enter_context(tc.tile_pool(name="arena", bufs=1))
         psum = ctx.enter_context(tc.psum_pool(name="psum", bufs=1))
+        place = {"end": 0}
 
         def bank(i):
             return psum.tile([P, BANK], F32, name="bank%d" % i)
 
-        def own(name, shape, dtype):
-            return keep.tile([P] + shape, dtype, name=name, align_bytes=64)
+        def region(name, size):
+            place[name] = place["end"]
+            place["end"] = place["end"] + size
 
-        def placed(name, shape, dtype, offset):
-            return arena.tile([P] + shape, dtype, name=name, offset=offset, align_bytes=64)
-
-        def tile_at(name, shape, dtype, offset):
-            return own(name, shape, dtype) if offset is None else placed(name, shape, dtype, offset)
+        def tile(name, shape, dtype, over=None, at=0):
+            size = SIZE[dtype]
+            for d in shape:
+                size = size * d
+            if over is None:
+                place[name] = place["end"]
+                place["end"] = place["end"] + (size + 63) // 64 * 64
+            else:
+                place[name] = place[over] + at
+            return arena.tile([P] + shape, dtype, name=name, offset=place[name], align_bytes=64)
 
         offs_sb = keep.tile([P, S // 16], U16, name="offs_sb")
         pos1_sb = keep.tile([P, J // 16], U16, name="pos1_sb")
         pos2_sb = keep.tile([P, J // 16], U16, name="pos2_sb")
-        tab_w = [placed("tab_w%d" % a, [T], I32, 8 * KB * a) for a in range(KA)]
-        tab_s = placed("tab_s", [T], U8, 24 * KB)
-        w4_w = own("w4_w", [HB, 2 * N], U8)
-        w4_s = own("w4_s", [HB, N], U8)
-        b1_sb = own("b1_sb", [HB, PACK], F32)
-        b3_sb = own("b3_sb", [NC], F32)
-        w1_raw = {(a, b): own("w1_raw%d%d" % (a, b), [PACK, PASS], F32) for b in range(HB) for a in range(KA)}
-        w2_raw = [own("w2_raw%d" % b, [PACK, N], F32) for b in range(HB)]
+        tab_w = [tile("tab_w%d" % a, [T], I32) for a in range(KA)]
+        tab_s = tile("tab_s", [T], U8)
+        w4_w = tile("w4_w", [HB, 2 * N], U8)
+        w4_s = tile("w4_s", [HB, N], U8)
+        for c in range(PACK):
+            region("bias%d" % c, 2048)
+        b1_a = [tile("b1_a%d" % c, [1], F32, over="bias%d" % c) for c in range(PACK)]
+        b1_b = tile("b1_b", [PACK], F32)
+        b3_sb = tile("b3_sb", [NC], F32)
+        raw_s = {(n, a): tile("raw_s%d%d" % (n, a), [PACK, P], F32) for n in range(2) for a in range(KA)}
+        region("pad", 2048)
+        raw_a = [tile("raw_a%d" % a, [PACK, 2 * P], F32) for a in range(KA)]
+        raw_b = [tile("raw_b%d" % a, [PACK, PASS], F32) for a in range(KA)]
+        w2_raw = [tile("w2_raw%d" % b, [PACK, N], F32) for b in range(HB)]
 
-        nc.gpsimd.memset(tab_s[:].bitcast(I32), 0)
-        nc.gpsimd.memset(w4_s[:].rearrange("p b n -> p (b n)").bitcast(I32), 0)
+        nc.vector.memset(tab_s[:].bitcast(I32), 0)
+        nc.vector.memset(w4_s[:].rearrange("p b n -> p (b n)").bitcast(I32), 0)
 
         def load_tab(a):
             nc.sync.dma_start(out=tab_w[a][:], in_=tab_words[a].rearrange("p t i -> p (t i)").bitcast(I32))
 
-        def load_w1(a, b):
-            rows = w1[a * PASS : (a + 1) * PASS, b * PASS : (b + 1) * PASS]
-            nc.sync.dma_start(out=w1_raw[a, b][:], in_=rows.rearrange("(p i) c -> p i c", i=PACK))
+        def load_w1(dst, a, c0, c1):
+            rows = w1[a * PASS : (a + 1) * PASS, c0:c1]
+            nc.sync.dma_start(out=dst[:], in_=rows.rearrange("(p i) c -> p i c", i=PACK))
+
+        def load_b1(c):
+            with nc.allow_non_contiguous_dma(reason="one bias value a partition"):
+                nc.sync.dma_start(out=b1_a[c][:], in_=b1[c * P : (c + 1) * P].rearrange("(p o) -> p o", o=1))
 
         load_tab(0)
         nc.sync.dma_start(offs_sb[:], offs)
-        nc.scalar.dma_start(out=b1_sb[:], in_=b1.rearrange("(b p t) -> p b t", b=HB, t=PACK))
+        nc.sync.dma_start(pos2_sb[:], pos2)
         for q in range(4):
             nc.scalar.dma_start(
                 out=tab_s[32 * q : 32 * q + 4 * KA, :].bitcast(I32),
                 in_=tab_scales[:, 4 * q : 4 * q + 4, :].bitcast(I32),
             )
         load_tab(1)
-        load_w1(0, 0)
+        for a in range(KA):
+            load_w1(raw_s[0, a], a, 0, P)
         load_tab(2)
-        load_w1(1, 0)
-        load_w1(2, 0)
-        nc.sync.dma_start(pos2_sb[:], pos2)
+        for a in range(KA):
+            load_w1(raw_s[1, a], a, P, 2 * P)
+        load_b1(0)
         nc.sync.dma_start(pos1_sb[:], pos1)
         for a in range(KA):
-            load_w1(a, 1)
+            load_w1(raw_a[a], a, 2 * P, PASS)
+        load_b1(1)
+        load_w1(raw_b[0], 0, PASS, H)
+        load_b1(2)
+        load_w1(raw_b[1], 1, PASS, H)
+        load_b1(3)
+        load_w1(raw_b[2], 2, PASS, H)
+        nc.sync.dma_start(out=b1_b[:], in_=b1[PASS:].rearrange("(p t) -> p t", t=PACK))
         for b in range(HB):
             nc.sync.dma_start(
                 out=w2_raw[b][:], in_=w2[b * PASS : (b + 1) * PASS, :].rearrange("(p i) n -> p i n", i=PACK)
@@ -100,246 +126,261 @@ def tile_list_limb_pair_scores_kernel(
         with nc.allow_non_contiguous_dma(reason="one bias value a partition"):
             nc.sync.dma_start(out=b3_sb[:], in_=b3.rearrange("(c p) -> p c", p=P))
 
-        v_w = [own("v_w0", [S], U32), own("v_w1", [S], U32), placed("v_w2", [S], U32, 29 * KB)]
-        groups = {
-            0: [[(0, 0), (0, 1)], [(1, 0)], [(1, 1)], [(2, 0)], [(2, 1)]],
-            1: [[(0, 0)], [(1, 0), (2, 0)], [(0, 1), (1, 1)], [(2, 1)]],
-        }
-        w1_w_at = {(0, 3): KB + 512, (0, 4): 9 * KB + 512, (1, 1): 33 * KB, (1, 3): 17 * KB + 512}
-        w1_s_at = {(0, 0): 24 * KB}
-        w1_w, w1_s, w1_home = {}, {}, {}
-        for b in range(HB):
-            for n, group in enumerate(groups[b]):
-                w1_w[b, n] = tile_at("w1_w%d%d" % (b, n), [2 * P * len(group)], U32, w1_w_at.get((b, n)))
-                w1_s[b, n] = tile_at("w1_s%d%d" % (b, n), [2 * P * len(group)], U8, w1_s_at.get((b, n)))
-                for m, (a, u) in enumerate(group):
-                    w1_home[a, b, u] = (n, 2 * P * m)
-        w2_w = [own("w2_w%d" % b, [N], U32) for b in range(HB)]
-        w2_s = [own("w2_s%d" % b, [N], U8) for b in range(HB)]
-        h = {(b, t): own("h%d%d" % (b, t), [S], F32) for b in range(HB) for t in range(PACK)}
-        cut = HALF + P
-        runs = {0: [(0, HALF), (HALF, J)], 1: [(0, HALF), (HALF, J)]}
-        z_f = {(b, j0): own("z_f%d_%d" % (b, j0), [PACK, j1 - j0], F32) for b in range(HB) for j0, j1 in runs[b]}
+        v_w = [tile("v_w%d" % a, [S], U32, over=(None, "raw_s01", None)[a]) for a in range(KA)]
+        v_s = tile("v_s", [S], U8)
+        batches = [
+            [(0, 0), (0, 1)], [(0, 2)], [(1, 0), (1, 1)], [(1, 2)],
+            [(2, 0), (3, 0), (2, 1), (3, 1)], [(2, 2), (3, 2)],
+            [(4, 0), (5, 0)], [(4, 2), (5, 2)],
+            [(6, 2), (7, 2)], [(6, 1), (7, 1), (6, 0), (7, 0)], [(4, 1), (5, 1)],
+        ]
+        for name in ("w2_late", "r9", "z_first", "w2_first"):
+            region(name, 4096)
+        g_over = {9: "r9"}
+        w_over = {2: "tab_w2", 4: "bias0", 6: "bias2", 7: "r9", 9: "z_first"}
+        s_over = {7: "w2_first", 9: "w2_late"}
+        w1_g = [tile("w1_g%d" % k, [PASS * len(b)], BF16, over=g_over.get(k), at=(2048 if k == 10 else 0)) for k, b in enumerate(batches)]
+        w1_w = [tile("w1_w%d" % k, [P * len(b)], U32, over=w_over.get(k)) for k, b in enumerate(batches)]
+        w1_s = [tile("w1_s%d" % k, [P * len(b)], U8, over=s_over.get(k), at=2048) for k, b in enumerate(batches)]
+        home = {piece: (k, m) for k, b in enumerate(batches) for m, piece in enumerate(b)}
+        w2_w = [tile("w2_w%d" % b, [N], U32) for b in range(HB)]
+        w2_s = [tile("w2_s%d" % b, [N], U8) for b in range(HB)]
+        h = [tile("h%d" % n, [S], F32, over={0: "raw_s12", 1: "raw_a2"}.get(n)) for n in range(8)]
+        z_rows = [tile("z_rows%d" % c, [J], F32, over=("raw_a1", None, None, "w2_late")[c]) for c in range(PACK)]
+        z_a = tile("z_a", [PACK, J], F32)
+        z_b = [tile("z_b%d" % r, [PACK, j1 - j0], F32) for r, (j0, j1) in enumerate(RUNS)]
+        z_w = [tile("z_w%d" % b, [J], U32) for b in range(HB)]
+        z_s = [tile("z_s%d" % b, [J], U8) for b in range(HB)]
+        acc = {}
 
-        def z_part(b, t, j0, j1):
-            r0 = max(x for x, y in runs[b] if x <= j0)
-            return z_f[b, r0][:, t, j0 - r0 : j1 - r0]
-
-        z_w = [own("z_w%d" % b, [J], U32) for b in range(HB)]
-        z_s = [own("z_s%d" % b, [J], U8) for b in range(HB)]
-
-        def gather_tab(a):
-            nc.vector.tensor_copy(v_w[a][:], tab_w[a][:].bitcast(U32).indirect(offs_sb[:]))
+        def gather_tab(a, e0=0, e1=S):
+            nc.vector.tensor_copy(v_w[a][:, e0:e1], tab_w[a][:].bitcast(U32).indirect(offs_sb[:, e0 // 16 : e1 // 16]))
 
         def quant(words, scales, src):
             nc.vector.quantize_mx(out=words.bitcast(FP8X4), scales=scales, in_=src)
 
-        def round_w1(g, a, b, u, engine_copy=nc.scalar.copy, m0=0, m1=P):
-            col = PACK * w1_home[a, b, u][1]
-            dst = g[:, col : col + 2 * PASS].rearrange("p (t m i) -> p m i t", t=2, i=PACK)
-            src = w1_raw[a, b][:].rearrange("p i (m u t) -> p u m i t", u=2, t=2)
-            engine_copy(out=dst[:, m0:m1], in_=src[:, u, m0:m1])
-
-        def quant_w1(g, b, n):
-            quant(w1_w[b, n][:], w1_s[b, n][:], g)
-
-        def interleave(g, src, engine_copy):
-            engine_copy(
-                out=g.rearrange("p (c u t) -> p c t u", u=4, t=PACK),
-                in_=src.rearrange("p t (c u) -> p c t u", u=4),
-            )
-
-        def h_pass(acc, a, b, t, s, start, stop):
-            n, col = w1_home[a, b, t // 2]
-            cols = slice(col + (t % 2) * P, col + (t % 2 + 1) * P)
-            ent = slice(s * BANK, (s + 1) * BANK)
-            nc.tensor.matmul_mx(
-                out=acc[:],
-                lhsT=w1_w[b, n][:, cols].bitcast(FP8X4),
-                lhsT_scale=w1_s[b, n][:, cols],
-                rhs=v_w[a][:, ent].bitcast(FP8X4),
-                rhs_scale=v_s[4 * a :, ent],
-                start=start,
-                stop=stop,
-            )
-
-        def h_passes(acc, b, t, order, first=False, last=True):
-            for a in order:
-                for s in range(2):
-                    h_pass(acc[t, s], a, b, t, s, first and a == order[0], last and a == order[-1])
-
-        def evict_h(acc, b, t, s, on_vector=False):
-            dst = h[b, t][:, s * BANK : (s + 1) * BANK]
-            if on_vector:
-                nc.vector.tensor_scalar(dst, acc[t, s][:], b1_sb[:, b, t : t + 1], 0.0, ALU.add, ALU.max)
-            else:
-                nc.scalar.activation(out=dst, in_=acc[t, s][:], func=ACT.Relu, bias=b1_sb[:, b, t : t + 1])
-
-        def evict_slice(acc, b, t):
-            for s in range(2):
-                evict_h(acc, b, t, s)
-
-        def pair(b, units, child):
-            ends = [sum(j1 - j0 for t, j0, j1 in units[:n]) for n in range(len(units) + 1)]
-            for n, (t, j0, j1) in enumerate(units):
-                nc.vector.tensor_copy(child[:, ends[n] : ends[n + 1]], h[b, t][:].indirect(pos2_sb[:, j0 // 16 : j1 // 16]))
-            for n, (t, j0, j1) in enumerate(units):
-                nc.vector.tensor_tensor(
-                    z_part(b, t, j0, j1),
-                    h[b, t][:].indirect(pos1_sb[:, j0 // 16 : j1 // 16]),
-                    child[:, ends[n] : ends[n + 1]],
-                    ALU.subtract,
-                )
-
-        def slice_pairs(b, t, offset=None):
-            pair(b, [(t, 0, HALF), (t, HALF, J)], tile_at("child%d%d" % (b, t), [J], F32, offset))
-
         def scalar_identity(out, in_):
             nc.scalar.activation(out=out, in_=in_, func=ACT.Identity)
 
-        def quant_z(g, b, j0, j1):
-            quant(z_w[b][:, j0:j1], z_s[b][:, j0:j1], g)
+        def interleave(dst, src, engine_copy=nc.scalar.copy, run=2):
+            engine_copy(
+                out=dst.rearrange("p (c u t) -> p c t u", u=run, t=PACK),
+                in_=src.rearrange("p t (c u) -> p c t u", u=run),
+            )
 
-        def y_passes(y, u, b, j0, j1):
-            for c in range(NC):
-                cols = slice(c * P, (c + 1) * P)
-                lo, hi = j0 - u * HALF, j1 - u * HALF
-                nc.tensor.matmul_mx(
-                    out=y[c][:, lo:hi],
-                    lhsT=w2_w[b][:, cols].bitcast(FP8X4),
-                    lhsT_scale=w2_s[b][:, cols],
-                    rhs=z_w[b][:, j0:j1].bitcast(FP8X4),
-                    rhs_scale=z_s[b][:, j0:j1],
-                    start=(b == 0),
-                    stop=False,
+        def round_w1(n, a, engine_copy=nc.scalar.copy, m0=0, m1=P):
+            k, m = home[n, a]
+            if n < 2:
+                interleave(w1_g[k][:, m * PASS : (m + 1) * PASS], raw_s[n, a][:], engine_copy)
+            elif n < PACK:
+                interleave(w1_g[k][:, m * PASS : (m + 2) * PASS], raw_a[a][:], engine_copy)
+            else:
+                dst = w1_g[k][:, m * PASS : (m + 2) * PASS].rearrange("p (t m i) -> p m i t", t=2, i=PACK)
+                src = raw_b[a][:].rearrange("p i (m u t) -> p u m i t", u=2, t=2)
+                engine_copy(out=dst[:, m0:m1], in_=src[:, (n - PACK) // 2, m0:m1])
+
+        def quant_w1(k):
+            quant(w1_w[k][:], w1_s[k][:], w1_g[k][:])
+
+        def h_pass(n, a, s):
+            first = (n, s) not in acc
+            if first:
+                acc[n, s] = bank(2 * (n % 4) + s)
+            k, m = home[n, a]
+            cols = slice(m * P, (m + 1) * P)
+            ent = slice(s * BANK, (s + 1) * BANK)
+            nc.tensor.matmul_mx(
+                out=acc[n, s][:],
+                lhsT=w1_w[k][:, cols].bitcast(FP8X4),
+                lhsT_scale=w1_s[k][:, cols],
+                rhs=v_w[a][:, ent].bitcast(FP8X4),
+                rhs_scale=v_s[4 * a :, ent],
+                start=first,
+                stop=(a == (1 if n in (3, 6, 7) else KA - 1)),
+            )
+
+        def h_passes(slices, order):
+            for n in slices:
+                for s in range(2):
+                    for a in order:
+                        h_pass(n, a, s)
+
+        def evict_h(n, s, on_vector=False):
+            dst = h[n][:, s * BANK : (s + 1) * BANK]
+            bias = b1_a[n][:] if n < PACK else b1_b[:, n - PACK : n - PACK + 1]
+            if on_vector:
+                nc.vector.tensor_scalar(dst, acc[n, s][:], bias, 0.0, ALU.add, ALU.max)
+            else:
+                nc.scalar.activation(out=dst, in_=acc[n, s][:], func=ACT.Relu, bias=bias)
+
+        def evict_slice(n):
+            for s in range(2):
+                evict_h(n, s)
+
+        def differences(units, child):
+            ends = [sum(j1 - j0 for n, j0, j1, dst in units[:k]) for k in range(len(units) + 1)]
+            for k, (n, j0, j1, dst) in enumerate(units):
+                nc.vector.tensor_copy(child[:, ends[k] : ends[k + 1]], h[n][:].indirect(pos2_sb[:, j0 // 16 : j1 // 16]))
+            for k, (n, j0, j1, dst) in enumerate(units):
+                nc.vector.tensor_tensor(
+                    dst, h[n][:].indirect(pos1_sb[:, j0 // 16 : j1 // 16]), child[:, ends[k] : ends[k + 1]], ALU.subtract
                 )
-                for j in range(lo, hi, P):
+
+        def slice_a(c):
+            child = tile("child%d" % c, [J], F32, over={3: "w1_g7"}.get(c))
+            differences([(c, j0, j0 + HALF, z_rows[c][:, j0 : j0 + HALF]) for j0 in (0, HALF)], child)
+
+        def slice_around_quant(c, k):
+            child = tile("child%d" % c, [J], F32, over=None)
+            nc.vector.tensor_copy(child[:], h[c][:].indirect(pos2_sb[:]))
+            quant_w1(k)
+            nc.vector.tensor_tensor(z_rows[c][:], h[c][:].indirect(pos1_sb[:]), child[:], ALU.subtract)
+
+        def deal(c):
+            nc.sync.dma_start(out=z_a[32 * c : 32 * (c + 1), :, :], in_=z_rows[c][:])
+
+        def unit_b(t, r):
+            return (PACK + t, RUNS[r][0], RUNS[r][1], z_b[r][:, t, :])
+
+        def y_passes(y, r, b):
+            j0, j1 = RUNS[r]
+            w = j1 - j0
+            per = BANK // w
+            for c0 in range(0, NC, per):
+                for c in range(c0, c0 + per):
+                    cols = slice(c * P, (c + 1) * P)
                     nc.tensor.matmul_mx(
-                        out=y[c][:, HALF + j : HALF + j + P],
-                        lhsT=w4_w[:, b, 2 * c * P : 2 * (c + 1) * P].bitcast(FP4X4),
-                        lhsT_scale=w4_s[:, b, cols],
-                        rhs=z_w[b][:, u * HALF + j : u * HALF + j + P].bitcast(FP8X4),
-                        rhs_scale=z_s[b][:, u * HALF + j : u * HALF + j + P],
-                        start=False,
-                        stop=(b == HB - 1 and j + P == HALF),
+                        out=y[0][c // per][:, (c % per) * w : (c % per + 1) * w],
+                        lhsT=w2_w[b][:, cols].bitcast(FP8X4),
+                        lhsT_scale=w2_s[b][:, cols],
+                        rhs=z_w[b][:, j0:j1].bitcast(FP8X4),
+                        rhs_scale=z_s[b][:, j0:j1],
+                        start=(b == 0 and c % per == 0),
+                        stop=(b == HB - 1 and c % per == per - 1),
                     )
+                for c in range(c0, c0 + per):
+                    cols = slice(c * P, (c + 1) * P)
+                    for j in range(0, w, P):
+                        nc.tensor.matmul_mx(
+                            out=y[1][c // per][:, (c % per) * w + j : (c % per) * w + j + P],
+                            lhsT=w4_w[:, b, 2 * c * P : 2 * (c + 1) * P].bitcast(FP4X4),
+                            lhsT_scale=w4_s[:, b, cols],
+                            rhs=z_w[b][:, j0 + j : j0 + j + P].bitcast(FP8X4),
+                            rhs_scale=z_s[b][:, j0 + j : j0 + j + P],
+                            start=(b == 0 and c % per == 0 and j == 0),
+                            stop=(b == HB - 1 and c % per == per - 1 and j + P == w),
+                        )
 
-        def finish_y(y, u):
+        def finish_y(y, r, stores):
+            j0, j1 = RUNS[r]
+            w = j1 - j0
+            per = BANK // w
+            y1b = tile("y1b%d" % r, [NC, w], F32, over="tab_w0", at=16 * j0)
+            res = tile("res%d" % r, [NC, w], F32, over="tab_w1", at=16 * j0)
             for c in range(NC):
-                y1b = own("y1b%d_%d" % (u, c), [HALF], F32)
-                nc.scalar.activation(out=y1b[:], in_=y[c][:, :HALF], func=ACT.Identity, bias=b3_sb[:, c : c + 1])
-                res = own("res%d_%d" % (u, c), [HALF], F32)
-                nc.vector.scalar_tensor_tensor(res[:], y[c][:, HALF:], b3_sb[:, c : c + 1], y1b[:], ALU.add, ALU.max)
-                nc.sync.dma_start(out=out[c * P : (c + 1) * P, u * HALF : (u + 1) * HALF], in_=res[:])
+                part = slice((c % per) * w, (c % per + 1) * w)
+                nc.scalar.activation(out=y1b[:, c, :], in_=y[0][c // per][:, part], func=ACT.Identity, bias=b3_sb[:, c : c + 1])
+            for c in range(NC):
+                part = slice((c % per) * w, (c % per + 1) * w)
+                nc.vector.scalar_tensor_tensor(
+                    res[:, c, :], y[1][c // per][:, part], b3_sb[:, c : c + 1], y1b[:, c, :], ALU.add, ALU.max
+                )
+            step = NC // stores
+            for c in range(0, NC, step):
+                nc.sync.dma_start(
+                    out=out[c * P : (c + step) * P, j0:j1].rearrange("(c p) j -> p c j", p=P), in_=res[:, c : c + step, :]
+                )
 
-        def stage(name, offset, width=2 * PASS):
-            return tile_at(name, [width], BF16, offset)[:]
+        def round_w2(g, b, n0, n1, engine_copy=nc.scalar.copy):
+            interleave(g[:, PACK * n0 : PACK * n1], w2_raw[b][:, :, n0:n1], engine_copy)
 
-        def w1_stage(b, n, offset=None):
-            return stage("g%d%d" % (b, n), offset, 2 * PASS * len(groups[b][n]))
-
-        def round_w2(g, b, n):
-            interleave(g[:, n * 2 * PASS : (n + 1) * 2 * PASS], w2_raw[b][:, :, n * HALF : (n + 1) * HALF], nc.scalar.copy)
-
-        def round_z(g, b, j0, j1, engine_copy=nc.scalar.copy):
-            r0 = j0 // HALF * HALF
-            interleave(g[:, PACK * (j0 - r0) : PACK * (j1 - r0)], z_f[b, r0][:, :, j0 - r0 : j1 - r0], engine_copy)
-
-        def finish_z(b, j0):
-            g = stage("gz%d_%d" % (b, j0), None)
-            round_z(g, b, j0, j0 + HALF)
-            quant_z(g, b, j0, j0 + HALF)
+        def slice_differences(n):
+            if n < PACK:
+                slice_a(n)
+            else:
+                differences([unit_b(n - PACK, r) for r in range(2)], tile("child%d" % n, [J], F32))
 
         gather_tab(0)
-        gather_tab(1)
-        v_s = placed("v_s", [S], U8, 14 * KB)
         nc.vector.tensor_copy(v_s[:], tab_s[:].indirect(offs_sb[:]))
-        acc0 = {(t, s): bank(2 * t + s) for t in range(PACK) for s in range(2)}
-        g0 = [w1_stage(0, n, 26 * KB if n == 0 else None) for n in range(5)]
-        round_w1(g0[0], 0, 0, 0, scalar_identity)
-        round_w1(g0[0], 0, 0, 1)
-        quant_w1(g0[0], 0, 0)
-        for t in range(PACK):
-            h_passes(acc0, 0, t, (0,), first=True, last=False)
-        gather_tab(2)
-        round_w1(g0[1], 1, 0, 0)
-        round_w1(g0[2], 1, 0, 1)
-        quant_w1(g0[1], 0, 1)
-        round_w1(g0[3], 2, 0, 0, nc.scalar.copy, 0, 40)
-        round_w1(g0[3], 2, 0, 0, nc.vector.tensor_copy, 40, P)
-        quant_w1(g0[2], 0, 2)
-        quant_w1(g0[3], 0, 3)
-        round_w1(g0[4], 2, 0, 1)
-        h_passes(acc0, 0, 0, (1, 2))
-        h_passes(acc0, 0, 1, (2, 1))
-        evict_h(acc0, 0, 0, 0)
-        evict_h(acc0, 0, 0, 1, on_vector=True)
-        quant_w1(g0[4], 0, 4)
-        h_passes(acc0, 0, 2, (2, 1))
-        h_passes(acc0, 0, 3, (2, 1))
+        round_w1(0, 0, scalar_identity)
+        round_w1(0, 1)
+        round_w1(0, 2)
+        quant_w1(0)
+        quant_w1(1)
+        h_passes((0,), (0,))
+        gather_tab(1)
+        h_passes((0,), (1,))
+        gather_tab(2, 0, BANK)
+        gather_tab(2, BANK, S)
+        h_passes((0,), (2,))
+        for a in range(KA):
+            round_w1(1, a)
+        quant_w1(2)
+        quant_w1(3)
+        h_passes((1,), (0, 1, 2))
+        evict_h(0, 0)
+        evict_h(0, 1, on_vector=True)
 
-        acc1 = {}
-        slice_pairs(0, 0)
-        evict_slice(acc0, 0, 1)
-        slice_pairs(0, 1)
-        g10 = w1_stage(1, 0, 0)
-        round_w1(g10, 0, 1, 0)
-        quant_w1(g10, 1, 0)
-        for t in range(2):
-            for s in range(2):
-                acc1[t, s] = bank(2 * t + s)
-            h_passes(acc1, 1, t, (0,), first=True, last=False)
-        g11 = w1_stage(1, 1, 2 * KB)
-        round_w1(g11, 1, 1, 0)
-        evict_slice(acc0, 0, 2)
-        slice_pairs(0, 2)
-        round_w1(g11, 2, 1, 0)
-        quant_w1(g11, 1, 1)
-        for t in range(2):
-            h_passes(acc1, 1, t, (1, 2))
-        evict_slice(acc0, 0, 3)
-        slice_pairs(0, 3, 4 * KB)
-        g12 = w1_stage(1, 2, 6 * KB)
-        round_w1(g12, 0, 1, 1)
-        round_w1(g12, 1, 1, 1)
-        quant_w1(g12, 1, 2)
-        evict_slice(acc1, 1, 0)
-        g13 = w1_stage(1, 3, 10 * KB)
-        round_w1(g13, 2, 1, 1)
-        quant_w1(g13, 1, 3)
-        for t in range(2, PACK):
-            for s in range(2):
-                acc1[t, s] = bank(2 * t + s)
-            h_passes(acc1, 1, t, (0, 1, 2), first=True)
+        round_w1(2, 0)
+        round_w1(2, 1)
+        slice_around_quant(0, 4)
+        h_passes((2,), (0, 1))
+        round_w1(2, 2)
+        quant_w1(5)
+        h_passes((2,), (2,))
+        h_passes((3,), (2, 0, 1))
+        evict_slice(1)
+        slice_differences(1)
 
-        slice_pairs(1, 0)
-        evict_slice(acc1, 1, 1)
-        slice_pairs(1, 1)
-        finish_z(0, 0)
-        evict_slice(acc1, 1, 2)
-        gw20 = stage("gw20", 33 * KB, 4 * PASS)
-        round_w2(gw20, 0, 0)
-        evict_slice(acc1, 1, 3)
-        pair(1, [(2, 0, HALF), (3, 0, HALF)], own("child_a", [J], F32))
-        round_w2(gw20, 0, 1)
-        quant(w2_w[0][:], w2_s[0][:], gw20)
-        y_a = [bank(c) for c in range(NC)]
-        y_passes(y_a, 0, 0, 0, HALF)
-        pair(1, [(2, HALF, cut), (3, HALF, cut)], keep.tile([P, HALF], F32, name="child_b", tag="w2_raw0", align_bytes=64))
-        gw21 = stage("gw21", 16 * KB, 4 * PASS)
-        round_w2(gw21, 1, 0)
-        round_w2(gw21, 1, 1)
-        quant(w2_w[1][:], w2_s[1][:], gw21)
-        finish_z(1, 0)
-        y_passes(y_a, 0, 1, 0, HALF)
-        pair(1, [(2, cut, J), (3, cut, J)], keep.tile([P, HALF], F32, name="child_c", tag="z_f1_0", align_bytes=64))
-        finish_z(0, HALF)
-        y_b = [bank(NC + c) for c in range(NC)]
-        y_passes(y_b, 1, 0, HALF, J)
-        gz = stage("gz_last", None)
-        round_z(gz, 1, HALF, cut)
-        round_z(gz, 1, cut, J, nc.vector.tensor_copy)
-        quant_z(gz, 1, HALF, J)
-        y_passes(y_b, 1, 1, HALF, J)
-        finish_y(y_a, 0)
-        finish_y(y_b, 1)
+        round_w1(4, 0)
+        evict_slice(2)
+        slice_around_quant(2, 6)
+        h_passes((4, 5), (0,))
+        round_w1(4, 1)
+        quant_w1(10)
+        h_passes((4, 5), (1,))
+        evict_slice(3)
+        round_w1(4, 2)
+        quant_w1(7)
+        h_passes((4, 5), (2,))
+        slice_differences(3)
+        for c in (0, 2, 1, 3):
+            deal(c)
+
+        round_w1(6, 2)
+        quant_w1(8)
+        h_passes((6, 7), (2,))
+        evict_slice(4)
+        slice_differences(4)
+        round_w1(6, 0)
+        round_w1(6, 1)
+        quant_w1(9)
+        h_passes((6, 7), (0, 1))
+        evict_slice(5)
+        slice_differences(5)
+
+        gw2 = [tile("gw20", [PACK * N], BF16, over="w2_first"), tile("gw21", [PACK * N], BF16, over="w2_late")]
+        round_w2(gw2[0], 0, 0, N)
+        quant(w2_w[0][:], w2_s[0][:], gw2[0][:])
+        evict_slice(6)
+        evict_slice(7)
+        differences([unit_b(2, 0), unit_b(3, 0)], tile("child6", [J], F32))
+        gz = [tile("gz0", [PACK * J], BF16, over="z_first"), tile("gz1", [PACK * HALF], BF16, over="z_a", at=2048)]
+        interleave(gz[0][:], z_a[:])
+        quant(z_w[0][:], z_s[0][:], gz[0][:])
+        y = [[[bank(0), bank(1)], [bank(2), bank(3)]], [[bank(4), bank(5)], [bank(6), bank(7)]]]
+        for r in range(2):
+            y_passes(y[r], r, 0)
+        round_w2(gw2[1], 1, 0, N)
+        differences([unit_b(2, 1), unit_b(3, 1)], tile("child7", [J], F32, over="z_a"))
+        quant(w2_w[1][:], w2_s[1][:], gw2[1][:])
+        interleave(gz[1][:], z_b[0][:])
+        quant(z_w[1][:, :HALF], z_s[1][:, :HALF], gz[1][:])
+        y_passes(y[0], 0, 1)
+        gz_last = tile("gz_last", [PACK * HALF], BF16, over="z_b0")
+        interleave(gz_last[:, : PACK * P], z_b[1][:, :, :P])
+        interleave(gz_last[:, PACK * P :], z_b[1][:, :, P:], nc.vector.tensor_copy, 4)
+        quant(z_w[1][:, HALF:], z_s[1][:, HALF:], gz_last[:])
+        y_passes(y[1], 1, 1)
+        finish_y(y[0], 0, 2)
+        finish_y(y[1], 1, 4)

@@ -90,19 +90,19 @@ def tile_list_limb_pair_scores_kernel(
 
         load_tab(0)
         nc.sync.dma_start(offs_sb[:], offs)
-        nc.sync.dma_start(pos2_sb[:], pos2)
+        load_tab(1)
         for q in range(4):
-            nc.scalar.dma_start(
+            nc.sync.dma_start(
                 out=tab_s[32 * q : 32 * q + 4 * KA, :].bitcast(I32),
                 in_=tab_scales[:, 4 * q : 4 * q + 4, :].bitcast(I32),
             )
-        load_tab(1)
         for a in range(KA):
             load_w1(raw_s[0, a], a, 0, P)
         load_tab(2)
         for a in range(KA):
             load_w1(raw_s[1, a], a, P, 2 * P)
         load_b1(0)
+        nc.sync.dma_start(pos2_sb[:], pos2)
         nc.sync.dma_start(pos1_sb[:], pos1)
         for a in range(KA):
             load_w1(raw_a[a], a, 2 * P, PASS)
@@ -126,7 +126,7 @@ def tile_list_limb_pair_scores_kernel(
         with nc.allow_non_contiguous_dma(reason="one bias value a partition"):
             nc.sync.dma_start(out=b3_sb[:], in_=b3.rearrange("(c p) -> p c", p=P))
 
-        v_w = [tile("v_w%d" % a, [S], U32, over=(None, "raw_s01", None)[a]) for a in range(KA)]
+        v_w = [tile("v_w%d" % a, [S], U32, over=(None, None, "raw_s01")[a]) for a in range(KA)]
         v_s = tile("v_s", [S], U8)
         batches = [
             [(0, 0), (0, 1)], [(0, 2)], [(1, 0), (1, 1)], [(1, 2)],
@@ -301,15 +301,14 @@ def tile_list_limb_pair_scores_kernel(
                 differences([unit_b(n - PACK, r) for r in range(2)], tile("child%d" % n, [J], F32))
 
         gather_tab(0)
+        gather_tab(1)
         nc.vector.tensor_copy(v_s[:], tab_s[:].indirect(offs_sb[:]))
         round_w1(0, 0, scalar_identity)
         round_w1(0, 1)
         round_w1(0, 2)
         quant_w1(0)
         quant_w1(1)
-        h_passes((0,), (0,))
-        gather_tab(1)
-        h_passes((0,), (1,))
+        h_passes((0,), (0, 1))
         gather_tab(2, 0, BANK)
         gather_tab(2, BANK, S)
         h_passes((0,), (2,))

@@ -102,10 +102,11 @@ def tile_list_limb_pair_scores_kernel(
         for a in range(KA):
             load_w1(raw_s[1, a], a, P, 2 * P)
         load_b1(0)
+        load_w1(raw_a[0], 0, 2 * P, PASS)
         nc.sync.dma_start(pos2_sb[:], pos2)
+        load_w1(raw_a[1], 1, 2 * P, PASS)
         nc.sync.dma_start(pos1_sb[:], pos1)
-        for a in range(KA):
-            load_w1(raw_a[a], a, 2 * P, PASS)
+        load_w1(raw_a[2], 2, 2 * P, PASS)
         load_b1(1)
         load_w1(raw_b[0], 0, PASS, H)
         load_b1(2)
@@ -132,15 +133,16 @@ def tile_list_limb_pair_scores_kernel(
             [(0, 0), (0, 1)], [(0, 2)], [(1, 0), (1, 1)], [(1, 2)],
             [(2, 0), (3, 0), (2, 1), (3, 1)], [(2, 2), (3, 2)],
             [(4, 0), (5, 0)], [(4, 2), (5, 2)],
-            [(6, 2), (7, 2)], [(6, 1), (7, 1), (6, 0), (7, 0)], [(4, 1), (5, 1)],
+            [(6, 2), (7, 2)], [(6, 0), (7, 0)], [(4, 1), (5, 1)], [(6, 1), (7, 1)],
         ]
         for name in ("w2_late", "r9", "z_first", "w2_first"):
             region(name, 4096)
-        g_over = {9: "r9"}
-        w_over = {2: "tab_w2", 4: "bias0", 6: "bias2", 7: "r9", 9: "z_first"}
-        s_over = {7: "w2_first", 9: "w2_late"}
-        w1_g = [tile("w1_g%d" % k, [PASS * len(b)], BF16, over=g_over.get(k), at=(2048 if k == 10 else 0)) for k, b in enumerate(batches)]
-        w1_w = [tile("w1_w%d" % k, [P * len(b)], U32, over=w_over.get(k)) for k, b in enumerate(batches)]
+        g_over = {9: "r9", 11: "r9"}
+        w_over = {2: "tab_w2", 4: "bias0", 6: "bias2", 11: "z_first"}
+        s_over = {7: "w2_first", 11: "w2_late"}
+        w1_g = [tile("w1_g%d" % k, [PASS * len(b)], BF16, over=g_over.get(k), at=(2048 if k == 11 else 0)) for k, b in enumerate(batches)]
+        place["r9_mid"] = place["r9"] + 1536
+        w1_w = [tile("w1_w%d" % k, [P * len(b)], U32, over=("r9_mid" if k == 7 else w_over.get(k))) for k, b in enumerate(batches)]
         w1_s = [tile("w1_s%d" % k, [P * len(b)], U8, over=s_over.get(k), at=2048) for k, b in enumerate(batches)]
         home = {piece: (k, m) for k, b in enumerate(batches) for m, piece in enumerate(b)}
         w2_w = [tile("w2_w%d" % b, [N], U32) for b in range(HB)]
@@ -148,7 +150,7 @@ def tile_list_limb_pair_scores_kernel(
         h = [tile("h%d" % n, [S], F32, over={0: "raw_s12", 1: "raw_a2"}.get(n)) for n in range(8)]
         z_rows = [tile("z_rows%d" % c, [J], F32, over=("raw_a1", None, None, "w2_late")[c]) for c in range(PACK)]
         z_a = tile("z_a", [PACK, J], F32)
-        z_b = [tile("z_b%d" % r, [PACK, j1 - j0], F32) for r, (j0, j1) in enumerate(RUNS)]
+        z_b = [tile("z_b%d" % r, [PACK, j1 - j0], F32, over="raw_b0", at=4096 * r) for r, (j0, j1) in enumerate(RUNS)]
         z_w = [tile("z_w%d" % b, [J], U32) for b in range(HB)]
         z_s = [tile("z_s%d" % b, [J], U8) for b in range(HB)]
         acc = {}
@@ -173,7 +175,9 @@ def tile_list_limb_pair_scores_kernel(
             if n < 2:
                 interleave(w1_g[k][:, m * PASS : (m + 1) * PASS], raw_s[n, a][:], engine_copy)
             elif n < PACK:
-                interleave(w1_g[k][:, m * PASS : (m + 2) * PASS], raw_a[a][:], engine_copy)
+                lo, hi = 2 * m0, 2 * m1
+                dst = w1_g[k][:, m * PASS + PACK * lo : m * PASS + PACK * hi]
+                interleave(dst, raw_a[a][:, :, lo:hi], engine_copy, 4 if m0 else 2)
             else:
                 dst = w1_g[k][:, m * PASS : (m + 2) * PASS].rearrange("p (t m i) -> p m i t", t=2, i=PACK)
                 src = raw_b[a][:].rearrange("p i (m u t) -> p u m i t", u=2, t=2)
@@ -230,10 +234,14 @@ def tile_list_limb_pair_scores_kernel(
             child = tile("child%d" % c, [J], F32, over={3: "w1_g7"}.get(c))
             differences([(c, j0, j0 + HALF, z_rows[c][:, j0 : j0 + HALF]) for j0 in (0, HALF)], child)
 
-        def slice_around_quant(c, k):
+        def head_share():
+            round_w1(2, 1, nc.vector.tensor_copy, 64, P)
+            quant_w1(4)
+
+        def slice_around(c, between):
             child = tile("child%d" % c, [J], F32, over=None)
             nc.vector.tensor_copy(child[:], h[c][:].indirect(pos2_sb[:]))
-            quant_w1(k)
+            between()
             nc.vector.tensor_tensor(z_rows[c][:], h[c][:].indirect(pos1_sb[:]), child[:], ALU.subtract)
 
         def deal(c):
@@ -321,8 +329,8 @@ def tile_list_limb_pair_scores_kernel(
         evict_h(0, 1, on_vector=True)
 
         round_w1(2, 0)
-        round_w1(2, 1)
-        slice_around_quant(0, 4)
+        round_w1(2, 1, nc.scalar.copy, 0, 64)
+        slice_around(0, head_share)
         h_passes((2,), (0, 1))
         round_w1(2, 2)
         quant_w1(5)
@@ -333,7 +341,7 @@ def tile_list_limb_pair_scores_kernel(
 
         round_w1(4, 0)
         evict_slice(2)
-        slice_around_quant(2, 6)
+        slice_around(2, lambda: quant_w1(6))
         h_passes((4, 5), (0,))
         round_w1(4, 1)
         quant_w1(10)
@@ -350,11 +358,18 @@ def tile_list_limb_pair_scores_kernel(
         quant_w1(8)
         h_passes((6, 7), (2,))
         evict_slice(4)
-        slice_differences(4)
         round_w1(6, 0)
-        round_w1(6, 1)
+        child = tile("child4", [J], F32)
+        nc.vector.tensor_copy(child[:], h[4][:].indirect(pos2_sb[:]))
         quant_w1(9)
-        h_passes((6, 7), (0, 1))
+        h_passes((6, 7), (0,))
+        for r, (j0, j1) in enumerate(RUNS):
+            nc.vector.tensor_tensor(
+                z_b[r][:, 0, :], h[4][:].indirect(pos1_sb[:, j0 // 16 : j1 // 16]), child[:, j0:j1], ALU.subtract
+            )
+        round_w1(6, 1)
+        quant_w1(11)
+        h_passes((6, 7), (1,))
         evict_slice(5)
         slice_differences(5)
 
@@ -365,10 +380,10 @@ def tile_list_limb_pair_scores_kernel(
         evict_slice(7)
         differences([unit_b(2, 0), unit_b(3, 0)], tile("child6", [J], F32))
         gz = [tile("gz0", [PACK * J], BF16, over="z_first"), tile("gz1", [PACK * HALF], BF16, over="z_a", at=2048)]
-        interleave(gz[0][:], z_a[:])
-        quant(z_w[0][:], z_s[0][:], gz[0][:])
         y = [[[bank(0), bank(1)], [bank(2), bank(3)]], [[bank(4), bank(5)], [bank(6), bank(7)]]]
-        for r in range(2):
+        for r, (j0, j1) in enumerate(RUNS):
+            interleave(gz[0][:, PACK * j0 : PACK * j1], z_a[:, :, j0:j1])
+            quant(z_w[0][:, j0:j1], z_s[0][:, j0:j1], gz[0][:, PACK * j0 : PACK * j1])
             y_passes(y[r], r, 0)
         round_w2(gw2[1], 1, 0, N)
         differences([unit_b(2, 1), unit_b(3, 1)], tile("child7", [J], F32, over="z_a"))

@@ -88,32 +88,31 @@ def tile_list_limb_pair_scores_kernel(
             with nc.allow_non_contiguous_dma(reason="one bias value a partition"):
                 nc.sync.dma_start(out=b1_a[c][:], in_=b1[c * P : (c + 1) * P].rearrange("(p o) -> p o", o=1))
 
-        load_tab(0)
         nc.sync.dma_start(offs_sb[:], offs)
+        load_tab(0)
         load_tab(1)
         for q in range(4):
             nc.sync.dma_start(
                 out=tab_s[32 * q : 32 * q + 4 * KA, :].bitcast(I32),
                 in_=tab_scales[:, 4 * q : 4 * q + 4, :].bitcast(I32),
             )
+        load_b1(0)
         for a in range(KA):
             load_w1(raw_s[0, a], a, 0, P)
+        nc.sync.dma_start(pos2_sb[:], pos2)
         load_tab(2)
+        load_b1(1)
         for a in range(KA):
             load_w1(raw_s[1, a], a, P, 2 * P)
-        load_b1(0)
-        load_w1(raw_a[0], 0, 2 * P, PASS)
-        nc.sync.dma_start(pos2_sb[:], pos2)
-        load_w1(raw_a[1], 1, 2 * P, PASS)
         nc.sync.dma_start(pos1_sb[:], pos1)
-        load_w1(raw_a[2], 2, 2 * P, PASS)
-        load_b1(1)
+        for a in range(KA):
+            load_w1(raw_a[a], a, 2 * P, PASS)
+        load_b1(3)
         load_w1(raw_b[0], 0, PASS, H)
         load_b1(2)
-        load_w1(raw_b[1], 1, PASS, H)
-        load_b1(3)
-        load_w1(raw_b[2], 2, PASS, H)
         nc.sync.dma_start(out=b1_b[:], in_=b1[PASS:].rearrange("(p t) -> p t", t=PACK))
+        load_w1(raw_b[1], 1, PASS, H)
+        load_w1(raw_b[2], 2, PASS, H)
         for b in range(HB):
             nc.sync.dma_start(
                 out=w2_raw[b][:], in_=w2[b * PASS : (b + 1) * PASS, :].rearrange("(p i) n -> p i n", i=PACK)
@@ -133,16 +132,15 @@ def tile_list_limb_pair_scores_kernel(
             [(0, 0), (0, 1)], [(0, 2)], [(1, 0), (1, 1)], [(1, 2)],
             [(2, 0), (3, 0), (2, 1), (3, 1)], [(2, 2), (3, 2)],
             [(4, 0), (5, 0)], [(4, 2), (5, 2)],
-            [(6, 2), (7, 2)], [(6, 0), (7, 0)], [(4, 1), (5, 1)], [(6, 1), (7, 1)],
+            [(6, 2), (7, 2), (6, 0), (7, 0)], [(6, 1), (7, 1)], [(4, 1), (5, 1)],
         ]
         for name in ("w2_late", "r9", "z_first", "w2_first"):
             region(name, 4096)
-        g_over = {9: "r9", 11: "r9"}
-        w_over = {2: "tab_w2", 4: "bias0", 6: "bias2", 11: "z_first"}
-        s_over = {7: "w2_first", 11: "w2_late"}
-        w1_g = [tile("w1_g%d" % k, [PASS * len(b)], BF16, over=g_over.get(k), at=(2048 if k == 11 else 0)) for k, b in enumerate(batches)]
-        place["r9_mid"] = place["r9"] + 1536
-        w1_w = [tile("w1_w%d" % k, [P * len(b)], U32, over=("r9_mid" if k == 7 else w_over.get(k))) for k, b in enumerate(batches)]
+        g_over = {9: "r9"}
+        w_over = {2: "tab_w2", 4: "bias0", 6: "bias2", 7: "r9", 9: "z_first"}
+        s_over = {7: "w2_first", 9: "w2_late"}
+        w1_g = [tile("w1_g%d" % k, [PASS * len(b)], BF16, over=g_over.get(k)) for k, b in enumerate(batches)]
+        w1_w = [tile("w1_w%d" % k, [P * len(b)], U32, over=w_over.get(k)) for k, b in enumerate(batches)]
         w1_s = [tile("w1_s%d" % k, [P * len(b)], U8, over=s_over.get(k), at=2048) for k, b in enumerate(batches)]
         home = {piece: (k, m) for k, b in enumerate(batches) for m, piece in enumerate(b)}
         w2_w = [tile("w2_w%d" % b, [N], U32) for b in range(HB)]
@@ -150,7 +148,7 @@ def tile_list_limb_pair_scores_kernel(
         h = [tile("h%d" % n, [S], F32, over={0: "raw_s12", 1: "raw_a2"}.get(n)) for n in range(8)]
         z_rows = [tile("z_rows%d" % c, [J], F32, over=("raw_a1", None, None, "w2_late")[c]) for c in range(PACK)]
         z_a = tile("z_a", [PACK, J], F32)
-        z_b = [tile("z_b%d" % r, [PACK, j1 - j0], F32, over="raw_b0", at=4096 * r) for r, (j0, j1) in enumerate(RUNS)]
+        z_b = [tile("z_b%d" % r, [PACK, j1 - j0], F32) for r, (j0, j1) in enumerate(RUNS)]
         z_w = [tile("z_w%d" % b, [J], U32) for b in range(HB)]
         z_s = [tile("z_s%d" % b, [J], U8) for b in range(HB)]
         acc = {}
@@ -340,6 +338,7 @@ def tile_list_limb_pair_scores_kernel(
         slice_differences(1)
 
         round_w1(4, 0)
+        round_w1(6, 0, nc.vector.tensor_copy)
         evict_slice(2)
         slice_around(2, lambda: quant_w1(6))
         h_passes((4, 5), (0,))
@@ -356,19 +355,11 @@ def tile_list_limb_pair_scores_kernel(
 
         round_w1(6, 2)
         quant_w1(8)
-        h_passes((6, 7), (2,))
+        h_passes((6, 7), (2, 0))
         evict_slice(4)
-        round_w1(6, 0)
-        child = tile("child4", [J], F32)
-        nc.vector.tensor_copy(child[:], h[4][:].indirect(pos2_sb[:]))
-        quant_w1(9)
-        h_passes((6, 7), (0,))
-        for r, (j0, j1) in enumerate(RUNS):
-            nc.vector.tensor_tensor(
-                z_b[r][:, 0, :], h[4][:].indirect(pos1_sb[:, j0 // 16 : j1 // 16]), child[:, j0:j1], ALU.subtract
-            )
+        slice_differences(4)
         round_w1(6, 1)
-        quant_w1(11)
+        quant_w1(9)
         h_passes((6, 7), (1,))
         evict_slice(5)
         slice_differences(5)

@@ -72,6 +72,8 @@ def tile_list_limb_pair_scores_kernel(
         region("pad", 2048)
         raw_a = [tile("raw_a%d" % a, [PACK, 2 * P], F32) for a in range(KA)]
         raw_b = [tile("raw_b%d" % a, [PACK, PASS], F32) for a in range(KA)]
+        place["w2_late"] = place["end"] - 1024
+        place["end"] = place["end"] + 3072
         w2_raw = [tile("w2_raw%d" % b, [PACK, N], F32) for b in range(HB)]
 
         nc.vector.memset(tab_s[:].bitcast(I32), 0)
@@ -134,7 +136,7 @@ def tile_list_limb_pair_scores_kernel(
             [(4, 0), (5, 0)], [(4, 2), (5, 2)],
             [(6, 2), (7, 2), (6, 0), (7, 0)], [(6, 1), (7, 1)], [(4, 1), (5, 1)],
         ]
-        for name in ("w2_late", "r9", "z_first", "w2_first"):
+        for name in ("r9", "z_first", "w2_first"):
             region(name, 4096)
         g_over = {9: "r9"}
         w_over = {2: "tab_w2", 4: "bias0", 6: "bias2", 7: "r9", 9: "z_first"}
@@ -148,7 +150,7 @@ def tile_list_limb_pair_scores_kernel(
         h = [tile("h%d" % n, [S], F32, over={0: "raw_s12", 1: "raw_a2"}.get(n)) for n in range(8)]
         z_rows = [tile("z_rows%d" % c, [J], F32, over=("raw_a1", None, None, "w2_late")[c]) for c in range(PACK)]
         z_a = tile("z_a", [PACK, J], F32)
-        z_b = [tile("z_b%d" % r, [PACK, j1 - j0], F32) for r, (j0, j1) in enumerate(RUNS)]
+        z_b = [tile("z_b%d" % r, [PACK, j1 - j0], F32, over="raw_b1", at=16 * j0) for r, (j0, j1) in enumerate(RUNS)]
         z_w = [tile("z_w%d" % b, [J], U32) for b in range(HB)]
         z_s = [tile("z_s%d" % b, [J], U8) for b in range(HB)]
         acc = {}
@@ -236,8 +238,8 @@ def tile_list_limb_pair_scores_kernel(
             round_w1(2, 1, nc.vector.tensor_copy, 64, P)
             quant_w1(4)
 
-        def slice_around(c, between):
-            child = tile("child%d" % c, [J], F32, over=None)
+        def slice_around(c, between, over=None):
+            child = tile("child%d" % c, [J], F32, over=over)
             nc.vector.tensor_copy(child[:], h[c][:].indirect(pos2_sb[:]))
             between()
             nc.vector.tensor_tensor(z_rows[c][:], h[c][:].indirect(pos1_sb[:]), child[:], ALU.subtract)
@@ -266,16 +268,15 @@ def tile_list_limb_pair_scores_kernel(
                     )
                 for c in range(c0, c0 + per):
                     cols = slice(c * P, (c + 1) * P)
-                    for j in range(0, w, P):
-                        nc.tensor.matmul_mx(
-                            out=y[1][c // per][:, (c % per) * w + j : (c % per) * w + j + P],
-                            lhsT=w4_w[:, b, 2 * c * P : 2 * (c + 1) * P].bitcast(FP4X4),
-                            lhsT_scale=w4_s[:, b, cols],
-                            rhs=z_w[b][:, j0 + j : j0 + j + P].bitcast(FP8X4),
-                            rhs_scale=z_s[b][:, j0 + j : j0 + j + P],
-                            start=(b == 0 and c % per == 0 and j == 0),
-                            stop=(b == HB - 1 and c % per == per - 1 and j + P == w),
-                        )
+                    nc.tensor.matmul_mx(
+                        out=y[1][c // per][:, (c % per) * w : (c % per + 1) * w],
+                        lhsT=w4_w[:, b, 2 * c * P : 2 * (c + 1) * P].bitcast(FP4X4),
+                        lhsT_scale=w4_s[:, b, cols],
+                        rhs=z_w[b][:, j0:j1].bitcast(FP8X4),
+                        rhs_scale=z_s[b][:, j0:j1],
+                        start=(b == 0 and c % per == 0),
+                        stop=(b == HB - 1 and c % per == per - 1),
+                    )
 
         def finish_y(y, r, stores):
             j0, j1 = RUNS[r]
@@ -349,18 +350,22 @@ def tile_list_limb_pair_scores_kernel(
         round_w1(4, 2)
         quant_w1(7)
         h_passes((4, 5), (2,))
-        slice_differences(3)
+        round_w1(6, 2)
+        slice_around(3, lambda: quant_w1(8), "w1_g7")
         for c in (0, 2, 1, 3):
             deal(c)
 
-        round_w1(6, 2)
-        quant_w1(8)
         h_passes((6, 7), (2, 0))
         evict_slice(4)
-        slice_differences(4)
+        child4 = tile("child4", [J], F32)
+        nc.vector.tensor_copy(child4[:], h[4][:].indirect(pos2_sb[:]))
         round_w1(6, 1)
         quant_w1(9)
         h_passes((6, 7), (1,))
+        for r, (j0, j1) in enumerate(RUNS):
+            nc.vector.tensor_tensor(
+                z_b[r][:, 0, :], h[4][:].indirect(pos1_sb[:, j0 // 16 : j1 // 16]), child4[:, j0:j1], ALU.subtract
+            )
         evict_slice(5)
         slice_differences(5)
 
@@ -376,15 +381,14 @@ def tile_list_limb_pair_scores_kernel(
             interleave(gz[0][:, PACK * j0 : PACK * j1], z_a[:, :, j0:j1])
             quant(z_w[0][:, j0:j1], z_s[0][:, j0:j1], gz[0][:, PACK * j0 : PACK * j1])
             y_passes(y[r], r, 0)
-        round_w2(gw2[1], 1, 0, N)
         differences([unit_b(2, 1), unit_b(3, 1)], tile("child7", [J], F32, over="z_a"))
-        quant(w2_w[1][:], w2_s[1][:], gw2[1][:])
         interleave(gz[1][:], z_b[0][:])
         quant(z_w[1][:, :HALF], z_s[1][:, :HALF], gz[1][:])
+        round_w2(gw2[1], 1, 0, N)
+        quant(w2_w[1][:], w2_s[1][:], gw2[1][:])
         y_passes(y[0], 0, 1)
         gz_last = tile("gz_last", [PACK * HALF], BF16, over="z_b0")
-        interleave(gz_last[:, : PACK * P], z_b[1][:, :, :P])
-        interleave(gz_last[:, PACK * P :], z_b[1][:, :, P:], nc.vector.tensor_copy, 4)
+        interleave(gz_last[:], z_b[1][:])
         quant(z_w[1][:, HALF:], z_s[1][:, HALF:], gz_last[:])
         y_passes(y[1], 1, 1)
         finish_y(y[0], 0, 2)

@@ -24,8 +24,31 @@ KA = K // PASS
 HB = H // PASS
 NC = N // P
 BANK = 512
-HALF = J // 2
-RUNS = [(0, 256), (256, 512)]
+QUAD = 32
+LIST = 16
+ALIGN = 64
+KB = 1024
+RUN = J // 2
+RUNS = [(0, RUN), (RUN, J)]
+PER_BANK = BANK // RUN
+SCALAR_WALK = 2
+VECTOR_WALK = 4
+STORES = (2, 4)
+
+BATCHES = {
+    "s0_first": [(0, 0), (0, 1)],
+    "s0_close": [(0, 2)],
+    "s1_first": [(1, 0), (1, 1)],
+    "s1_close": [(1, 2)],
+    "s23_first": [(2, 0), (3, 0), (2, 1), (3, 1)],
+    "s23_last": [(2, 2), (3, 2)],
+    "s45_first": [(4, 0), (5, 0)],
+    "s45_close": [(4, 2), (5, 2)],
+    "s67_first": [(6, 2), (7, 2), (6, 0), (7, 0)],
+    "s67_close": [(6, 1), (7, 1)],
+    "s45_mid": [(4, 1), (5, 1)],
+}
+CLOSES_WITH_PASS_1 = (3, 6, 7)
 
 
 def tile_list_limb_pair_scores_kernel(
@@ -33,7 +56,7 @@ def tile_list_limb_pair_scores_kernel(
 ):
     nc = tc.nc
     with ExitStack() as ctx:
-        keep = ctx.enter_context(tc.tile_pool(name="keep", bufs=1))
+        lists = ctx.enter_context(tc.tile_pool(name="keep", bufs=1))
         arena = ctx.enter_context(tc.tile_pool(name="arena", bufs=1))
         psum = ctx.enter_context(tc.psum_pool(name="psum", bufs=1))
         place = {"end": 0}
@@ -41,9 +64,9 @@ def tile_list_limb_pair_scores_kernel(
         def bank(i):
             return psum.tile([P, BANK], F32, name="bank%d" % i)
 
-        def region(name, size):
-            place[name] = place["end"]
-            place["end"] = place["end"] + size
+        def region(name, size, back=0):
+            place[name] = place["end"] - back
+            place["end"] = place[name] + size
 
         def tile(name, shape, dtype, over=None, at=0):
             size = SIZE[dtype]
@@ -51,29 +74,28 @@ def tile_list_limb_pair_scores_kernel(
                 size = size * d
             if over is None:
                 place[name] = place["end"]
-                place["end"] = place["end"] + (size + 63) // 64 * 64
+                place["end"] = place["end"] + (size + ALIGN - 1) // ALIGN * ALIGN
             else:
                 place[name] = place[over] + at
-            return arena.tile([P] + shape, dtype, name=name, offset=place[name], align_bytes=64)
+            return arena.tile([P] + shape, dtype, name=name, offset=place[name], align_bytes=ALIGN)
 
-        offs_sb = keep.tile([P, S // 16], U16, name="offs_sb")
-        pos1_sb = keep.tile([P, J // 16], U16, name="pos1_sb")
-        pos2_sb = keep.tile([P, J // 16], U16, name="pos2_sb")
+        offs_sb = lists.tile([P, S // LIST], U16, name="offs_sb")
+        pos1_sb = lists.tile([P, J // LIST], U16, name="pos1_sb")
+        pos2_sb = lists.tile([P, J // LIST], U16, name="pos2_sb")
         tab_w = [tile("tab_w%d" % a, [T], I32) for a in range(KA)]
         tab_s = tile("tab_s", [T], U8)
         w4_w = tile("w4_w", [HB, 2 * N], U8)
         w4_s = tile("w4_s", [HB, N], U8)
         for c in range(PACK):
-            region("bias%d" % c, 2048)
-        b1_a = [tile("b1_a%d" % c, [1], F32, over="bias%d" % c) for c in range(PACK)]
-        b1_b = tile("b1_b", [PACK], F32)
+            region("bias%d" % c, 2 * KB)
+        b1_low = [tile("b1_a%d" % c, [1], F32, over="bias%d" % c) for c in range(PACK)]
+        b1_high = tile("b1_b", [PACK], F32)
         b3_sb = tile("b3_sb", [NC], F32)
-        raw_s = {(n, a): tile("raw_s%d%d" % (n, a), [PACK, P], F32) for n in range(2) for a in range(KA)}
-        region("pad", 2048)
-        raw_a = [tile("raw_a%d" % a, [PACK, 2 * P], F32) for a in range(KA)]
-        raw_b = [tile("raw_b%d" % a, [PACK, PASS], F32) for a in range(KA)]
-        place["w2_late"] = place["end"] - 1024
-        place["end"] = place["end"] + 3072
+        raw_one = {(n, a): tile("raw_s%d%d" % (n, a), [PACK, P], F32) for n in range(2) for a in range(KA)}
+        region("h0_rest", 2 * KB)
+        raw_two = [tile("raw_a%d" % a, [PACK, 2 * P], F32) for a in range(KA)]
+        raw_four = [tile("raw_b%d" % a, [PACK, PASS], F32) for a in range(KA)]
+        region("w2_late", 4 * KB, back=KB)
         w2_raw = [tile("w2_raw%d" % b, [PACK, N], F32) for b in range(HB)]
 
         nc.vector.memset(tab_s[:].bitcast(I32), 0)
@@ -88,41 +110,42 @@ def tile_list_limb_pair_scores_kernel(
 
         def load_b1(c):
             with nc.allow_non_contiguous_dma(reason="one bias value a partition"):
-                nc.sync.dma_start(out=b1_a[c][:], in_=b1[c * P : (c + 1) * P].rearrange("(p o) -> p o", o=1))
+                nc.sync.dma_start(out=b1_low[c][:], in_=b1[c * P : (c + 1) * P].rearrange("(p o) -> p o", o=1))
 
         nc.sync.dma_start(offs_sb[:], offs)
         load_tab(0)
         load_tab(1)
-        for q in range(4):
+        for q in range(P // QUAD):
             nc.sync.dma_start(
-                out=tab_s[32 * q : 32 * q + 4 * KA, :].bitcast(I32),
+                out=tab_s[QUAD * q : QUAD * q + 4 * KA, :].bitcast(I32),
                 in_=tab_scales[:, 4 * q : 4 * q + 4, :].bitcast(I32),
             )
         load_b1(0)
         for a in range(KA):
-            load_w1(raw_s[0, a], a, 0, P)
+            load_w1(raw_one[0, a], a, 0, P)
         nc.sync.dma_start(pos2_sb[:], pos2)
         load_tab(2)
-        load_b1(1)
         for a in range(KA):
-            load_w1(raw_s[1, a], a, P, 2 * P)
+            load_w1(raw_one[1, a], a, P, 2 * P)
+        load_w1(raw_two[0], 0, 2 * P, PASS)
         nc.sync.dma_start(pos1_sb[:], pos1)
-        for a in range(KA):
-            load_w1(raw_a[a], a, 2 * P, PASS)
-        load_b1(3)
-        load_w1(raw_b[0], 0, PASS, H)
+        load_b1(1)
+        for a in (1, 2):
+            load_w1(raw_two[a], a, 2 * P, PASS)
+        load_w1(raw_four[0], 0, PASS, H)
         load_b1(2)
-        nc.sync.dma_start(out=b1_b[:], in_=b1[PASS:].rearrange("(p t) -> p t", t=PACK))
-        load_w1(raw_b[1], 1, PASS, H)
-        load_w1(raw_b[2], 2, PASS, H)
+        load_w1(raw_four[1], 1, PASS, H)
+        load_b1(3)
+        load_w1(raw_four[2], 2, PASS, H)
+        nc.sync.dma_start(out=b1_high[:], in_=b1[PASS:].rearrange("(p t) -> p t", t=PACK))
         for b in range(HB):
             nc.sync.dma_start(
                 out=w2_raw[b][:], in_=w2[b * PASS : (b + 1) * PASS, :].rearrange("(p i) n -> p i n", i=PACK)
             )
         nc.sync.dma_start(out=w4_w[:].bitcast(I32), in_=w4_words.rearrange("b p n -> p b n").bitcast(I32))
-        for q in range(4):
+        for q in range(P // QUAD):
             nc.sync.dma_start(
-                out=w4_s[32 * q : 32 * q + 4, :, :].bitcast(I32),
+                out=w4_s[QUAD * q : QUAD * q + 4, :, :].bitcast(I32),
                 in_=w4_scales[:, 4 * q : 4 * q + 4, :].rearrange("b r n -> r b n").bitcast(I32),
             )
         with nc.allow_non_contiguous_dma(reason="one bias value a partition"):
@@ -130,33 +153,29 @@ def tile_list_limb_pair_scores_kernel(
 
         v_w = [tile("v_w%d" % a, [S], U32, over=(None, None, "raw_s01")[a]) for a in range(KA)]
         v_s = tile("v_s", [S], U8)
-        batches = [
-            [(0, 0), (0, 1)], [(0, 2)], [(1, 0), (1, 1)], [(1, 2)],
-            [(2, 0), (3, 0), (2, 1), (3, 1)], [(2, 2), (3, 2)],
-            [(4, 0), (5, 0)], [(4, 2), (5, 2)],
-            [(6, 2), (7, 2), (6, 0), (7, 0)], [(6, 1), (7, 1)], [(4, 1), (5, 1)],
-        ]
-        for name in ("r9", "z_first", "w2_first"):
-            region(name, 4096)
-        g_over = {9: "r9"}
-        w_over = {2: "tab_w2", 4: "bias0", 6: "bias2", 7: "r9", 9: "z_first"}
-        s_over = {7: "w2_first", 9: "w2_late"}
-        w1_g = [tile("w1_g%d" % k, [PASS * len(b)], BF16, over=g_over.get(k)) for k, b in enumerate(batches)]
-        w1_w = [tile("w1_w%d" % k, [P * len(b)], U32, over=w_over.get(k)) for k, b in enumerate(batches)]
-        w1_s = [tile("w1_s%d" % k, [P * len(b)], U8, over=s_over.get(k), at=2048) for k, b in enumerate(batches)]
-        home = {piece: (k, m) for k, b in enumerate(batches) for m, piece in enumerate(b)}
+        for name in ("after45", "z_first", "w2_first"):
+            region(name, 4 * KB)
+        rounded_over = {"s67_close": "after45"}
+        words_over = {
+            "s1_first": "tab_w2", "s23_first": "bias0", "s45_first": "bias2", "s45_close": "after45", "s67_close": "z_first",
+        }
+        scales_over = {"s45_close": "w2_first", "s67_close": "w2_late"}
+        w1_g = {k: tile("g_" + k, [PASS * len(b)], BF16, over=rounded_over.get(k)) for k, b in BATCHES.items()}
+        w1_w = {k: tile("w_" + k, [P * len(b)], U32, over=words_over.get(k)) for k, b in BATCHES.items()}
+        w1_s = {k: tile("s_" + k, [P * len(b)], U8, over=scales_over.get(k), at=2 * KB) for k, b in BATCHES.items()}
+        home = {piece: (k, m) for k, b in BATCHES.items() for m, piece in enumerate(b)}
         w2_w = [tile("w2_w%d" % b, [N], U32) for b in range(HB)]
         w2_s = [tile("w2_s%d" % b, [N], U8) for b in range(HB)]
-        h = [tile("h%d" % n, [S], F32, over={0: "raw_s12", 1: "raw_a2"}.get(n)) for n in range(8)]
+        h = [tile("h%d" % n, [S], F32, over={0: "raw_s12", 1: "raw_a2"}.get(n)) for n in range(H // P)]
         z_rows = [tile("z_rows%d" % c, [J], F32, over=("raw_a1", None, None, "w2_late")[c]) for c in range(PACK)]
-        z_a = tile("z_a", [PACK, J], F32)
-        z_b = [tile("z_b%d" % r, [PACK, j1 - j0], F32, over="raw_b1", at=16 * j0) for r, (j0, j1) in enumerate(RUNS)]
+        z_low = tile("z_a", [PACK, J], F32)
+        z_high = [tile("z_b%d" % r, [PACK, RUN], F32, over="raw_b1", at=4 * PACK * j0) for r, (j0, j1) in enumerate(RUNS)]
         z_w = [tile("z_w%d" % b, [J], U32) for b in range(HB)]
         z_s = [tile("z_s%d" % b, [J], U8) for b in range(HB)]
         acc = {}
 
         def gather_tab(a, e0=0, e1=S):
-            nc.vector.tensor_copy(v_w[a][:, e0:e1], tab_w[a][:].bitcast(U32).indirect(offs_sb[:, e0 // 16 : e1 // 16]))
+            nc.vector.tensor_copy(v_w[a][:, e0:e1], tab_w[a][:].bitcast(U32).indirect(offs_sb[:, e0 // LIST : e1 // LIST]))
 
         def quant(words, scales, src):
             nc.vector.quantize_mx(out=words.bitcast(FP8X4), scales=scales, in_=src)
@@ -164,24 +183,26 @@ def tile_list_limb_pair_scores_kernel(
         def scalar_identity(out, in_):
             nc.scalar.activation(out=out, in_=in_, func=ACT.Identity)
 
-        def interleave(dst, src, engine_copy=nc.scalar.copy, run=2):
+        def interleave(dst, src, engine_copy=nc.scalar.copy, walk=SCALAR_WALK):
             engine_copy(
-                out=dst.rearrange("p (c u t) -> p c t u", u=run, t=PACK),
-                in_=src.rearrange("p t (c u) -> p c t u", u=run),
+                out=dst.rearrange("p (c u t) -> p c t u", u=walk, t=PACK),
+                in_=src.rearrange("p t (c u) -> p c t u", u=walk),
             )
 
-        def round_w1(n, a, engine_copy=nc.scalar.copy, m0=0, m1=P):
+        def round_one(n, a, engine_copy=nc.scalar.copy):
             k, m = home[n, a]
-            if n < 2:
-                interleave(w1_g[k][:, m * PASS : (m + 1) * PASS], raw_s[n, a][:], engine_copy)
-            elif n < PACK:
-                lo, hi = 2 * m0, 2 * m1
-                dst = w1_g[k][:, m * PASS + PACK * lo : m * PASS + PACK * hi]
-                interleave(dst, raw_a[a][:, :, lo:hi], engine_copy, 4 if m0 else 2)
-            else:
-                dst = w1_g[k][:, m * PASS : (m + 2) * PASS].rearrange("p (t m i) -> p m i t", t=2, i=PACK)
-                src = raw_b[a][:].rearrange("p i (m u t) -> p u m i t", u=2, t=2)
-                engine_copy(out=dst[:, m0:m1], in_=src[:, (n - PACK) // 2, m0:m1])
+            interleave(w1_g[k][:, m * PASS : (m + 1) * PASS], raw_one[n, a][:], engine_copy)
+
+        def round_two(a, c0=0, c1=2 * P, engine_copy=nc.scalar.copy, walk=SCALAR_WALK):
+            k, m = home[2, a]
+            dst = w1_g[k][:, m * PASS + PACK * c0 : m * PASS + PACK * c1]
+            interleave(dst, raw_two[a][:, :, c0:c1], engine_copy, walk)
+
+        def round_pair(n, a, engine_copy=nc.scalar.copy):
+            k, first = home[n, a]
+            dst = w1_g[k][:, first * PASS : (first + 2) * PASS].rearrange("p (t m i) -> p m i t", t=2, i=PACK)
+            src = raw_four[a][:].rearrange("p i (m u t) -> p u m i t", u=2, t=2)
+            engine_copy(out=dst, in_=src[:, (n - PACK) // 2])
 
         def quant_w1(k):
             quant(w1_w[k][:], w1_s[k][:], w1_g[k][:])
@@ -192,204 +213,184 @@ def tile_list_limb_pair_scores_kernel(
                 acc[n, s] = bank(2 * (n % 4) + s)
             k, m = home[n, a]
             cols = slice(m * P, (m + 1) * P)
-            ent = slice(s * BANK, (s + 1) * BANK)
+            entries = slice(s * BANK, (s + 1) * BANK)
             nc.tensor.matmul_mx(
                 out=acc[n, s][:],
                 lhsT=w1_w[k][:, cols].bitcast(FP8X4),
                 lhsT_scale=w1_s[k][:, cols],
-                rhs=v_w[a][:, ent].bitcast(FP8X4),
-                rhs_scale=v_s[4 * a :, ent],
+                rhs=v_w[a][:, entries].bitcast(FP8X4),
+                rhs_scale=v_s[4 * a :, entries],
                 start=first,
-                stop=(a == (1 if n in (3, 6, 7) else KA - 1)),
+                stop=(a == (1 if n in CLOSES_WITH_PASS_1 else KA - 1)),
             )
 
         def h_passes(slices, order):
             for n in slices:
-                for s in range(2):
+                for s in range(S // BANK):
                     for a in order:
                         h_pass(n, a, s)
 
-        def evict_h(n, s, on_vector=False):
-            dst = h[n][:, s * BANK : (s + 1) * BANK]
-            bias = b1_a[n][:] if n < PACK else b1_b[:, n - PACK : n - PACK + 1]
-            if on_vector:
-                nc.vector.tensor_scalar(dst, acc[n, s][:], bias, 0.0, ALU.add, ALU.max)
-            else:
-                nc.scalar.activation(out=dst, in_=acc[n, s][:], func=ACT.Relu, bias=bias)
+        def h_bias(n):
+            return b1_low[n][:] if n < PACK else b1_high[:, n - PACK : n - PACK + 1]
+
+        def evict_bank(n, s):
+            nc.scalar.activation(out=h[n][:, s * BANK : (s + 1) * BANK], in_=acc[n, s][:], func=ACT.Relu, bias=h_bias(n))
 
         def evict_slice(n):
-            for s in range(2):
-                evict_h(n, s)
+            for s in range(S // BANK):
+                evict_bank(n, s)
 
-        def differences(units, child):
-            ends = [sum(j1 - j0 for n, j0, j1, dst in units[:k]) for k in range(len(units) + 1)]
-            for k, (n, j0, j1, dst) in enumerate(units):
-                nc.vector.tensor_copy(child[:, ends[k] : ends[k + 1]], h[n][:].indirect(pos2_sb[:, j0 // 16 : j1 // 16]))
-            for k, (n, j0, j1, dst) in enumerate(units):
-                nc.vector.tensor_tensor(
-                    dst, h[n][:].indirect(pos1_sb[:, j0 // 16 : j1 // 16]), child[:, ends[k] : ends[k + 1]], ALU.subtract
-                )
+        def children(dst, n, j0, j1):
+            nc.vector.tensor_copy(dst, h[n][:].indirect(pos2_sb[:, j0 // LIST : j1 // LIST]))
 
-        def slice_a(c):
-            child = tile("child%d" % c, [J], F32, over={3: "w1_g7"}.get(c))
-            differences([(c, j0, j0 + HALF, z_rows[c][:, j0 : j0 + HALF]) for j0 in (0, HALF)], child)
+        def parents_less(dst, n, j0, j1, kids):
+            nc.vector.tensor_tensor(dst, h[n][:].indirect(pos1_sb[:, j0 // LIST : j1 // LIST]), kids, ALU.subtract)
 
-        def head_share():
-            round_w1(2, 1, nc.vector.tensor_copy, 64, P)
-            quant_w1(4)
+        def z_part(n, r):
+            j0, j1 = RUNS[r]
+            return z_rows[n][:, j0:j1] if n < PACK else z_high[r][:, n - PACK, :]
 
-        def slice_around(c, between, over=None):
-            child = tile("child%d" % c, [J], F32, over=over)
-            nc.vector.tensor_copy(child[:], h[c][:].indirect(pos2_sb[:]))
-            between()
-            nc.vector.tensor_tensor(z_rows[c][:], h[c][:].indirect(pos1_sb[:]), child[:], ALU.subtract)
+        def differences(units, kids):
+            for k, (n, r) in enumerate(units):
+                children(kids[:, k * RUN : (k + 1) * RUN], n, *RUNS[r])
+            for k, (n, r) in enumerate(units):
+                parents_less(z_part(n, r), n, *RUNS[r], kids[:, k * RUN : (k + 1) * RUN])
 
         def deal(c):
-            nc.sync.dma_start(out=z_a[32 * c : 32 * (c + 1), :, :], in_=z_rows[c][:])
+            nc.sync.dma_start(out=z_low[QUAD * c : QUAD * (c + 1), :, :], in_=z_rows[c][:])
 
-        def unit_b(t, r):
-            return (PACK + t, RUNS[r][0], RUNS[r][1], z_b[r][:, t, :])
-
-        def y_passes(y, r, b):
+        def y_passes(banks, r, b):
             j0, j1 = RUNS[r]
-            w = j1 - j0
-            per = BANK // w
-            for c0 in range(0, NC, per):
-                for c in range(c0, c0 + per):
-                    cols = slice(c * P, (c + 1) * P)
-                    nc.tensor.matmul_mx(
-                        out=y[0][c // per][:, (c % per) * w : (c % per + 1) * w],
-                        lhsT=w2_w[b][:, cols].bitcast(FP8X4),
-                        lhsT_scale=w2_s[b][:, cols],
-                        rhs=z_w[b][:, j0:j1].bitcast(FP8X4),
-                        rhs_scale=z_s[b][:, j0:j1],
-                        start=(b == 0 and c % per == 0),
-                        stop=(b == HB - 1 and c % per == per - 1),
-                    )
-                for c in range(c0, c0 + per):
-                    cols = slice(c * P, (c + 1) * P)
-                    nc.tensor.matmul_mx(
-                        out=y[1][c // per][:, (c % per) * w : (c % per + 1) * w],
-                        lhsT=w4_w[:, b, 2 * c * P : 2 * (c + 1) * P].bitcast(FP4X4),
-                        lhsT_scale=w4_s[:, b, cols],
-                        rhs=z_w[b][:, j0:j1].bitcast(FP8X4),
-                        rhs_scale=z_s[b][:, j0:j1],
-                        start=(b == 0 and c % per == 0),
-                        stop=(b == HB - 1 and c % per == per - 1),
-                    )
+            for c0 in range(0, NC, PER_BANK):
+                for view in range(2):
+                    for c in range(c0, c0 + PER_BANK):
+                        cols = slice(c * P, (c + 1) * P)
+                        if view == 0:
+                            weights, scales = w2_w[b][:, cols].bitcast(FP8X4), w2_s[b][:, cols]
+                        else:
+                            weights, scales = w4_w[:, b, 2 * c * P : 2 * (c + 1) * P].bitcast(FP4X4), w4_s[:, b, cols]
+                        nc.tensor.matmul_mx(
+                            out=banks[view][c // PER_BANK][:, (c % PER_BANK) * RUN : (c % PER_BANK + 1) * RUN],
+                            lhsT=weights,
+                            lhsT_scale=scales,
+                            rhs=z_w[b][:, j0:j1].bitcast(FP8X4),
+                            rhs_scale=z_s[b][:, j0:j1],
+                            start=(b == 0 and c % PER_BANK == 0),
+                            stop=(b == HB - 1 and c % PER_BANK == PER_BANK - 1),
+                        )
 
-        def finish_y(y, r, stores):
+        def finish_run(banks, r):
             j0, j1 = RUNS[r]
-            w = j1 - j0
-            per = BANK // w
-            y1b = tile("y1b%d" % r, [NC, w], F32, over="tab_w0", at=16 * j0)
-            res = tile("res%d" % r, [NC, w], F32, over="tab_w1", at=16 * j0)
+            y1_biased = tile("y1b%d" % r, [NC, RUN], F32, over="tab_w0", at=4 * NC * j0)
+            res = tile("res%d" % r, [NC, RUN], F32, over="tab_w1", at=4 * NC * j0)
             for c in range(NC):
-                part = slice((c % per) * w, (c % per + 1) * w)
-                nc.scalar.activation(out=y1b[:, c, :], in_=y[0][c // per][:, part], func=ACT.Identity, bias=b3_sb[:, c : c + 1])
-            for c in range(NC):
-                part = slice((c % per) * w, (c % per + 1) * w)
-                nc.vector.scalar_tensor_tensor(
-                    res[:, c, :], y[1][c // per][:, part], b3_sb[:, c : c + 1], y1b[:, c, :], ALU.add, ALU.max
+                part = slice((c % PER_BANK) * RUN, (c % PER_BANK + 1) * RUN)
+                nc.scalar.activation(
+                    out=y1_biased[:, c, :], in_=banks[0][c // PER_BANK][:, part], func=ACT.Identity, bias=b3_sb[:, c : c + 1]
                 )
-            step = NC // stores
+            for c in range(NC):
+                part = slice((c % PER_BANK) * RUN, (c % PER_BANK + 1) * RUN)
+                nc.vector.scalar_tensor_tensor(
+                    res[:, c, :], banks[1][c // PER_BANK][:, part], b3_sb[:, c : c + 1], y1_biased[:, c, :], ALU.add, ALU.max
+                )
+            step = NC // STORES[r]
             for c in range(0, NC, step):
                 nc.sync.dma_start(
                     out=out[c * P : (c + step) * P, j0:j1].rearrange("(c p) j -> p c j", p=P), in_=res[:, c : c + step, :]
                 )
 
-        def round_w2(g, b, n0, n1, engine_copy=nc.scalar.copy):
-            interleave(g[:, PACK * n0 : PACK * n1], w2_raw[b][:, :, n0:n1], engine_copy)
-
-        def slice_differences(n):
-            if n < PACK:
-                slice_a(n)
-            else:
-                differences([unit_b(n - PACK, r) for r in range(2)], tile("child%d" % n, [J], F32))
-
         gather_tab(0)
         gather_tab(1)
         nc.vector.tensor_copy(v_s[:], tab_s[:].indirect(offs_sb[:]))
-        round_w1(0, 0, scalar_identity)
-        round_w1(0, 1)
-        round_w1(0, 2)
-        quant_w1(0)
-        quant_w1(1)
+        round_one(0, 0, scalar_identity)
+        round_one(0, 1)
+        round_one(0, 2)
+        quant_w1("s0_first")
+        quant_w1("s0_close")
         h_passes((0,), (0, 1))
         gather_tab(2, 0, BANK)
         gather_tab(2, BANK, S)
         h_passes((0,), (2,))
         for a in range(KA):
-            round_w1(1, a)
-        quant_w1(2)
-        quant_w1(3)
+            round_one(1, a)
+        quant_w1("s1_first")
+        quant_w1("s1_close")
         h_passes((1,), (0, 1, 2))
-        evict_h(0, 0)
-        evict_h(0, 1, on_vector=True)
+        evict_bank(0, 0)
+        nc.vector.tensor_scalar(h[0][:, BANK:], acc[0, 1][:], h_bias(0), 0.0, ALU.add, ALU.max)
 
-        round_w1(2, 0)
-        round_w1(2, 1, nc.scalar.copy, 0, 64)
-        slice_around(0, head_share)
+        round_two(0)
+        round_two(1, 0, P)
+        kids = tile("child0", [J], F32)
+        children(kids[:], 0, 0, J)
+        round_two(1, P, 2 * P, nc.vector.tensor_copy, VECTOR_WALK)
+        quant_w1("s23_first")
+        parents_less(z_rows[0][:], 0, 0, J, kids[:])
         h_passes((2,), (0, 1))
-        round_w1(2, 2)
-        quant_w1(5)
+        round_two(2)
+        quant_w1("s23_last")
         h_passes((2,), (2,))
         h_passes((3,), (2, 0, 1))
         evict_slice(1)
-        slice_differences(1)
+        differences([(1, 0), (1, 1)], tile("child1", [J], F32))
 
-        round_w1(4, 0)
-        round_w1(6, 0, nc.vector.tensor_copy)
+        round_pair(4, 0)
+        round_pair(6, 0, nc.vector.tensor_copy)
         evict_slice(2)
-        slice_around(2, lambda: quant_w1(6))
+        kids = tile("child2", [J], F32)
+        children(kids[:], 2, 0, J)
+        quant_w1("s45_first")
+        parents_less(z_rows[2][:], 2, 0, J, kids[:])
         h_passes((4, 5), (0,))
-        round_w1(4, 1)
-        quant_w1(10)
+        round_pair(4, 1)
+        quant_w1("s45_mid")
         h_passes((4, 5), (1,))
         evict_slice(3)
-        round_w1(4, 2)
-        quant_w1(7)
+        round_pair(4, 2)
+        quant_w1("s45_close")
         h_passes((4, 5), (2,))
-        round_w1(6, 2)
-        slice_around(3, lambda: quant_w1(8), "w1_g7")
+        round_pair(6, 2)
+        kids = tile("child3", [J], F32, over="g_s45_close")
+        children(kids[:], 3, 0, J)
+        quant_w1("s67_first")
+        parents_less(z_rows[3][:], 3, 0, J, kids[:])
         for c in (0, 2, 1, 3):
             deal(c)
 
         h_passes((6, 7), (2, 0))
         evict_slice(4)
-        child4 = tile("child4", [J], F32)
-        nc.vector.tensor_copy(child4[:], h[4][:].indirect(pos2_sb[:]))
-        round_w1(6, 1)
-        quant_w1(9)
+        kids = tile("child4", [J], F32)
+        children(kids[:], 4, 0, J)
+        round_pair(6, 1)
+        quant_w1("s67_close")
         h_passes((6, 7), (1,))
         for r, (j0, j1) in enumerate(RUNS):
-            nc.vector.tensor_tensor(
-                z_b[r][:, 0, :], h[4][:].indirect(pos1_sb[:, j0 // 16 : j1 // 16]), child4[:, j0:j1], ALU.subtract
-            )
+            parents_less(z_part(4, r), 4, j0, j1, kids[:, j0:j1])
         evict_slice(5)
-        slice_differences(5)
+        differences([(5, 0), (5, 1)], tile("child5", [J], F32))
 
-        gw2 = [tile("gw20", [PACK * N], BF16, over="w2_first"), tile("gw21", [PACK * N], BF16, over="w2_late")]
-        round_w2(gw2[0], 0, 0, N)
-        quant(w2_w[0][:], w2_s[0][:], gw2[0][:])
+        w2_g = [tile("gw20", [PACK * N], BF16, over="w2_first"), tile("gw21", [PACK * N], BF16, over="w2_late")]
+        interleave(w2_g[0][:], w2_raw[0][:])
+        quant(w2_w[0][:], w2_s[0][:], w2_g[0][:])
         evict_slice(6)
         evict_slice(7)
-        differences([unit_b(2, 0), unit_b(3, 0)], tile("child6", [J], F32))
-        gz = [tile("gz0", [PACK * J], BF16, over="z_first"), tile("gz1", [PACK * HALF], BF16, over="z_a", at=2048)]
-        y = [[[bank(0), bank(1)], [bank(2), bank(3)]], [[bank(4), bank(5)], [bank(6), bank(7)]]]
+        differences([(6, 0), (7, 0)], tile("child6", [J], F32))
+        z_low_g = tile("gz0", [PACK * J], BF16, over="z_first")
+        z_high_g = [tile("gz1", [PACK * RUN], BF16, over="z_a", at=2 * KB)]
+        y = [[[bank(4 * r + 2 * view + k) for k in range(2)] for view in range(2)] for r in range(2)]
         for r, (j0, j1) in enumerate(RUNS):
-            interleave(gz[0][:, PACK * j0 : PACK * j1], z_a[:, :, j0:j1])
-            quant(z_w[0][:, j0:j1], z_s[0][:, j0:j1], gz[0][:, PACK * j0 : PACK * j1])
+            interleave(z_low_g[:, PACK * j0 : PACK * j1], z_low[:, :, j0:j1])
+            quant(z_w[0][:, j0:j1], z_s[0][:, j0:j1], z_low_g[:, PACK * j0 : PACK * j1])
             y_passes(y[r], r, 0)
-        differences([unit_b(2, 1), unit_b(3, 1)], tile("child7", [J], F32, over="z_a"))
-        interleave(gz[1][:], z_b[0][:])
-        quant(z_w[1][:, :HALF], z_s[1][:, :HALF], gz[1][:])
-        round_w2(gw2[1], 1, 0, N)
-        quant(w2_w[1][:], w2_s[1][:], gw2[1][:])
+        differences([(6, 1), (7, 1)], tile("child7", [J], F32, over="z_a"))
+        interleave(z_high_g[0][:], z_high[0][:])
+        quant(z_w[1][:, :RUN], z_s[1][:, :RUN], z_high_g[0][:])
+        interleave(w2_g[1][:], w2_raw[1][:])
+        quant(w2_w[1][:], w2_s[1][:], w2_g[1][:])
         y_passes(y[0], 0, 1)
-        gz_last = tile("gz_last", [PACK * HALF], BF16, over="z_b0")
-        interleave(gz_last[:], z_b[1][:])
-        quant(z_w[1][:, HALF:], z_s[1][:, HALF:], gz_last[:])
+        z_high_g.append(tile("gz_last", [PACK * RUN], BF16, over="z_b0"))
+        interleave(z_high_g[1][:], z_high[1][:])
+        quant(z_w[1][:, RUN:], z_s[1][:, RUN:], z_high_g[1][:])
         y_passes(y[1], 1, 1)
-        finish_y(y[0], 0, 2)
-        finish_y(y[1], 1, 4)
+        for r in range(2):
+            finish_run(y[r], r)

from contextlib import ExitStack

import concourse.mybir as mybir

K, T, S, J, H, N = 1536, 2048, 1024, 512, 1024, 512
FLOPS = 2 * K * H * S + 2 * 2 * H * N * J

F32 = mybir.dt.float32
BF16 = mybir.dt.bfloat16
I32 = mybir.dt.int32
U32 = mybir.dt.uint32
U16 = mybir.dt.uint16
U8 = mybir.dt.uint8
FP8X4 = mybir.dt.float8_e4m3fn_x4
FP4X4 = mybir.dt.float4_e2m1fn_x4
ALU = mybir.AluOpType
ACT = mybir.ActivationFunctionType
SIZE = {F32: 4, BF16: 2, I32: 4, U32: 4, U8: 1}

P = 128
PACK = 4
PASS = P * PACK
KA = K // PASS
HB = H // PASS
NC = N // P
BANK = 512
QUAD = 32
LIST = 16
ALIGN = 64
KB = 1024
RUN = J // 2
RUNS = [(0, RUN), (RUN, J)]
PER_BANK = BANK // RUN
SCALAR_WALK = 2
VECTOR_WALK = 4
STORES = (2, 4)

BATCHES = {
    "s0_first": [(0, 0), (0, 1)],
    "s0_close": [(0, 2)],
    "s1_first": [(1, 0), (1, 1)],
    "s1_close": [(1, 2)],
    "s23_first": [(2, 0), (3, 0), (2, 1), (3, 1)],
    "s23_last": [(2, 2), (3, 2)],
    "s45_first": [(4, 0), (5, 0)],
    "s45_close": [(4, 2), (5, 2)],
    "s67_first": [(6, 2), (7, 2), (6, 0), (7, 0)],
    "s67_close": [(6, 1), (7, 1)],
    "s45_mid": [(4, 1), (5, 1)],
}
CLOSES_WITH_PASS_1 = (3, 6, 7)


def tile_list_limb_pair_scores_kernel(
    tc, tab_words, tab_scales, offs, pos1, pos2, w1, b1, w2, w4_words, w4_scales, b3, out
):
    nc = tc.nc
    with ExitStack() as ctx:
        lists = ctx.enter_context(tc.tile_pool(name="keep", bufs=1))
        arena = ctx.enter_context(tc.tile_pool(name="arena", bufs=1))
        psum = ctx.enter_context(tc.psum_pool(name="psum", bufs=1))
        place = {"end": 0}

        def bank(i):
            return psum.tile([P, BANK], F32, name="bank%d" % i)

        def region(name, size, back=0):
            place[name] = place["end"] - back
            place["end"] = place[name] + size

        def tile(name, shape, dtype, over=None, at=0):
            size = SIZE[dtype]
            for d in shape:
                size = size * d
            if over is None:
                place[name] = place["end"]
                place["end"] = place["end"] + (size + ALIGN - 1) // ALIGN * ALIGN
            else:
                place[name] = place[over] + at
            return arena.tile([P] + shape, dtype, name=name, offset=place[name], align_bytes=ALIGN)

        offs_sb = lists.tile([P, S // LIST], U16, name="offs_sb")
        pos1_sb = lists.tile([P, J // LIST], U16, name="pos1_sb")
        pos2_sb = lists.tile([P, J // LIST], U16, name="pos2_sb")
        tab_w = [tile("tab_w%d" % a, [T], I32) for a in range(KA)]
        tab_s = tile("tab_s", [T], U8)
        w4_w = tile("w4_w", [HB, 2 * N], U8)
        w4_s = tile("w4_s", [HB, N], U8)
        for c in range(PACK):
            region("bias%d" % c, 2 * KB)
        b1_low = [tile("b1_a%d" % c, [1], F32, over="bias%d" % c) for c in range(PACK)]
        b1_high = tile("b1_b", [PACK], F32)
        b3_sb = tile("b3_sb", [NC], F32)
        raw_one = {(n, a): tile("raw_s%d%d" % (n, a), [PACK, P], F32) for n in range(2) for a in range(KA)}
        region("h0_rest", 2 * KB)
        raw_two = [tile("raw_a%d" % a, [PACK, 2 * P], F32) for a in range(KA)]
        raw_four = [tile("raw_b%d" % a, [PACK, PASS], F32) for a in range(KA)]
        region("w2_late", 4 * KB, back=KB)
        w2_raw = [tile("w2_raw%d" % b, [PACK, N], F32) for b in range(HB)]

        nc.vector.memset(tab_s[:].bitcast(I32), 0)
        nc.vector.memset(w4_s[:].rearrange("p b n -> p (b n)").bitcast(I32), 0)

        def load_tab(a):
            nc.sync.dma_start(out=tab_w[a][:], in_=tab_words[a].rearrange("p t i -> p (t i)").bitcast(I32))

        def load_w1(dst, a, c0, c1):
            rows = w1[a * PASS : (a + 1) * PASS, c0:c1]
            nc.sync.dma_start(out=dst[:], in_=rows.rearrange("(p i) c -> p i c", i=PACK))

        def load_b1(c):
            with nc.allow_non_contiguous_dma(reason="one bias value a partition"):
                nc.sync.dma_start(out=b1_low[c][:], in_=b1[c * P : (c + 1) * P].rearrange("(p o) -> p o", o=1))

        nc.sync.dma_start(offs_sb[:], offs)
        load_tab(0)
        load_tab(1)
        for q in range(P // QUAD):
            nc.sync.dma_start(
                out=tab_s[QUAD * q : QUAD * q + 4 * KA, :].bitcast(I32),
                in_=tab_scales[:, 4 * q : 4 * q + 4, :].bitcast(I32),
            )
        load_b1(0)
        for a in range(KA):
            load_w1(raw_one[0, a], a, 0, P)
        nc.sync.dma_start(pos2_sb[:], pos2)
        load_tab(2)
        for a in range(KA):
            load_w1(raw_one[1, a], a, P, 2 * P)
        load_w1(raw_two[0], 0, 2 * P, PASS)
        nc.sync.dma_start(pos1_sb[:], pos1)
        load_b1(1)
        for a in (1, 2):
            load_w1(raw_two[a], a, 2 * P, PASS)
        load_w1(raw_four[0], 0, PASS, H)
        load_b1(2)
        load_w1(raw_four[1], 1, PASS, H)
        load_b1(3)
        load_w1(raw_four[2], 2, PASS, H)
        nc.sync.dma_start(out=b1_high[:], in_=b1[PASS:].rearrange("(p t) -> p t", t=PACK))
        for b in range(HB):
            nc.sync.dma_start(
                out=w2_raw[b][:], in_=w2[b * PASS : (b + 1) * PASS, :].rearrange("(p i) n -> p i n", i=PACK)
            )
        nc.sync.dma_start(out=w4_w[:].bitcast(I32), in_=w4_words.rearrange("b p n -> p b n").bitcast(I32))
        for q in range(P // QUAD):
            nc.sync.dma_start(
                out=w4_s[QUAD * q : QUAD * q + 4, :, :].bitcast(I32),
                in_=w4_scales[:, 4 * q : 4 * q + 4, :].rearrange("b r n -> r b n").bitcast(I32),
            )
        with nc.allow_non_contiguous_dma(reason="one bias value a partition"):
            nc.sync.dma_start(out=b3_sb[:], in_=b3.rearrange("(c p) -> p c", p=P))

        v_w = [tile("v_w%d" % a, [S], U32, over=(None, None, "raw_s01")[a]) for a in range(KA)]
        v_s = tile("v_s", [S], U8)
        for name in ("after45", "z_first", "w2_first"):
            region(name, 4 * KB)
        rounded_over = {"s67_close": "after45"}
        words_over = {
            "s1_first": "tab_w2", "s23_first": "bias0", "s45_first": "bias2", "s45_close": "after45", "s67_close": "z_first",
        }
        scales_over = {"s45_close": "w2_first", "s67_close": "w2_late"}
        w1_g = {k: tile("g_" + k, [PASS * len(b)], BF16, over=rounded_over.get(k)) for k, b in BATCHES.items()}
        w1_w = {k: tile("w_" + k, [P * len(b)], U32, over=words_over.get(k)) for k, b in BATCHES.items()}
        w1_s = {k: tile("s_" + k, [P * len(b)], U8, over=scales_over.get(k), at=2 * KB) for k, b in BATCHES.items()}
        home = {piece: (k, m) for k, b in BATCHES.items() for m, piece in enumerate(b)}
        w2_w = [tile("w2_w%d" % b, [N], U32) for b in range(HB)]
        w2_s = [tile("w2_s%d" % b, [N], U8) for b in range(HB)]
        h = [tile("h%d" % n, [S], F32, over={0: "raw_s12", 1: "raw_a2"}.get(n)) for n in range(H // P)]
        z_rows = [tile("z_rows%d" % c, [J], F32, over=("raw_a1", None, None, "w2_late")[c]) for c in range(PACK)]
        z_low = tile("z_a", [PACK, J], F32)
        z_high = [tile("z_b%d" % r, [PACK, RUN], F32, over="raw_b1", at=4 * PACK * j0) for r, (j0, j1) in enumerate(RUNS)]
        z_w = [tile("z_w%d" % b, [J], U32) for b in range(HB)]
        z_s = [tile("z_s%d" % b, [J], U8) for b in range(HB)]
        acc = {}

        def gather_tab(a, e0=0, e1=S):
            nc.vector.tensor_copy(v_w[a][:, e0:e1], tab_w[a][:].bitcast(U32).indirect(offs_sb[:, e0 // LIST : e1 // LIST]))

        def quant(words, scales, src):
            nc.vector.quantize_mx(out=words.bitcast(FP8X4), scales=scales, in_=src)

        def scalar_identity(out, in_):
            nc.scalar.activation(out=out, in_=in_, func=ACT.Identity)

        def interleave(dst, src, engine_copy=nc.scalar.copy, walk=SCALAR_WALK):
            engine_copy(
                out=dst.rearrange("p (c u t) -> p c t u", u=walk, t=PACK),
                in_=src.rearrange("p t (c u) -> p c t u", u=walk),
            )

        def round_one(n, a, engine_copy=nc.scalar.copy):
            k, m = home[n, a]
            interleave(w1_g[k][:, m * PASS : (m + 1) * PASS], raw_one[n, a][:], engine_copy)

        def round_two(a, c0=0, c1=2 * P, engine_copy=nc.scalar.copy, walk=SCALAR_WALK):
            k, m = home[2, a]
            dst = w1_g[k][:, m * PASS + PACK * c0 : m * PASS + PACK * c1]
            interleave(dst, raw_two[a][:, :, c0:c1], engine_copy, walk)

        def round_pair(n, a, engine_copy=nc.scalar.copy):
            k, first = home[n, a]
            dst = w1_g[k][:, first * PASS : (first + 2) * PASS].rearrange("p (t m i) -> p m i t", t=2, i=PACK)
            src = raw_four[a][:].rearrange("p i (m u t) -> p u m i t", u=2, t=2)
            engine_copy(out=dst, in_=src[:, (n - PACK) // 2])

        def quant_w1(k):
            quant(w1_w[k][:], w1_s[k][:], w1_g[k][:])

        def h_pass(n, a, s):
            first = (n, s) not in acc
            if first:
                acc[n, s] = bank(2 * (n % 4) + s)
            k, m = home[n, a]
            cols = slice(m * P, (m + 1) * P)
            entries = slice(s * BANK, (s + 1) * BANK)
            nc.tensor.matmul_mx(
                out=acc[n, s][:],
                lhsT=w1_w[k][:, cols].bitcast(FP8X4),
                lhsT_scale=w1_s[k][:, cols],
                rhs=v_w[a][:, entries].bitcast(FP8X4),
                rhs_scale=v_s[4 * a :, entries],
                start=first,
                stop=(a == (1 if n in CLOSES_WITH_PASS_1 else KA - 1)),
            )

        def h_passes(slices, order):
            for n in slices:
                for s in range(S // BANK):
                    for a in order:
                        h_pass(n, a, s)

        def h_bias(n):
            return b1_low[n][:] if n < PACK else b1_high[:, n - PACK : n - PACK + 1]

        def evict_bank(n, s):
            nc.scalar.activation(out=h[n][:, s * BANK : (s + 1) * BANK], in_=acc[n, s][:], func=ACT.Relu, bias=h_bias(n))

        def evict_slice(n):
            for s in range(S // BANK):
                evict_bank(n, s)

        def children(dst, n, j0, j1):
            nc.vector.tensor_copy(dst, h[n][:].indirect(pos2_sb[:, j0 // LIST : j1 // LIST]))

        def parents_less(dst, n, j0, j1, kids):
            nc.vector.tensor_tensor(dst, h[n][:].indirect(pos1_sb[:, j0 // LIST : j1 // LIST]), kids, ALU.subtract)

        def z_part(n, r):
            j0, j1 = RUNS[r]
            return z_rows[n][:, j0:j1] if n < PACK else z_high[r][:, n - PACK, :]

        def differences(units, kids):
            for k, (n, r) in enumerate(units):
                children(kids[:, k * RUN : (k + 1) * RUN], n, *RUNS[r])
            for k, (n, r) in enumerate(units):
                parents_less(z_part(n, r), n, *RUNS[r], kids[:, k * RUN : (k + 1) * RUN])

        def deal(c):
            nc.sync.dma_start(out=z_low[QUAD * c : QUAD * (c + 1), :, :], in_=z_rows[c][:])

        def y_passes(banks, r, b):
            j0, j1 = RUNS[r]
            for c0 in range(0, NC, PER_BANK):
                for view in range(2):
                    for c in range(c0, c0 + PER_BANK):
                        cols = slice(c * P, (c + 1) * P)
                        if view == 0:
                            weights, scales = w2_w[b][:, cols].bitcast(FP8X4), w2_s[b][:, cols]
                        else:
                            weights, scales = w4_w[:, b, 2 * c * P : 2 * (c + 1) * P].bitcast(FP4X4), w4_s[:, b, cols]
                        nc.tensor.matmul_mx(
                            out=banks[view][c // PER_BANK][:, (c % PER_BANK) * RUN : (c % PER_BANK + 1) * RUN],
                            lhsT=weights,
                            lhsT_scale=scales,
                            rhs=z_w[b][:, j0:j1].bitcast(FP8X4),
                            rhs_scale=z_s[b][:, j0:j1],
                            start=(b == 0 and c % PER_BANK == 0),
                            stop=(b == HB - 1 and c % PER_BANK == PER_BANK - 1),
                        )

        def finish_run(banks, r):
            j0, j1 = RUNS[r]
            y1_biased = tile("y1b%d" % r, [NC, RUN], F32, over="tab_w0", at=4 * NC * j0)
            res = tile("res%d" % r, [NC, RUN], F32, over="tab_w1", at=4 * NC * j0)
            for c in range(NC):
                part = slice((c % PER_BANK) * RUN, (c % PER_BANK + 1) * RUN)
                nc.scalar.activation(
                    out=y1_biased[:, c, :], in_=banks[0][c // PER_BANK][:, part], func=ACT.Identity, bias=b3_sb[:, c : c + 1]
                )
            for c in range(NC):
                part = slice((c % PER_BANK) * RUN, (c % PER_BANK + 1) * RUN)
                nc.vector.scalar_tensor_tensor(
                    res[:, c, :], banks[1][c // PER_BANK][:, part], b3_sb[:, c : c + 1], y1_biased[:, c, :], ALU.add, ALU.max
                )
            step = NC // STORES[r]
            for c in range(0, NC, step):
                nc.sync.dma_start(
                    out=out[c * P : (c + step) * P, j0:j1].rearrange("(c p) j -> p c j", p=P), in_=res[:, c : c + step, :]
                )

        gather_tab(0)
        gather_tab(1)
        nc.vector.tensor_copy(v_s[:], tab_s[:].indirect(offs_sb[:]))
        round_one(0, 0, scalar_identity)
        round_one(0, 1)
        round_one(0, 2)
        quant_w1("s0_first")
        quant_w1("s0_close")
        h_passes((0,), (0, 1))
        gather_tab(2, 0, BANK)
        gather_tab(2, BANK, S)
        h_passes((0,), (2,))
        for a in range(KA):
            round_one(1, a)
        quant_w1("s1_first")
        quant_w1("s1_close")
        h_passes((1,), (0, 1, 2))
        evict_bank(0, 0)
        nc.vector.tensor_scalar(h[0][:, BANK:], acc[0, 1][:], h_bias(0), 0.0, ALU.add, ALU.max)

        round_two(0)
        round_two(1, 0, P)
        kids = tile("child0", [J], F32)
        children(kids[:], 0, 0, J)
        round_two(1, P, 2 * P, nc.vector.tensor_copy, VECTOR_WALK)
        quant_w1("s23_first")
        parents_less(z_rows[0][:], 0, 0, J, kids[:])
        h_passes((2,), (0, 1))
        round_two(2)
        quant_w1("s23_last")
        h_passes((2,), (2,))
        h_passes((3,), (2, 0, 1))
        evict_slice(1)
        differences([(1, 0), (1, 1)], tile("child1", [J], F32))

        round_pair(4, 0)
        round_pair(6, 0, nc.vector.tensor_copy)
        evict_slice(2)
        kids = tile("child2", [J], F32)
        children(kids[:], 2, 0, J)
        quant_w1("s45_first")
        parents_less(z_rows[2][:], 2, 0, J, kids[:])
        h_passes((4, 5), (0,))
        round_pair(4, 1)
        quant_w1("s45_mid")
        h_passes((4, 5), (1,))
        evict_slice(3)
        round_pair(4, 2)
        quant_w1("s45_close")
        h_passes((4, 5), (2,))
        round_pair(6, 2)
        kids = tile("child3", [J], F32, over="g_s45_close")
        children(kids[:], 3, 0, J)
        quant_w1("s67_first")
        parents_less(z_rows[3][:], 3, 0, J, kids[:])
        for c in (0, 2, 1, 3):
            deal(c)

        h_passes((6, 7), (2, 0))
        evict_slice(4)
        kids = tile("child4", [J], F32)
        children(kids[:], 4, 0, J)
        round_pair(6, 1)
        quant_w1("s67_close")
        h_passes((6, 7), (1,))
        for r, (j0, j1) in enumerate(RUNS):
            parents_less(z_part(4, r), 4, j0, j1, kids[:, j0:j1])
        evict_slice(5)
        differences([(5, 0), (5, 1)], tile("child5", [J], F32))

        w2_g = [tile("gw20", [PACK * N], BF16, over="w2_first"), tile("gw21", [PACK * N], BF16, over="w2_late")]
        interleave(w2_g[0][:], w2_raw[0][:])
        quant(w2_w[0][:], w2_s[0][:], w2_g[0][:])
        evict_slice(6)
        evict_slice(7)
        differences([(6, 0), (7, 0)], tile("child6", [J], F32))
        z_low_g = tile("gz0", [PACK * J], BF16, over="z_first")
        z_high_g = [tile("gz1", [PACK * RUN], BF16, over="z_a", at=2 * KB)]
        y = [[[bank(4 * r + 2 * view + k) for k in range(2)] for view in range(2)] for r in range(2)]
        for r, (j0, j1) in enumerate(RUNS):
            interleave(z_low_g[:, PACK * j0 : PACK * j1], z_low[:, :, j0:j1])
            quant(z_w[0][:, j0:j1], z_s[0][:, j0:j1], z_low_g[:, PACK * j0 : PACK * j1])
            y_passes(y[r], r, 0)
        differences([(6, 1), (7, 1)], tile("child7", [J], F32, over="z_a"))
        interleave(z_high_g[0][:], z_high[0][:])
        quant(z_w[1][:, :RUN], z_s[1][:, :RUN], z_high_g[0][:])
        interleave(w2_g[1][:], w2_raw[1][:])
        quant(w2_w[1][:], w2_s[1][:], w2_g[1][:])
        y_passes(y[0], 0, 1)
        z_high_g.append(tile("gz_last", [PACK * RUN], BF16, over="z_b0"))
        interleave(z_high_g[1][:], z_high[1][:])
        quant(z_w[1][:, RUN:], z_s[1][:, RUN:], z_high_g[1][:])
        y_passes(y[1], 1, 1)
        for r in range(2):
            finish_run(y[r], r)
